import numpy as np, ml_dtypes
CORES = [40,41,42,43,44,45,46,47]
N = 8
BF = ml_dtypes.bfloat16
def gentries(a):
    return np.ascontiguousarray(a.reshape(8, 16, -1).transpose(0, 2, 1)).reshape(8, -1)
def gtable(e):
    e = np.asarray(e); return np.ascontiguousarray(e.reshape(8, -1, 16).transpose(0, 2, 1)).reshape(128, -1).astype(np.int32)
NW, E, EP, C, U = 4096, 128, 3, 3, 2
def at(a, d):
    return np.roll(a, -1, axis=0) if d == 2 else a
def pick(a, ix):
    return np.take_along_axis(a, ix.reshape(8, 1, -1), 2).reshape(8, 16, E, 16)
def children(L, last, st, b):
    n = np.where(st, np.minimum(C, 15 - last), 0); end = np.add.accumulate(n, axis=-1); m = np.arange(16)
    k = np.add.reduce((end[..., None, :] <= m[:, None]).astype(np.int64), axis=-1)
    real = k < 16; k = np.minimum(k, 15)
    bb = np.where(real, np.take_along_axis(last, k, 2) + 1 + m - np.take_along_axis(end - n, k, 2), 15)
    Lk = np.take_along_axis(L, k, 2); Bb = np.take_along_axis(b, bb, 2)
    return np.where(real, (((Lk * Bb) >> 5) + Lk + 37 * Bb) & (NW - 1), NW - 1), bb, k
def grow(w, tau, b):
    names, par, votes = [[], [], []], [[], [], []], []
    for r in range(N):
        L = b[r]; last = np.zeros((8, E, 16), np.int64) + np.arange(16); p = np.zeros((8, E, 16), np.int64); c = np.zeros((8, E), np.int64)
        for d in range(3):
            q = (r + d) % N
            st = np.count_nonzero(pick(at(w[q], d), L) >= at(tau[q], d)[:, :, None, d:d + 1], axis=1) >= 9
            c = c + np.count_nonzero(st, axis=-1); names[d].append(L); par[d].append(p)
            if d < 2: L, last, p = children(L, last, st, b[r])
        votes.append(c)
    return names, par, np.stack(votes)
def winnow(w, names, fp, fn):
    new = []
    for q in range(N):
        bad = np.zeros((8, NW), bool); miss = np.zeros((8, NW), bool)
        for d in range(3):
            r = (q - d) % N; ix = names[d][r][:, :, :U]
            h = np.zeros(ix.shape, np.int64) + ((np.arange(8) + (d == 2)) % 8)[:, None, None]
            for flag, hit in ((fp, bad), (fn, miss)):
                on = np.zeros(ix.shape, bool) | flag[r][:, :, None]
                hit[h[on], ix[on]] = True
        fac = np.where(miss, 2.0, np.where(bad, 0.5, 1.0)).astype(np.float32)
        v = np.minimum(np.maximum(w[q] * fac[:, None, :], np.float32(0.25)), np.float32(4.0)); v[:, :, NW - 1] = 0
        new.append(v)
    return np.stack(new)
def bf(a):
    return np.asarray(a).astype(BF).astype(np.float32)
def parts(rng, off=0.8):
    f = 0.5 + 0.75 * rng.random((128, NW))
    t0 = bf(np.exp2(0.8 * rng.random((N, 8, 16, 3)) - 0.4)); up = rng.integers(0, 4, t0.shape)
    tau = np.where(up < 2, t0, np.where(up == 2, t0 * np.float32(1.0 + 2.0 ** -12), np.nextafter(t0, np.float32(8.0)))).astype(np.float32)
    z = off * (2.0 * rng.random((N, 8, 1, 1), dtype=np.float32) - 1.0) + 3.2 * rng.random((N, 8, 1, NW), dtype=np.float32) - 1.6 + 1.2 * rng.random((N, 8, 16, NW), dtype=np.float32) - 0.6
    w = np.where(rng.random((N, 8, 16, NW), dtype=np.float32) < 0.1, np.take_along_axis(t0, rng.integers(0, 3, (N, 8, 1, NW)), 3), np.exp2(z))
    w = bf(np.minimum(np.maximum(w, 0.25), 4.0)); w[..., NW - 1] = 0
    b = rng.integers(0, NW - 1, (EP, N, 8, E, 16))
    x = 0.5 + 0.5 * rng.random((N, 128, EP * E))
    return f, w, b, x, tau
def tune(rng, w, tau, b, codes, share):
    lab, ask = [], []; codes = np.broadcast_to(codes, (EP - 1, N, 8, E))
    for t in range(EP - 1):
        names, par, c = grow(w, tau, b[t]); code = codes[t]
        near = c + rng.integers(0, 2, c.shape)
        loose = np.where(rng.random(c.shape) < 0.7, c + rng.integers(-2, 4, c.shape), rng.integers(1, 49, c.shape))
        ends = np.where(rng.random(c.shape) < 0.7, rng.choice(np.array([1, 48]), c.shape), near)
        a = np.where(code == 0, loose, np.where(code == 1, c, np.where(code == 2, c + 1, np.where(code == 3, near, ends))))
        a = np.minimum(np.maximum(a, 1), 48)
        y = np.where((code == 1) | (code == 3), 0, np.where(code == 2, 1, (rng.random(c.shape) < share).astype(np.int64)))
        lab.append(y); ask.append(a)
        if t < EP - 2: w = winnow(w, names, (c >= a) & (y == 0), (c < a) & (y == 1))
    return np.stack(lab), np.stack(ask)
def pack(rng, f, w, b, x, tau, code, share):
    lab, ask = tune(rng, w, tau, b, code, share)
    f = np.array(f); f[:, NW - 1] = 0
    flat = lambda a: np.ascontiguousarray(a.transpose(1, 2, 0, 3).reshape(N, 8, -1)).astype(np.int32)
    return {"ft": np.stack([f.astype(BF)] * N), "wt": np.ascontiguousarray(w.reshape(N, 128, NW)).astype(BF),
            "bn": np.stack([gtable(b[:, r].transpose(1, 0, 2, 3).reshape(8, -1)) for r in range(N)]), "xv": x.astype(BF),
            "tau": np.ascontiguousarray(tau.reshape(N, 128, 3)).astype(np.float32), "lab": flat(lab), "ask": flat(ask)}
def setup_inputs(rng):
    f, w, b, x, tau = parts(rng)
    return pack(rng, f, w, b, x, tau, np.zeros((N, 8, E), np.int64), rng.choice(np.array([0.15, 0.3, 0.5]), (N, 8, 1)))
def setup_inputs_spread(rng):
    f, w, b, x, tau = parts(rng)
    x = x * np.exp2(rng.integers(-1, 2, (N, 1, EP * E)))
    b = np.minimum(((NW - 1) * rng.random(b.shape) ** 3).astype(np.int64), NW - 2)
    w = bf(np.exp2(4.0 * rng.random(w.shape, dtype=np.float32) - 2.0)); w[..., NW - 1] = 0
    return pack(rng, f, w, b, x, tau, np.zeros((N, 8, E), np.int64), rng.choice(np.array([0.05, 0.3, 0.6]), (N, 8, 1)))
def setup_inputs_ends(rng):
    f, w, b, x, tau = parts(rng)
    f = np.where(rng.random(f.shape) < 0.5, 0.5, 1.25); x = np.where(rng.random(x.shape) < 0.5, 0.25, 2.0)
    w = np.where(rng.random(w.shape) < rng.choice(np.array([0.0, 0.5, 1.0]), (N, 8, 1, NW)), 4.0, 0.25).astype(np.float32)
    w[:, 1, :, 0] = 0.25; w[:, 1, :, NW - 2] = 0.25; w[:, 6, :, 0] = 0.25; w[:, 6, :, NW - 2] = 0.25; w[..., NW - 1] = 0
    low = np.array([9, 0, 5, 6, 7, 8, 6, 16])[None, :, None, None]
    tau = np.where(np.argsort(rng.random((N, 8, 16, 3)), axis=2) < low, 0.25, 4.0).astype(np.float32)
    two = rng.choice(np.array([0, NW - 2]), b.shape); m = rng.random(b.shape) < 0.7; m[:, :, 1, ::2] = True; m[:, :, 6, ::2] = True
    b = np.where(m, two, b)
    return pack(rng, f, w, b, x, tau, np.full((N, 8, E), 4), np.array([0.5, 0.03, 0.97, 0.3, 0.5, 0.1, 0.9, 0.3])[None, :, None])
def pattern(T):
    on = np.zeros(16, bool)
    for k in range(15):
        n = min(C, 15 - k)
        if n <= T: on[k] = True; T = T - n
    return on
def setup_inputs_corners(rng):
    f, w, b, x, tau = parts(rng); tau[:, 1:] = 0.375; slot = np.arange(16); e = np.arange(E)[:, None]
    size = (0, NW - 1, NW - 2, NW - 2, 64, 64, 64, NW >> 1)
    pats = np.stack([pattern(T) for T in (0, 1, C, 15, 16, 17, 40)] + [slot >= 0, slot == 15])
    for r in range(N):
        for g in range(1, 8):
            o = rng.permutation(NW - 1); H = size[g]; m = np.zeros(NW, bool); m[o[:H]] = True
            w[r, g] = bf(np.where(m, 3.0 + rng.random((16, NW)), 0.25 + 0.05 * rng.random((16, NW))))
            for t in range(EP):
                if g == 1: want = np.ones((E, 16), bool)
                elif g < 4: want = (slot < 15) | ((e + t) % 2 == 0)
                elif g < 7: want = slot >= 16 - ((e + t + r) & 3)
                else: want = pats[(np.arange(E) + t) % len(pats)]
                b[t, r, g] = o[np.where(want, rng.integers(0, H, (E, 16)), rng.integers(min(H, NW - 2), NW - 1, (E, 16)))]
    w[..., NW - 1] = 0
    code = np.zeros((N, 8, E), np.int64); code[:, 0] = 2; code[:, 1:7] = 3
    return pack(rng, f, w, b, x, tau, code, np.full((N, 8, 1), 0.4))
def setup_inputs_crowd(rng):
    f, w, b, x, tau = parts(rng)
    b[:, :, :5] = 0
    for t in range(EP):
        for r in range(N): b[t, r, 4, int(rng.integers(0, E)), int(rng.integers(0, U))] = int(rng.integers(1, NW - 1))
    b[:, :, 5] = rng.choice(rng.integers(0, NW - 1, 3), (EP, N, E, 16)); b[:, :, 6] = int(rng.integers(1, NW - 1))
    w[:, :5, :, 0] = 1.0; tau[..., :2] = 0.3; tau[..., 2] = 3.0
    other = rng.integers(1, NW - 1, (EP, N)); w[:, 2:4, :, other.reshape(-1)] = 1.0
    code = np.zeros((N, 8, E), np.int64); code[:, :5] = 1; code[:, 6] = 2
    for r in range(N):
        e = int(rng.integers(0, E)); code[r, 2, e] = 2; b[:, r, 2, e, 0] = other[:, r]
        code[r, 4, int(rng.integers(0, E))] = 2
    return pack(rng, f, w, b, x, tau, code, np.full((N, 8, 1), 0.3))
def setup_inputs_full(rng):
    f, w, b, x, tau = parts(rng, 0.0); tau = np.nextafter(bf(tau), np.float32(8.0))
    b[..., :U] = np.argsort(rng.random((EP, N, 8, NW - 1)), axis=-1)[..., :E * U].reshape(EP, N, 8, E, U)
    return pack(rng, f, w, b, x, tau, np.where(np.arange(EP - 1) % 2 == 0, 2, 1)[:, None, None, None], np.full((N, 8, 1), 0.5))
def check_ranges(d):
    bad = []
    for k, lo, hi in (("bn", 0, NW - 2), ("lab", 0, 1), ("ask", 1, 48), ("tau", 0.25, 4)):
        v = np.asarray(d[k])
        if not np.all((v >= lo) & (v <= hi)): bad.append("range of " + k)
    for k, lo, hi in (("ft", 0.5, 1.25), ("wt", 0.25, 4)):
        v = np.asarray(d[k]).astype(np.float32)
        if not np.all((v[..., :NW - 1] >= lo) & (v[..., :NW - 1] <= hi)): bad.append("range of " + k)
        if not np.all(v[..., NW - 1] == 0): bad.append("last column of " + k)
    v = np.asarray(d["ft"]).astype(np.float32)
    if not np.all(v == v[:1]): bad.append("ft is not alike on all ranks")
    v = np.asarray(d["xv"]).astype(np.float32)
    if not np.all((v >= 0.25) & (v <= 2)): bad.append("range of xv")
    return bad
def reference(ft, wt, bn, xv, tau, lab, ask):
    f = np.asarray(ft).astype(np.float64).reshape(N, 8, 16, NW); w = np.asarray(wt).astype(np.float32).reshape(N, 8, 16, NW); ta = np.asarray(tau).astype(np.float32).reshape(N, 8, 16, 3)
    b = np.stack([gentries(a) for a in bn]).astype(np.int64).reshape(N, 8, EP, E, 16)
    la = np.asarray(lab).reshape(N, 8, EP - 1, E); need = np.asarray(ask).reshape(N, 8, EP - 1, E); ys, cs = [], []
    for t in range(EP):
        names, par, c = grow(w, ta, b[:, :, t]); s = np.zeros((N, 8, 16, E))
        for r in range(N):
            for d in range(3):
                q = (r + d) % N; L = names[d][r]; fl = pick(at(f[q], d), L)
                v = fl if d == 0 else np.take_along_axis(v, par[d][r][:, None], 3) * fl
                s[r] += np.add.reduce(v * pick(at(w[q], d), L), axis=3)
        ys.append(s); cs.append(c)
        if t < EP - 1:
            yes = c >= need[:, :, t]
            w = winnow(w, names, yes & (la[:, :, t] == 0), ~yes & (la[:, :, t] == 1))
    y = np.stack(ys).transpose(1, 2, 3, 0, 4).reshape(N, 128, EP * E) * np.asarray(xv).astype(np.float64)
    return {"y": y.astype(np.float32), "cv": np.stack(cs).transpose(1, 2, 0, 3).reshape(N, 8, EP * E).astype(np.float32)}

def check_inputs(d):
    bad = list(check_ranges(d))
    if not bad:
        for name, y in reference(**d).items():
            for q in range(N):
                v = np.abs(np.asarray(y[q], np.float64)); s = np.sqrt(np.mean(v * v))
                if v.max() > 8 * s or s < 2.0 ** 3: bad.append('%s of rank %d is uneven or too small' % (name, q))
    return bad

@@ -1,0 +1,676 @@
+import numpy as np
+from concourse.bass import DstId, RemoteDMATransfer
+from concourse.mybir import AluOpType as A, ActivationFunctionType as AF
+
+NW, E, EP = 4096, 128, 3
+BF, F16, F32, I32, U16 = "bfloat16", "float16", "float32", "int32", "uint16"
+
+
+def _sb(n, d):
+    return ("sbuf", [128, n], d)
+
+
+SCRATCH = {
+    "WA": _sb(3 * NW, BF), "WB": _sb(3 * NW, BF), "F": _sb(NW, BF), "Fr": _sb(NW, BF), "FW": _sb(NW, F32),
+    "X1": _sb(2048, F32), "X2": _sb(2048, F32), "X3": _sb(2048, F32), "C": _sb(2048, BF), "GB": _sb(2048, BF),
+    "TB": _sb(2048, BF), "TP": _sb(2048, BF), "R": _sb(2048, F16), "RL": _sb(2048, F32), "OH": _sb(48 * 128, BF), "AA": _sb(1536, BF),
+    "Aw": _sb(1536, BF),
+    "bni": _sb(384, I32), "taus": _sb(4, F32), "tw": _sb(16, F32), "ti": _sb(4, I32), "xvs": _sb(384, BF),
+    "LA": _sb(512, I32), "LAl": _sb(512, I32), "nask": _sb(256, F16), "sig": _sb(256, F32),
+    "dig": _sb(768, BF), "digl": _sb(768, BF), "L1": _sb(384, U16), "bf": _sb(384, F32),
+    "IX": _sb(176, I32), "IP": _sb(4, I32), "col": _sb(16, F32), "Yi": _sb(176, I32), "Yj": _sb(176, I32), "Ym": _sb(176, F32),
+    "Y5": _sb(176, F16), "MM": _sb(176, BF), "M16": _sb(176, F16), "Ms": _sb(176, F16), "MF": _sb(176, F32), "Mr": _sb(6 * 176, BF),
+    "B0": _sb(176, F16), "B0F": _sb(176, F32), "Blk": _sb(176, F16), "TriL": _sb(128, F16), "TriB": _sb(128, F16),
+    "I16": _sb(128, F16), "ShI": _sb(128, F16), "ShF": _sb(128, F32), "IU": _sb(144, F32), "CE1": _sb(128, F16), "CE2": _sb(128, F16),
+    "Ibf": _sb(128, BF), "I4k": _sb(128, BF), "Dg": _sb(128, BF), "ones": _sb(128, BF), "zero": _sb(256, BF), "cst": _sb(256, BF), "xt": _sb(128, F16), "IB": _sb(128, F16),
+    "SCi": _sb(16, I32), "SelC": _sb(16, F16), "SAi": _sb(576, I32), "SelA": _sb(512, F16),
+    "SelN": _sb(512, F16), "SelW": _sb(576, BF), "AL": _sb(512, F32),
+    "nn": _sb(128, F16), "nt": _sb(128, F16), "st": _sb(128, F16), "ua": _sb(128, F16), "xi": _sb(128, I32), "xj": _sb(128, I32),
+    "qi": _sb(128, I32), "fr": _sb(128, F32), "IDX": _sb(128, U16), "Lp": _sb(128, F32), "lin": _sb(128, F32),
+    "flag": _sb(128, F16), "pa": _sb(128, I32), "pb": _sb(128, I32), "S1": _sb(128, F32),
+    "ndb": _sb(256, F16), "bT": _sb(48, F32), "tv": _sb(128, F32),
+    "s1": _sb(256, BF), "s2": _sb(256, BF), "UL": _sb(256, U16), "ys": _sb(384, F32),
+    "s1a": _sb(768, U16), "l1a": _sb(768, U16), "s1b": _sb(768, F32), "l1b": _sb(768, F32), "s1c": _sb(1152, F16), "l1c": _sb(1152, F16),
+    "s2a": _sb(768, U16), "l2a": _sb(768, U16), "s2b": _sb(384, U16), "l2b": _sb(384, U16),
+    "s2c": _sb(384, F16), "l2c": _sb(384, F16), "s3": _sb(256, BF), "l3a": _sb(256, BF), "l3b": _sb(256, BF),
+    "s4": _sb(384, F32), "l4": _sb(384, F32), "s5": _sb(768, F32), "l5": _sb(768, F32),
+}
+for _b in range(8):
+    SCRATCH["ps%d" % _b] = ("psum", [128, 512], F32)
+NDMA, NMSG = 48, 32
+SEMAPHORES = ["qv", "qs", "qp", "qg", "sent"] + ["d%d" % i for i in range(NDMA)] + ["a%d" % i for i in range(NMSG)]
+
+CY, PC, GC, FIX, WAKE, HOP, ISSUE = 0.00104, 0.00052, 1.56, 0.03, 0.12, 2.2, 0.35
+CH = 512
+UP, LEAN, LOOK, ROUNDS, MIX, NOISE, MARGIN, CLIMB = 3.0, 15.0, 0.4, 40, 0.5, 2.0, 3.0, 700
+
+
+def build(g, T, nxt, prv, prv2, nx2):
+    ops, boost = [], [0.0]
+    V, S, P = g.vector, g.scalar, g.tensor
+
+    def add(alts, r, w, kind="c", lat=0.0):
+        ops.append({"alts": alts, "r": list(r), "w": list(w), "kind": kind, "lat": lat, "up": boost[0]})
+
+    def vd(c):
+        return FIX + max(64, c) * CY
+
+    def ts(out, in0, s1, s2, o0, o1, r, w, c=128):
+        if o1 is None:
+            add({"v": (vd(c), lambda: V.tensor_scalar(out, in0, s1, None, o0))}, r, w)
+        else:
+            add({"v": (vd(c), lambda: V.tensor_scalar(out, in0, s1, s2, o0, o1))}, r, w)
+
+    def tt(out, a, b, o, r, w, c=256):
+        add({"v": (vd(c), lambda: V.tensor_tensor(out, a, b, o))}, r, w)
+
+    def cp(out, a, r, w, c=128, both=False):
+        al = {"v": (vd(c), lambda: V.tensor_copy(out, a))}
+        if both:
+            al["s"] = (vd(c), lambda: S.activation(out, a, AF.Copy))
+        add(al, r, w)
+
+    def ms(ap, val, w, c):
+        add({"v": (vd(c), lambda: V.memset(ap, val))}, [], w)
+
+    def mm(lst, r, w, cyc):
+        def run():
+            last = None
+            for (o, l, x, a, b) in lst:
+                last = P.matmul(o, l, x, a, b)
+            return last
+        add({"p": (FIX + cyc * PC, run)}, r, w)
+
+    def dma(q, out, a, r, w, nbytes):
+        eng = g.sync if q == "y" else g.scalar
+        add({q: (0.1, lambda: eng.dma_start(out, a))}, r, w, "dma", nbytes / 450e3)
+
+    def send(dsts, src, r, w, nbytes):
+        add({"g": (ISSUE, (dsts, src))}, r, w, "msg", HOP + nbytes / 150e3)
+
+    def iota(out, pat, base, cm, w, n, small=False):
+        if small:
+            add({"g": (0.15 + 2 * n * CY, lambda: g.iota(out, pat, base, cm, allow_small_or_imprecise_dtypes=True))}, [], w)
+        else:
+            add({"g": (0.15 + 2 * n * CY, lambda: g.iota(out, pat, base, cm))}, [], w)
+
+    gd = FIX + CH * GC * CY
+    nch = 2048 // CH
+    oc = CH // 16
+
+    def gather(kind, out, okey, win, wkeys, off, o0, okeys, d=0):
+        for j in range(nch):
+            src = win.indirect(off[:, o0 + j * oc:o0 + (j + 1) * oc])
+            dst = out[:, j * CH:(j + 1) * CH]
+            k = "%s%d" % (okey, j)
+            if kind == "cmp":
+                add({"v": (gd, lambda s=src, t=dst: V.tensor_scalar(t, s, T.taus[:, d:d + 1], 0.5, A.is_ge, A.subtract)),
+                     "s": (gd, lambda s=src, t=dst: S.activation(t, s, AF.Sign, bias=T.tw[:, 12 + d:13 + d]))},
+                    wkeys + okeys + ["tau"], [k])
+            elif kind == "copy":
+                add({"v": (gd, lambda s=src, t=dst: V.tensor_copy(t, s)),
+                     "s": (gd, lambda s=src, t=dst: S.activation(t, s, AF.Copy))}, wkeys + okeys, [k])
+            elif kind == "scopy":
+                add({"s": (gd, lambda s=src, t=dst: S.activation(t, s, AF.Copy))}, wkeys + okeys, [k])
+            else:
+                add({"v": (gd, lambda s=src, t=dst: V.tensor_tensor(t, s, t, A.mult))}, wkeys + okeys + [k], [k])
+
+    def narrow(ps, bank, M, mkey, wide, wkey, m0=0):
+        for h in range(2):
+            lst = [(ps[:, 64 * h:64 * h + 64], M[:, m0 + 32 - k:m0 + 160 - k], wide[:, 1024 * h + k:1024 * (h + 1):16], k == 0, k == 15)
+                   for k in range(16)]
+            mm(lst, [mkey] + ["%s%d" % (wkey, j) for j in range(h * nch // 2, (h + 1) * nch // 2)], [bank], 16 * 64)
+
+    def reduce(ps, bank, perm, wide, wkey):
+        for h in range(2):
+            for a in range(4):
+                lst = [(ps[:, 64 * h:64 * h + 64], perm, wide[:, 1024 * h + k:1024 * (h + 1):16], k == 0, k == 15) for k in range(4 * a, 4 * a + 4)]
+                mm(lst, ["IU"] + ["%s%d" % (wkey, j) for j in range(h * nch // 2, (h + 1) * nch // 2)], [bank], 4 * 256)
+
+    def act(out, a, f, bias, scale, r, w, c=128):
+        add({"s": (vd(c), lambda: S.activation(out, a, f, bias=bias, scale=scale))}, r, w)
+
+    col = T.col
+    c_k, c_g, c_kh, c_k5, c_k4, c_k0, c_nk, c_cap, c_32p, c_p, c_k16, c_u1, c_u2, c_ks = [col[:, i:i + 1] for i in range(14)]
+    ps = [T["ps%d" % b] for b in range(8)]
+    W = [T.WA, T.WB, T.WA]
+    wk = [["W%s%d" % ("ABA"[t], j) for j in range(8)] for t in range(EP)]
+    fwk = ["FW%d" % j for j in range(8)]
+
+    boost[0] = 20.0
+    dma("y", T.bni[:], T.bn[:], [], ["bni"], 196e3)
+    boost[0] = 0.0
+    dma("s", T.taus[:, 0:3], T.tau[:], [], ["taus"], 2e3)
+    dma("y", T.WA[:, 0:NW], T.wt[:], [], wk[0], 1048e3)
+    dma("y", T.F[:], T.ft[:], [], ["F"], 1048e3)
+    iota(T.LA[:], [[0, 512]], 0, 0, ["LA0", "LA1"], 512)
+    dma("y", T.LA[0::16, 0:256], T.lab[:], [], ["LA0"], 8e3)
+    dma("y", T.LA[0::16, 256:512], T.ask[:], [], ["LA1"], 8e3)
+    iota(T.IP[:, 0:1], [[0, 1]], 0, 1, ["IP"], 1)
+    iota(T.IX[:], [[1, 176]], 0, 0, ["IX"], 176)
+    ms(T.TB[:], 0.0, ["TB%d" % i for i in range(6)], 1024)
+    ts(T.IP[:, 1:2], T.IP[:, 0:1], 15, None, A.bitwise_and, None, ["IP"], ["IP1"], 1)
+    ts(T.IP[:, 2:3], T.IP[:, 0:1], 14, None, A.bitwise_and, None, ["IP"], ["IP2"], 1)
+    ts(T.IP[:, 3:4], T.IP[:, 0:1], 112, None, A.bitwise_and, None, ["IP"], ["IP3"], 1)
+    cp(c_k, T.IP[:, 1:2], ["IP1"], ["c_k"], 1)
+    ts(c_g, T.IP[:, 3:4], -1.0, 96.0, A.mult, A.add, ["IP3"], ["c_g"], 1)
+    ts(c_u1, T.IP[:, 1:2], 15.0, -16.0, A.is_equal, A.mult, ["IP1"], ["c_u1"], 1)
+    ts(c_u2, T.IP[:, 1:2], 15.0, 1536.0, A.is_equal, A.mult, ["IP1"], ["c_u2"], 1)
+    ts(c_ks, T.IP[:, 1:2], 1.0, 1.0 / 16, A.add, A.mult, ["IP1"], ["c_ks"], 1)
+    ts(c_kh, T.IP[:, 2:3], 500.0, None, A.mult, None, ["IP2"], ["c_kh"], 1)
+    ts(c_k5, T.IP[:, 1:2], 5.0, None, A.add, None, ["IP1"], ["c_k5"], 1)
+    ts(c_k4, T.IP[:, 1:2], 4.0, None, A.add, None, ["IP1"], ["c_k4"], 1)
+    ts(c_k0, T.IP[:, 1:2], 0.0, None, A.is_equal, None, ["IP1"], ["c_k0"], 1)
+    ts(c_nk, T.IP[:, 1:2], -1.0, None, A.mult, None, ["IP1"], ["c_nk"], 1)
+    ts(c_cap, T.IP[:, 1:2], 12.0, 15.0, A.max, A.subtract, ["IP1"], ["c_cap"], 1)
+    ts(c_32p, T.IP[:, 0:1], 32.0, None, A.mult, None, ["IP"], ["c_32p"], 1)
+    ts(c_p, T.IP[:, 0:1], -1.0, 128.0, A.mult, A.add, ["IP"], ["c_p"], 1)
+    ts(T.Yj[:], T.IX[:], c_g, None, A.add, None, ["IX", "c_g"], ["Yj"], 176)
+    ts(T.Yi[:], T.Yj[:], 127, None, A.bitwise_and, None, ["Yj"], ["Yi"], 176)
+    ts(T.MM[:], T.Yi[:], 0.0, -4.0, A.is_equal, A.mult, ["Yi"], ["MM"], 176)
+    ts(T.MF[:], T.Yi[:], 0.0, 1.0 / 4096, A.is_equal, A.mult, ["Yi"], ["MF"], 176)
+    ms(T.cst[:, 0:128], -0.5 / 128, ["cst"], 64)
+    ms(T.cst[:, 128:256], 864.0 / 4096 / 128, ["cst"], 64)
+    ts(T.M16[:], T.Yi[:], 0.0, None, A.is_equal, None, ["Yi"], ["M16"], 176)
+    ts(T.Ms[:], T.Yi[:], 0.0, 1.0 / 16, A.is_equal, A.mult, ["Yi"], ["Ms"], 176)
+    for r in range(3):
+        ts(T.Mr[:, 176 * r:176 * (r + 1)], T.Yi[:], c_kh, 1000.0 * r, A.add, A.is_equal, ["Yi", "c_kh"], ["Mr%d" % r], 176)
+    ts(T.Ym[:], T.Yi[:], 15.0, None, A.is_le, None, ["Yi"], ["Ym"], 176)
+    ts(T.Yj[:], T.Yi[:], 5.0, None, A.add, None, ["Yi"], ["Yj"], 176)
+    tt(T.Y5[:], T.Yj[:], T.Ym[:], A.mult, ["Yj", "Ym"], ["Y5"], 352)
+    cp(T.Blk[:], T.Ym[:], ["Ym"], ["Blk"], 176)
+    ts(T.B0F[:], T.Ym[:], c_k0, 1.0 / 4096, A.mult, A.mult, ["Ym", "c_k0"], ["B0F"], 176)
+    ts(T.B0[:], T.Ym[:], c_k0, 1.0 / 16, A.mult, A.mult, ["Ym", "c_k0"], ["B0"], 176)
+    ts(T.TriL[:], T.Y5[:, 32:160], c_k5, 16384.0, A.is_ge, A.mult, ["Y5", "c_k5"], ["TriL"])
+    ts(T.TriB[:], T.Y5[:, 32:160], c_k5, 32.0, A.is_ge, A.mult, ["Y5", "c_k5"], ["TriB"])
+    ts(T.I16[:], T.Y5[:, 32:160], c_k5, None, A.is_equal, None, ["Y5", "c_k5"], ["I16"])
+    ts(T.ShI[:], T.Y5[:, 32:160], c_k4, None, A.is_equal, None, ["Y5", "c_k4"], ["ShI"])
+    tt(T.TriB[:], T.TriB[:], T.I16[:], A.add, ["TriB", "I16"], ["TriB"])
+    tt(T.ShF[:], T.ShI[:], T.I16[:], A.subtract, ["ShI", "I16"], ["ShF"])
+    cp(T.ShI[:], T.ShF[:], ["ShF"], ["ShI"])
+    ts(T.CE2[:], T.IX[:, 0:128], 1.0 / 2048, None, A.mult, None, ["IX"], ["CE2"])
+    ts(T.CE1[:], T.CE2[:], 0.0, c_ks, A.mult, A.add, ["CE2", "c_ks"], ["CE1"])
+    ts(T.Yj[:, 0:144], T.IX[:, 0:144], c_p, None, A.add, None, ["IX", "c_p"], ["Yj"], 144)
+    ts(T.Yj[:, 0:144], T.Yj[:, 0:144], 127, None, A.bitwise_and, None, ["Yj"], ["Yj"], 144)
+    ts(T.IU[:], T.Yj[:, 0:144], 0.0, None, A.is_equal, None, ["Yj"], ["IU"], 144)
+    cp(T.Ibf[:], T.IU[:, 0:128], ["IU"], ["Ibf"], 128, True)
+    ts(T.ti[:, 0:3], T.taus[:, 0:3], 512.0, None, A.mult, None, ["taus"], ["ti"], 3)
+    ts(T.tw[:, 0:3], T.taus[:, 0:3], 512.0, None, A.mult, None, ["taus"], ["tw0"], 3)
+    tt(T.tw[:, 4:7], T.ti[:, 0:3], T.tw[:, 0:3], A.is_lt, ["ti", "tw0"], ["tw1"], 3)
+    tt(T.tw[:, 8:11], T.tw[:, 4:7], T.ti[:, 0:3], A.add, ["ti", "tw1"], ["tw2"], 3)
+    ts(T.tw[:, 12:15], T.tw[:, 8:11], -0.5, -1.0 / 512, A.add, A.mult, ["tw2"], ["tau"], 3)
+    cp(T.L1[:], T.bni[:], ["bni"], ["L1"], 384)
+    ts(T.bf[:], T.bni[:], -2048.0, None, A.add, None, ["bni"], ["bf"], 384)
+    cp(T.dig[:, 0:384], T.bf[:], ["bf"], ["dighi"], 384, True)
+    tt(T.dig[:, 384:768], T.bf[:], T.dig[:, 0:384], A.subtract, ["bf", "dighi"], ["diglo"], 768)
+    for p in range(2):
+        dma("y", T.TB[p::16, :], T.dig[:, 384 * p:384 * p + 128], ["dighi", "diglo"], ["TB%d" % p], 60e3)
+    send([(nxt, T.digl[:])], T.dig[:], ["dighi", "diglo"], ["digl"], 196e3)
+    send([(nx2, T.LAl[:])], T.LA[:], ["LA0", "LA1"], ["LAl"], 262e3)
+
+    def prevtable(t):
+        for p in range(2):
+            row = 2 * t + p
+            a = 384 * p + 128 * t
+            dma("y", T.TP[16 + row::16, :], T.digl[0:112, a:a + 128], ["digl"], ["TP%d" % row], 60e3)
+            dma("y", T.TP[row:row + 1, :], T.digl[112:128, a:a + 128], ["digl"], ["TP%d" % (row + 6)], 20e3)
+
+    for t in (1, 2):
+        for p in range(2):
+            dma("y", T.TB[2 * t + p::16, :], T.dig[:, 384 * p + 128 * t:384 * p + 128 * (t + 1)], ["dighi", "diglo"],
+                ["TB%d" % (2 * t + p)], 60e3)
+    for j in range(4):
+        iota(T.TP[:, 512 * j:512 * (j + 1)], [[0, 512]], 0, 0, ["TP%d" % i for i in range(12)], 512, True)
+    for t in range(EP):
+        prevtable(t)
+    dma("y", T.Fr[16:128, :], T.ft[0:112, :], [], ["Fr0"], 917e3)
+    dma("y", T.Fr[0:16, :], T.ft[112:128, :], [], ["Fr1"], 300e3)
+    dma("y", T.xvs[:], T.xv[:], [], ["xvs"], 98e3)
+    tbk = ["TB%d" % i for i in range(6)]
+    tpk = ["TP%d" % i for i in range(12)]
+    iota(T.SCi[:], [[16, 8], [1, 2]], 0, -1, ["SCi"], 16)
+    iota(T.SAi[:, 0:512], [[16, 8], [1, 2], [0, 32]], 0, -1, ["SAi"], 512)
+    iota(T.AL[:], [[0, 16], [1, 16], [16, 2]], -51200, 0, ["AL"], 512, True)
+    iota(T.SelW[:], [[0, 576]], 0, 0, ["SelW"], 576, True)
+    for base in (-16, 112):
+        add({"g": (0.2 + 1152 * CY, lambda x=base: g.affine_select(T.SelW[:], T.SelW[:], [[16, 9], [0, 64]], A.not_equal, 1.0, x, -1))},
+            ["SelW"], ["SelW"])
+    ts(T.SelC[:], T.SCi[:], 0.0, None, A.is_equal, None, ["SCi"], ["SelC"], 16)
+    ts(T.SelA[:], T.SAi[:, 0:512], 0.0, None, A.is_equal, None, ["SAi"], ["SelA"], 512)
+    ts(T.SelN[:], T.SelA[:], -32.0, None, A.mult, None, ["SelA"], ["SelN"], 256)
+    ms(T.zero[:], 0.0, ["zero"], 128)
+    ts(T.I4k[:], T.IU[:, 0:128], 2048.0, None, A.mult, None, ["IU"], ["I4k"])
+    ts(T.Dg[:], T.IU[:, 0:128], c_32p, None, A.mult, None, ["IU", "c_32p"], ["Dg"])
+    ms(T.ones[:], 1.0, ["ones"], 64)
+    ts(T.IB[:], T.IX[:, 0:128], 1536.0, None, A.add, None, ["IX"], ["IB"])
+    ms(T.WA[:, 2 * NW - 1:2 * NW], 0.0, ["HzA"], 1)
+    ms(T.WB[:, 2 * NW - 1:2 * NW], 0.0, ["HzB"], 1)
+    ts(T.nask[:], T.LAl[:, 256:512], -1.0, 0.5, A.mult, A.add, ["LAl"], ["nask"], 256)
+    ts(T.sig[:], T.LAl[:, 0:256], -262146.0, 2.0, A.mult, A.add, ["LAl"], ["sig"], 256)
+
+    def fwtable(t):
+        for j in range(8):
+            b = 6 + j % 2
+            sl = slice(512 * j, 512 * (j + 1))
+            mm([(ps[b][:], T.Ibf[:], W[t][:, sl], True, True)], ["Ibf", wk[t][j]], ["ps%d" % b], 512)
+            tt(T.FW[:, sl], ps[b][:], T.F[:, sl], A.mult, ["F", "ps%d" % b], [fwk[j], "ps%d" % b], 512)
+
+    def halves(t):
+        n = "AB"[t]
+        for j in range(4):
+            a, b = 1024 * j, 1024 * (j + 1)
+            src = wk[t][2 * j:2 * j + 2]
+            e = b - 1 if j == 3 else b
+            ts(W[t][:, NW + a:NW + e], W[t][:, a:e], 0.5, 0.25, A.mult, A.max, src, ["H%s%d" % (n, j)], 512)
+            ts(W[t][:, 2 * NW + a:2 * NW + b], W[t][:, a:b], 2.0, 4.0, A.mult, A.min, src, ["D%s%d" % (n, j)], 512)
+
+    def names(Pm, pk, roll, off, out, okey, xb, xk):
+        c0 = 16 if roll else 32
+        u = ps[5][:, 0:128]
+        mm([(u, T.ShF[:], Pm, True, False)], pk + ["ShF"], ["ps5"], 512)
+        mm([(u, T.TriL[:], T.nn[:], False, True)], ["TriL", "nn"], ["ps5"], 128)
+        o = ps[3][:, 0:128]
+        lst = [(o, Pm, T.B0F[:, c0:c0 + 128], True, False)]
+        if off:
+            lst.append((o, T.ones[:], T.cst[:, 128 * off - 128:128 * off], False, False))
+        mm(lst, pk + ["B0F", "ones", "cst"], ["ps3"], 640)
+        for v in range(16):
+            act(T.RL[:, 128 * v:128 * (v + 1)], u, AF.Relu, 8192.0 + 16384.0 * v, 1.0, ["ps5"], ["RL%d" % v])
+            if v % 2 == 1:
+                mm([(ps[3][:, x:128:16], T.RL[:, 128 * x:128 * (x + 1)], T.MF[:, c0:c0 + 128:16], False, x == 15) for x in (v - 1, v)],
+                   ["RL%d" % (v - 1), "RL%d" % v, "MF"], ["ps3"], 512)
+        ts(xb, o, 2.0 ** -13, None, A.add, None, ["ps3"], ["ps3", xk])
+        tt(T.xt[:], o, xb, A.subtract, ["ps3", xk], ["ps3", "xt"], 128)
+        if xk == "xi":
+            mm([(ps[3][:, 128:256], T.I16[:], T.flag[:], True, False), (ps[3][:, 128:256], T.xt[:], T.I16[:], False, True)],
+               ["xt", "I16", "flag"], ["ps3"], 256)
+        else:
+            mm([(ps[3][:, 128:256], T.xt[:], T.I16[:], True, True)], ["xt", "I16"], ["ps3"], 128)
+        ts(out, ps[3][:, 128:256], 4096.0, 2048.0, A.mult, A.add, ["ps3"], ["ps3", okey])
+
+    def children(last, lk, Pm, pk, off, roll, tab, tk, t, outL, outP, okey, Lp, pkey, Ln, nkey):
+        c0 = 16 if roll else 32
+        u, o = ps[1][:, 0:128], ps[2][:, 0:128]
+        boost[0] = UP
+        lst = [(o, T.I16[:], T.CE1[:], True, False), (o, T.I16[:], T.CE2[:], False, False)]
+        if last is not None:
+            mm([(u, T.ShI[:], last, True, False)], lk + ["ShI"], ["ps1"], 128)
+            lst.append((o, T.B0[:, c0:c0 + 128], last, False, False))
+        mm(lst, lk + ["I16", "CE1", "CE2", "B0"], ["ps2"], 384)
+        mm([(u, T.TriB[:], T.nn[:], last is None, True)], ["TriB", "nn"], ["ps1"], 128)
+        if last is None:
+            ts(T.ua[:], u, c_u1, 17.0, A.add, A.add, ["ps1", "c_u1"], ["ps1", "ua"])
+        else:
+            ts(T.ua[:], u, c_u2, 16.0, A.add, A.add, ["ps1", "c_u2"], ["ps1", "ua"])
+        for v in range(16):
+            ts(T.R[:, 128 * v:128 * (v + 1)], T.ua[:], 32.0 * v, 0.0, A.add, A.max, ["ua"], ["R%d" % v], 64)
+            if v % 4 == 3:
+                mm([(o, T.Ms[:, c0 - x:c0 + 128 - x], T.R[:, 128 * x:128 * (x + 1)], False, x == 15) for x in range(v - 3, v + 1)],
+                   ["R%d" % x for x in range(v - 3, v + 1)] + ["Ms"], ["ps2"], 512)
+        ts(T.qi[:], o, -0.5 + 2.0 ** -12, None, A.add, None, ["ps2"], ["ps2", "qi"])
+        tt(T.fr[:], o, T.qi[:], A.subtract, ["ps2", "qi"], ["ps2", "fr"], 128)
+        ts(T.IDX[:], T.fr[:], 2048.0, None, A.mult, None, ["fr"], ["IDX"])
+        boost[0] = 0.0
+        mm([(ps[1][:, 128:256], T.Blk[:, c0:c0 + 128], T.nn[:], True, True)], ["Blk", "nn"], ["ps1"], 128)
+        ts(T.flag[:], ps[1][:, 128:256], c_nk, -8.0, A.is_ge, A.mult, ["ps1", "c_nk"], ["ps1", "flag"])
+        names(Pm, pk, roll, off, outP, okey + "P", T.xi[:], "xi")
+        gather("copy", T.GB, "GB", tab, tk, T.IDX, 0, ["IDX"])
+        act(Lp, ps[3][:, 128:256], AF.Relu, 3232.0, 4096.0, ["ps3"], ["ps3", pkey])
+        act(T.lin[:], ps[3][:, 128:256], AF.Relu, 65.0 * 2048 + 2048 + 4096 * 110 - 4095, 65.0 * 4096, ["ps3"], ["ps3", "lin"])
+        act(T.lin[:], T.lin[:], AF.Identity, 4095.0, 1.0, ["lin"], ["lin"])
+        narrow(ps[0], "ps0", T.Mr, "Mr%d" % t, T.GB, "GB", 176 * t)
+        tt(T.pa[:], ps[0][:, 0:128], Lp, A.mult, ["ps0", pkey], ["ps0", "pa"], 128)
+        ts(T.pb[:], T.pa[:], 5, None, A.arith_shift_right, None, ["pa"], ["pb"])
+        tt(T.pa[:], T.pb[:], T.lin[:], A.add, ["pb", "lin"], ["pa"])
+        ts(T.pb[:], T.pa[:], 4095, None, A.bitwise_and, None, ["pa"], ["pb"])
+        cp(outL, T.pb[:], ["pb"], [okey + "L"])
+        if Ln is not None:
+            cp(Ln, T.pb[:], ["pb"], [nkey])
+
+    def onehots(d, names, nk):
+        ts(T.ndb[:, 0:128], names, 1.0 / 32, 1536.0 - 31.0 / 64, A.mult, A.add, nk, ["nd0"])
+        ts(T.ndb[:, 128:256], names, -2048.0, None, A.add, None, nk, ["nd1"])
+        mm([(ps[6][:, 0:16], T.ndb[:, 0:128], T.SelC[:], True, True)], ["nd0", "SelC"], ["ps6"], 64)
+        cp(T.bT[:, 16 * d:16 * (d + 1)], ps[6][:, 0:16], ["ps6"], ["ps6", "bT%d" % d], 16, True)
+        mm([(ps[7][:], T.ndb[:, 128:256], T.SelA[:], True, False), (ps[7][:], T.ndb[:, 0:128], T.SelN[:], False, True)],
+           ["nd0", "nd1", "SelA", "SelN"], ["ps7"], 1024)
+        tt(T.AA[:, 512 * d:512 * (d + 1)], ps[7][:], T.AL[:], A.is_equal, ["ps7", "AL"], ["ps7", "AA%d" % d], 512)
+        for c in range(16 * d, 16 * (d + 1)):
+            ts(T.OH[:, 128 * c:128 * (c + 1)], T.IB[:], T.bT[:, c:c + 1], None, A.is_equal, None, ["IB", "bT%d" % d], ["OH%d" % c], 64)
+
+    def weigh(d, wgt, k, b):
+        o = 0 if d == 2 else 64
+        mm([(ps[b][:], wgt, T.SelW[:, o:o + 512], True, True)], [k, "SelW"], ["ps%d" % b], 512)
+        tt(T.Aw[:, 512 * d:512 * (d + 1)], ps[b][:], T.AA[:, 512 * d:512 * (d + 1)], A.mult, ["ps%d" % b, "AA%d" % d],
+           ["ps%d" % b, "Aw%d" % d], 512)
+
+    for t in range(EP):
+        n = str(t)
+        up = t < EP - 1
+        Wt = W[t][:, 0:NW]
+        a, b = 128 * t, 128 * (t + 1)
+        gather("cmp", T.C, "C", Wt, wk[t], T.L1, a, ["L1"], 0)
+        narrow(ps[0], "ps0", T.MM, "MM", T.C, "C")
+        ts(T.nn[:], ps[0][:, 0:128], c_cap, 0.0, A.max, A.min, ["ps0", "c_cap"], ["ps0", "nn"])
+        o1 = 384 * t
+        ts(T.s1c[:, o1 + 256:o1 + 384], ps[0][:, 0:128], -0.5, None, A.is_lt, None, ["ps0"], ["ps0", "s1c2" + n])
+        children(None, [], T.bf[:, a:b], ["bf"], 0, False, T.TB[:, :], tbk, t, T.s1a[:, 2 * a:2 * a + 128], T.s1a[:, 2 * a + 128:2 * b],
+                 "s1a" + n, T.s1b[:, 2 * a + 128:2 * b], "s1bP" + n, T.s1b[:, 2 * a:2 * a + 128], "s1bL" + n)
+        send([(nxt, T.l1a[:, 2 * a:2 * b])], T.s1a[:, 2 * a:2 * b], ["s1a" + n + "L", "s1a" + n + "P"], ["l1a" + n], 65e3)
+        send([(nxt, T.l1b[:, 2 * a:2 * b])], T.s1b[:, 2 * a:2 * b], ["s1bL" + n, "s1bP" + n, "s1a" + n + "L"], ["l1b" + n], 131e3)
+        ts(T.s1c[:, o1:o1 + 128], T.fr[:], 16.0, 1535.504, A.mult, A.add, ["fr"], ["s1c0" + n])
+        ts(T.s1c[:, o1 + 128:o1 + 256], T.s1c[:, o1:o1 + 128], 1548.0, 1551.0, A.max, A.subtract, ["s1c0" + n], ["s1c1" + n], 64)
+        send([(nxt, T.l1c[:, o1:o1 + 384])], T.s1c[:, o1:o1 + 384], ["s1c%d%s" % (i, n) for i in range(3)], ["l1c" + n], 98e3)
+        fwtable(t)
+        gather("scopy", T.X1, "X1", T.FW[:, :], fwk, T.L1, a, ["L1"])
+        if up:
+            onehots(0, T.L1[:, a:b], ["L1"])
+        gather("cmp", T.C, "C", Wt, wk[t], T.l1a, 2 * a, ["l1a" + n], 1)
+        narrow(ps[0], "ps0", T.MM, "MM", T.C, "C")
+        tt(T.nt[:], ps[0][:, 0:128], T.l1c[:, o1 + 128:o1 + 256], A.max, ["ps0", "l1c" + n], ["ps0", "nt"], 128)
+        ts(T.nn[:], T.nt[:], 0.0, None, A.min, None, ["nt"], ["nn"], 64)
+        ts(T.st[:], ps[0][:, 0:128], -0.5, None, A.is_lt, None, ["ps0"], ["ps0", "st"])
+        tt(T.s2c[:, a:b], T.st[:], T.l1c[:, o1 + 256:o1 + 384], A.add, ["st", "l1c" + n], ["s2c" + n])
+        send([(nxt, T.l2c[:, a:b])], T.s2c[:, a:b], ["s2c" + n], ["l2c" + n], 32e3)
+        children(T.l1c[:, o1:o1 + 128], ["l1c" + n], T.l1b[:, 2 * a:2 * a + 128], ["l1b" + n], 1, True, T.TP[:, :], tpk, t,
+                 T.s2a[:, 2 * a:2 * a + 128], T.s2a[:, 2 * a + 128:2 * b], "s2a" + n, T.Lp[:], "Lp", None, None)
+        send([(nxt, T.l2a[:, 2 * a:2 * b])], T.s2a[:, 2 * a:2 * b], ["s2a" + n + "L", "s2a" + n + "P"], ["l2a" + n], 65e3)
+        names(T.l1b[:, 2 * a + 128:2 * b], ["l1b" + n], True, 2, T.s2b[:, a:b], "s2b" + n, T.xj[:], "xj")
+        send([(nxt, T.l2b[:, a:b])], T.s2b[:, a:b], ["s2b" + n], ["l2b" + n], 32e3)
+        b1, b2 = (4, 4) if up else (6, 7)
+        reduce(ps[b1], "ps%d" % b1, T.IU[:, 0:128], T.X1, "X1")
+        cp(T.S1[:], ps[b1][:, 0:128], ["ps%d" % b1], ["ps%d" % b1, "S1"], 128, True)
+        gather("scopy", T.X2, "X2", T.FW[:, :], fwk, T.l1a, 2 * a, ["l1a" + n])
+        gather("mult", T.X2, "X2", T.F[:, :], ["F"], T.l1a, 2 * a + 128, ["l1a" + n])
+        reduce(ps[b2], "ps%d" % b2, T.IU[:, 0:128], T.X2, "X2")
+        cp(T.s4[:, a:b], ps[b2][:, 0:128], ["ps%d" % b2], ["ps%d" % b2, "s4" + n], 128, True)
+        send([(prv, T.l4[:, a:b])], T.s4[:, a:b], ["s4" + n], ["l4" + n], 65e3)
+        if up:
+            halves(t)
+            onehots(1, T.l1a[:, 2 * a:2 * a + 128], ["l1a" + n])
+        gather("cmp", T.C, "C", Wt, wk[t], T.l2a, 2 * a, ["l2a" + n], 2)
+        narrow(ps[0], "ps0", T.MM, "MM", T.C, "C")
+        ts(T.st[:], ps[0][:, 0:128], -0.5, None, A.is_lt, None, ["ps0"], ["ps0", "st"])
+        if up:
+            o = ps[2][:, 0:128]
+            mm([(o, T.M16[:, 32:160], T.l2c[:, a:b], True, False), (o, T.I16[:], T.nask[:, a:b], False, False)],
+               ["M16", "I16", "nask", "l2c" + n], ["ps2"], 256)
+            mm([(o, T.M16[:, 48:176], T.st[:], False, True)], ["M16", "st"], ["ps2"], 128)
+            tt(T.tv[:], o, T.sig[:, a:b], A.mult, ["ps2", "sig"], ["ps2", "tv"], 128)
+            ts(T.s3[:, a:b], T.tv[:], 0.0, None, A.max, None, ["tv"], ["s3" + n])
+            send([(prv, T.l3a[:, a:b]), (prv2, T.l3b[:, a:b])], T.s3[:, a:b], ["s3" + n], ["l3" + n], 65e3)
+            onehots(2, T.l2a[:, 2 * a:2 * a + 128], ["l2a" + n])
+        o = ps[0][:, 128:256]
+        mm([(o, T.M16[:, 32:160], T.l2c[:, a:b], True, False), (o, T.M16[:, 48:176], T.st[:], False, True)],
+           ["M16", "st", "l2c" + n], ["ps0"], 256)
+        cp(T.s5[:, 2 * a + 128:2 * b], o, ["ps0"], ["ps0", "s5v" + n], 128, True)
+        gather("scopy" if up else "copy", T.X3, "X3", T.FW[:, :], fwk, T.l2a, 2 * a, ["l2a" + n])
+        if up:
+            weigh(2, T.s3[:, a:b], "s3" + n, 6)
+            weigh(1, T.l3a[:, a:b], "l3" + n, 7)
+            weigh(0, T.l3b[:, a:b], "l3" + n, 6)
+            mm([(ps[1][:, 0:256], T.ones[:], T.zero[:], True, False)], ["ones", "zero"], ["ps1"], 256)
+            for d in (2, 1, 0):
+                cs = range(16 * d, 16 * (d + 1))
+                mm([(ps[1][:, 32 * (c % 16 // 2):32 * (c % 16 // 2 + 1)], T.OH[:, 128 * c:128 * (c + 1)], T.Aw[:, 32 * c:32 * (c + 1)], False, c == 15)
+                    for c in cs], ["Aw%d" % d] + ["OH%d" % c for c in cs], ["ps1"], 16 * 64)
+            act(T.s1[:], ps[1][:, 0:256], AF.Sign, -0.5, 1.0, ["ps1"], ["s1"], 256)
+            act(T.s2[:], ps[1][:, 0:256], AF.Sign, -100000.5, 1.0, ["ps1"], ["s2"], 256)
+            lst = []
+            for x in range(2):
+                o = ps[2][:, 128 * x:128 * (x + 1)]
+                lst += [(o, T.ones[:], T.Dg[:], True, False), (o, T.s1[:, x::2], T.I4k[:], False, False), (o, T.s2[:, x::2], T.I4k[:], False, True)]
+            mm(lst, ["ones", "Dg", "s1", "s2", "I4k"], ["ps2"], 768)
+            ts(T.UL[:, 0::2], ps[2][:, 0:128], c_k, 4096.0, A.add, A.add, ["ps2", "c_k"], ["UL0"])
+            ts(T.UL[:, 1::2], ps[2][:, 128:256], c_k, 4112.0, A.add, A.add, ["ps2", "c_k"], ["UL1"])
+            nm = "AB"[t]
+            src = wk[t] + ["%s%s%d" % (x, nm, j) for x in "HD" for j in range(4)] + ["Hz" + nm, "UL0", "UL1"]
+            for j in range(8):
+                s_ = W[t][:, :].indirect(T.UL[:, 32 * j:32 * (j + 1)])
+                d_ = W[t + 1][:, 512 * j:512 * (j + 1)]
+                u = FIX + 512 * GC * CY
+                add({"v": (u, lambda s=s_, x=d_: V.tensor_copy(x, s)), "s": (u, lambda s=s_, x=d_: S.activation(x, s, AF.Copy))},
+                    src, [wk[t + 1][j]])
+        gather("mult", T.X3, "X3", T.Fr[:, :], ["Fr0", "Fr1"], T.l2a, 2 * a + 128, ["l2a" + n])
+        gather("mult", T.X3, "X3", T.Fr[:, :], ["Fr0", "Fr1"], T.l2b, a, ["l2b" + n])
+        reduce(ps[4], "ps4", T.IU[:, 16:144], T.X3, "X3")
+        cp(T.s5[:, 2 * a:2 * a + 128], ps[4][:, 0:128], ["ps4"], ["ps4", "s5s" + n], 128, True)
+        send([(prv2, T.l5[:, 2 * a:2 * b])], T.s5[:, 2 * a:2 * b], ["s5s" + n, "s5v" + n], ["l5" + n], 131e3)
+        o, bk = ps[b1][:, 128:256], "ps%d" % b1
+        mm([(o, T.IU[:, 0:128], T.S1[:], True, False), (o, T.IU[:, 0:128], T.l4[:, a:b], False, False)], ["IU", "S1", "l4" + n], [bk], 1024)
+        mm([(o, T.IU[:, 0:128], T.l5[:, 2 * a:2 * a + 128], False, True)], ["IU", "l5" + n], [bk], 512)
+        tt(T.ys[:, a:b], o, T.xvs[:, a:b], A.mult, [bk, "xvs"], [bk, "ys" + n], 128)
+        dma("y", T.cv[:, a:b], T.l5[0::16, 2 * a + 128:2 * b], ["l5" + n], ["cv" + n], 8e3)
+        dma("y", T.y[:, a:b], T.ys[:, a:b], ["ys" + n], ["y" + n], 65e3)
+    return ops
+
+
+def depends(ops):
+    lastw, readers, deps = {}, {}, []
+    for i, o in enumerate(ops):
+        d = set()
+        for k in o["r"] + o["w"]:
+            if k in lastw:
+                d.add(lastw[k])
+        for k in o["w"]:
+            d.update(readers.get(k, []))
+        d.discard(i)
+        deps.append(sorted(d))
+        for k in o["r"]:
+            readers.setdefault(k, []).append(i)
+        for k in o["w"]:
+            lastw[k] = i
+            readers[k] = []
+    return deps
+
+
+def schedule(ops, deps):
+    n = len(ops)
+    succ = [[] for _ in range(n)]
+    for i in range(n):
+        for d in deps[i]:
+            succ[d].append(i)
+    full = [min(a[0] for a in o["alts"].values()) + o["lat"] + (1.6 if o["kind"] == "dma" else 0.0) + WAKE for o in ops]
+    prio = [0.0] * n
+    for i in range(n - 1, -1, -1):
+        prio[i] = full[i] + max([prio[s] for s in succ[i]] + [0.0])
+    prio = [prio[i] + ops[i]["up"] for i in range(n)]
+    best = None
+    rng = np.random.default_rng(1)
+    lean = [LEAN] * n
+    keep = prio
+    head = {}
+    run = []
+    for i, o in enumerate(ops):
+        k = o["w"][0].rstrip("0123456789")
+        if k not in head or i - head[k][1] > 2 or k == "ps":
+            head[k] = [i, i]
+        head[k][1] = i
+        run.append(head[k][0])
+    for rnd in range(ROUNDS):
+        plan = forward(ops, deps, succ, prio, lean)
+        if best is None or max(plan[3]) < max(best[3]):
+            best, keep = plan, prio
+        if rnd % 4 == 3:
+            plan = best
+        late = backward(ops, deps, succ, plan)
+        noise = rng.random(n)[run] * (NOISE if rnd % 4 == 3 else 0.0)
+        prio = [MIX * prio[i] + (1 - MIX) * (late[i] + ops[i]["up"]) + float(noise[i]) for i in range(n)]
+    for rnd in range(CLIMB):
+        step = (rng.normal(0.0, NOISE, n) * (rng.random(n) < 0.06))[run]
+        flip = rng.random(n) < 0.03
+        prio = [keep[i] + float(step[i]) for i in range(n)]
+        trial = [LEAN - lean[i] if flip[i] else lean[i] for i in range(n)]
+        plan = forward(ops, deps, succ, prio, trial)
+        if max(plan[3]) <= max(best[3]):
+            best, keep, lean = plan, prio, trial
+    return best
+
+
+def backward(ops, deps, succ, plan):
+    order, where, start, fin = plan
+    n = len(ops)
+    left = [len(s) for s in succ]
+    ready = [0.0] * n
+    late = [0.0] * n
+    pool = {q: [] for q in order}
+    free = {q: 0.0 for q in order}
+    lag = [o["lat"] + (1.6 if o["kind"] == "dma" else 0.0) for o in ops]
+    for i in range(n):
+        if left[i] == 0:
+            ready[i] = lag[i]
+            pool[where[i]].append(i)
+    for _ in range(n):
+        pick = None
+        for q in pool:
+            if pool[q]:
+                t0 = max(free[q], min(ready[i] for i in pool[q]))
+                if pick is None or t0 < pick[0]:
+                    pick = (t0, q)
+        t0, q = pick
+        c = max([i for i in pool[q] if ready[i] <= t0 + 1e-9], key=lambda i: fin[i])
+        pool[q].remove(c)
+        free[q] = late[c] = t0 + ops[c]["alts"][q][0]
+        for d in deps[c]:
+            ready[d] = max(ready[d], late[c] + lag[d] + (0.0 if q == "p" and where[d] == "p" else WAKE))
+            left[d] -= 1
+            if left[d] == 0:
+                pool[where[d]].append(d)
+    return late
+
+
+def forward(ops, deps, succ, prio, lean):
+    n = len(ops)
+    left = [len(d) for d in deps]
+    ready = [0.0] * n
+    pool = [i for i in range(n) if left[i] == 0]
+    free = {q: 0.0 for q in "vspgy"}
+    order = {q: [] for q in "vspgy"}
+    where, fin, start = [None] * n, [0.0] * n, [0.0] * n
+    wire = 0.0
+    done = 0
+    while done < n:
+        best = None
+        for q in "vspgy":
+            cand = [i for i in pool if q in ops[i]["alts"]]
+            if not cand:
+                continue
+            t0 = max(free[q], min(ready[i] for i in cand))
+            now = [i for i in cand if ready[i] <= t0 + 1e-9]
+            c = max(now, key=lambda i: (prio[i] - (lean[i] if len(ops[i]["alts"]) > 1 and q == "v" else 0.0), -i))
+            dur = ops[c]["alts"][q][0]
+            soon = [i for i in cand if t0 < ready[i] < t0 + LOOK * dur and prio[i] > prio[c] + MARGIN]
+            if soon:
+                c = min(soon, key=lambda i: ready[i])
+                t0 = ready[c]
+            if best is None or t0 < best[0]:
+                best = (t0, q, c)
+        t0, q, c = best
+        o = ops[c]
+        dur = o["alts"][q][0]
+        free[q] = t0 + dur
+        end = t0 + dur
+        if o["kind"] == "dma":
+            wire = max(wire, end + 1.0) + o["lat"]
+            end = wire + 0.6
+        elif o["kind"] == "msg":
+            end += o["lat"]
+        where[c], start[c], fin[c] = q, t0, end
+        order[q].append(c)
+        pool.remove(c)
+        done += 1
+        for s in succ[c]:
+            same = q == "p" and "p" in ops[s]["alts"]
+            ready[s] = max(ready[s], end + (0.0 if same else WAKE))
+            left[s] -= 1
+            if left[s] == 0:
+                pool.append(s)
+    return order, where, start, fin
+
+
+PLAN = {}
+
+
+def rank_program(g, core, T, topo):
+    rank = T.rank_of(core)
+    if rank is None:
+        return
+    N = len(T.cores)
+    peer = [T.cores[(rank + j) % N] for j in (1, -1, -2, 2)]
+    ops = build(g, T, peer[0], peer[1], peer[2], peer[3])
+    if "p" not in PLAN:
+        deps = depends(ops)
+        PLAN["p"] = (deps, schedule(ops, deps))
+    deps, (order, where, start, fin) = PLAN["p"]
+    queue = {"v": g.vector, "s": g.scalar, "p": g.tensor, "g": g, "y": g.sync}
+    n = len(ops)
+    pos = [0] * n
+    for q in order:
+        for j, i in enumerate(order[q]):
+            pos[i] = j
+    need, waits = [False] * n, [[] for _ in range(n)]
+    for q in order:
+        seen, got = {}, set()
+        for i in order[q]:
+            top = {}
+            for d in deps[i]:
+                if ops[d]["kind"] != "c":
+                    if d not in got:
+                        got.add(d)
+                        waits[i].append(d)
+                elif not (q == "p" and where[d] == "p"):
+                    e = where[d]
+                    if pos[d] > seen.get(e, -1) and (e not in top or pos[d] > pos[top[e]]):
+                        top[e] = d
+            for e in top:
+                seen[e] = pos[top[e]]
+                need[top[e]] = True
+                waits[i].append(top[e])
+    mark, nd, nm = [None] * n, 0, 0
+    for q in order:
+        c = 0
+        for i in order[q]:
+            if ops[i]["kind"] == "c" and need[i]:
+                c += 1
+                mark[i] = (T.sem["q" + q], c)
+    for i in range(n):
+        if ops[i]["kind"] == "dma":
+            mark[i] = (T.sem["d%d" % nd], 16)
+            nd += 1
+        elif ops[i]["kind"] == "msg":
+            mark[i] = (T.sem["a%d" % nm], len(topo.engines(core, peer[0])))
+            nm += 1
+    waited = set()
+    sent = 0
+    for q in order:
+        for i in order[q]:
+            for d in waits[i]:
+                queue[q].wait_ge(mark[d][0], mark[d][1])
+                waited.add(d)
+            o = ops[i]
+            if o["kind"] == "msg":
+                dsts, src = o["alts"][q][1]
+                if len(dsts) == 1:
+                    rid, pid, _ = topo.addr(dsts[0][0])
+                    g.remote_dma(dsts[0][1], src, mark[i][0], T.sem.sent, pid, rid, topo.mask(core, dsts[0][0]))
+                    sent += len(topo.engines(core, dsts[0][0]))
+                else:
+                    trs = []
+                    for j, (dst, ap) in enumerate(dsts):
+                        en = topo.engines(core, dst)
+                        en = en[j * len(en) // 2:(j + 1) * len(en) // 2]
+                        rid, pid, _ = topo.addr(dst)
+                        trs.append(RemoteDMATransfer(dst_ids=[DstId(rid=rid, pnc=pid)], dma_engine_mask=sum(1 << x for x in en),
+                                                     remote_sem=mark[i][0], src=src, dst=ap))
+                        sent += len(en)
+                    g.remote_dma_fused(trs, local_sem=T.sem.sent)
+            else:
+                ins = o["alts"][q][1]()
+                if o["kind"] == "dma":
+                    ins.then_inc(mark[i][0], 16)
+                elif need[i]:
+                    ins.then_inc(mark[i][0], 1)
+    for i in range(n):
+        if ops[i]["kind"] != "c" and i not in waited:
+            g.sync.wait_ge(mark[i][0], mark[i][1])
+    g.wait_ge(T.sem.sent, sent)

@@ -1,9 +1,15 @@
+import math
 import numpy as np
 from concourse.bass import DstId, RemoteDMATransfer
 from concourse.mybir import AluOpType as A, ActivationFunctionType as AF
 
 NW, E, EP = 4096, 128, 3
 BF, F16, F32, I32, U16 = "bfloat16", "float16", "float32", "int32", "uint16"
+NH = 2
+HE = E // NH
+BETA = 2296
+E2, E3 = 6144, 3 * BETA
+BIG, FNW = 2.0 ** 23, 147456.0
 
 
 def _sb(n, d):
@@ -11,46 +17,47 @@ def _sb(n, d):
 
 
 SCRATCH = {
-    "WA": _sb(3 * NW, BF), "WB": _sb(3 * NW, BF), "F": _sb(NW, BF), "Fr": _sb(NW, BF), "FW": _sb(NW, F32),
-    "X1": _sb(2048, F32), "X2": _sb(2048, F32), "X3": _sb(2048, F32), "C": _sb(2048, BF), "GB": _sb(2048, BF),
-    "TB": _sb(2048, BF), "TP": _sb(2048, BF), "R": _sb(2048, F16), "RL": _sb(2048, F32), "OH": _sb(48 * 128, BF), "AA": _sb(1536, BF),
-    "Aw": _sb(1536, BF),
-    "bni": _sb(384, I32), "taus": _sb(4, F32), "tw": _sb(16, F32), "ti": _sb(4, I32), "xvs": _sb(384, BF),
-    "LA": _sb(512, I32), "LAl": _sb(512, I32), "nask": _sb(256, F16), "sig": _sb(256, F32),
-    "dig": _sb(768, BF), "digl": _sb(768, BF), "L1": _sb(384, U16), "bf": _sb(384, F32),
-    "IX": _sb(176, I32), "IP": _sb(4, I32), "col": _sb(16, F32), "Yi": _sb(176, I32), "Yj": _sb(176, I32), "Ym": _sb(176, F32),
-    "Y5": _sb(176, F16), "MM": _sb(176, BF), "M16": _sb(176, F16), "Ms": _sb(176, F16), "MF": _sb(176, F32), "Mr": _sb(6 * 176, BF),
-    "B0": _sb(176, F16), "B0F": _sb(176, F32), "Blk": _sb(176, F16), "TriL": _sb(128, F16), "TriB": _sb(128, F16),
-    "I16": _sb(128, F16), "ShI": _sb(128, F16), "ShF": _sb(128, F32), "IU": _sb(144, F32), "CE1": _sb(128, F16), "CE2": _sb(128, F16),
-    "Ibf": _sb(128, BF), "I4k": _sb(128, BF), "Dg": _sb(128, BF), "ones": _sb(128, BF), "zero": _sb(256, BF), "cst": _sb(256, BF), "xt": _sb(128, F16), "IB": _sb(128, F16),
-    "SCi": _sb(16, I32), "SelC": _sb(16, F16), "SAi": _sb(576, I32), "SelA": _sb(512, F16),
-    "SelN": _sb(512, F16), "SelW": _sb(576, BF), "AL": _sb(512, F32),
-    "nn": _sb(128, F16), "nt": _sb(128, F16), "st": _sb(128, F16), "ua": _sb(128, F16), "xi": _sb(128, I32), "xj": _sb(128, I32),
-    "qi": _sb(128, I32), "fr": _sb(128, F32), "IDX": _sb(128, U16), "Lp": _sb(128, F32), "lin": _sb(128, F32),
-    "flag": _sb(128, F16), "pa": _sb(128, I32), "pb": _sb(128, I32), "S1": _sb(128, F32),
-    "ndb": _sb(256, F16), "bT": _sb(48, F32), "tv": _sb(128, F32),
-    "s1": _sb(256, BF), "s2": _sb(256, BF), "UL": _sb(256, U16), "ys": _sb(384, F32),
-    "s1a": _sb(768, U16), "l1a": _sb(768, U16), "s1b": _sb(768, F32), "l1b": _sb(768, F32), "s1c": _sb(1152, F16), "l1c": _sb(1152, F16),
-    "s2a": _sb(768, U16), "l2a": _sb(768, U16), "s2b": _sb(384, U16), "l2b": _sb(384, U16),
-    "s2c": _sb(384, F16), "l2c": _sb(384, F16), "s3": _sb(256, BF), "l3a": _sb(256, BF), "l3b": _sb(256, BF),
-    "s4": _sb(384, F32), "l4": _sb(384, F32), "s5": _sb(768, F32), "l5": _sb(768, F32),
+    "WA": _sb(4 * NW, BF), "W2": _sb(NW, BF), "W3": _sb(NW, BF), "F": _sb(NW, BF), "Fr": _sb(NW, BF),
+    "D0": ("dram", [144, 2048], BF), "D1": ("dram", [144, 2048], BF), "DT": ("dram", [32, 8192], BF),
+    "TT": _sb(4352, BF), "T2": _sb(E2 + 16, BF), "T3": _sb(E3 + 8, BF), "G3": _sb(2048, BF),
+    "Wg1": _sb(2048, BF), "Wg2": _sb(2048, BF), "Wg3": _sb(2048, BF), "C": _sb(2048, BF),
+    "X1": _sb(2048, F32), "X2": _sb(2048, F32), "X3": _sb(2048, F32), "V2": _sb(2048, F32),
+    "OH": _sb(48 * 128, BF), "Aw": _sb(1536, BF), "GA": _sb(512, BF), "GB": _sb(512, BF),
+    "SF": _sb(2560, BF), "VV": _sb(160, BF), "YY": _sb(288, BF), "YQ": _sb(288, F32), "RT": _sb(640, F16), "fe": _sb(384, BF),
+    "ST": _sb(2816, BF), "na": _sb(384, I32), "nb": _sb(384, I32), "bni": _sb(384, I32),
+    "taus": _sb(4, F32), "tau1": _sb(8, F32), "tau2": _sb(8, F32), "tau3": _sb(8, F32), "taur": _sb(8, F32),
+    "tw": _sb(16, F32), "ti": _sb(4, I32), "xvs": _sb(384, BF), "LA": _sb(512, I32), "nask": _sb(256, BF), "sig": _sb(256, F32),
+    "dig": _sb(768, BF), "L1": _sb(384, U16), "bf": _sb(384, F32), "Lp1": _sb(384, F32), "nm1": _sb(256, F16),
+    "IX": _sb(176, I32), "IP": _sb(12, I32), "col": _sb(40, F32), "cl2": _sb(20, F32), "Yi": _sb(176, I32), "Yj": _sb(176, I32),
+    "MM": _sb(176, BF), "M16": _sb(176, BF), "ML": _sb(176, BF), "MB": _sb(176, BF), "MP": _sb(176, BF), "OW": _sb(176, BF),
+    "OW1": _sb(176, BF), "Blk": _sb(176, BF), "IU": _sb(128, F32), "Ib": _sb(144, BF), "Ia": _sb(144, BF), "Iw": _sb(9 * 128, BF),
+    "CE": _sb(256, BF), "Dg": _sb(256, BF), "ones": _sb(128, BF), "zero": _sb(256, BF), "bs": _sb(16, F32),
+    "NQ": _sb(256, BF), "Tri": _sb(128, BF), "U": _sb(256, BF), "U2": _sb(256, BF), "DM": _sb(128, BF), "SelW": _sb(512, BF),
+    "nn": _sb(128, BF), "st": _sb(384, BF), "cap": _sb(128, BF), "flag": _sb(128, BF), "OF": _sb(32, U16), "AD": _sb(128, U16),
+    "L2": _sb(128, U16), "Pn": _sb(128, U16), "L3": _sb(128, U16), "pos": _sb(128, U16),
+    "Lp": _sb(128, F32), "lin": _sb(128, F32), "pa": _sb(128, I32), "pb": _sb(128, I32),
+    "nd": _sb(256, F16), "s1": _sb(256, BF), "s2": _sb(256, BF), "UL": _sb(256, U16), "ys": _sb(384, F32), "cvs": _sb(384, F32),
+    "sn2": _sb(256, F16), "ln2": _sb(256, F16), "sn3": _sb(256, F16), "ln3": _sb(256, F16),
+    "sw": _sb(256, BF), "lw2": _sb(256, BF), "lw3": _sb(256, BF),
 }
 for _b in range(8):
     SCRATCH["ps%d" % _b] = ("psum", [128, 512], F32)
-NDMA, NMSG = 48, 32
+NDMA, NMSG = 60, 32
 SEMAPHORES = ["qv", "qs", "qp", "qg", "sent"] + ["d%d" % i for i in range(NDMA)] + ["a%d" % i for i in range(NMSG)]
 
-CY, PC, GC, FIX, WAKE, HOP, ISSUE = 0.00104, 0.00052, 1.56, 0.03, 0.12, 2.2, 0.35
-CH = 512
-UP, LEAN, LOOK, ROUNDS, MIX, NOISE, MARGIN, CLIMB = 3.0, 15.0, 0.4, 40, 0.5, 2.0, 3.0, 700
+CY, PC, GC, FIX, WAKE, ISSUE = 0.00088, 0.00044, 1.56, 0.035, 0.12, 0.35
+CH, SUB = 512, 2
+EARLY, ACC, TDMA = (2,), (), False
+LEAN, ROUNDS, TURN, FLIP, HEAT, SLOWER, MEAN, SEED = 0.5, 40000, 6, 0.4, 0.1, 0.15, 0.3, 1
 
 
 def build(g, T, nxt, prv, prv2, nx2):
     ops, boost = [], [0.0]
     V, S, P = g.vector, g.scalar, g.tensor
 
-    def add(alts, r, w, kind="c", lat=0.0):
-        ops.append({"alts": alts, "r": list(r), "w": list(w), "kind": kind, "lat": lat, "up": boost[0]})
+    def add(alts, r, w, kind="c", lat=0.0, slow=1.4, can=None):
+        ops.append({"alts": alts, "r": list(r), "w": list(w), "kind": kind, "lat": lat, "up": boost[0], "slow": slow,
+                    "can": can or ("s" if len(alts) > 1 else None)})
 
     def vd(c):
         return FIX + max(64, c) * CY
@@ -70,6 +77,14 @@ def build(g, T, nxt, prv, prv2, nx2):
             al["s"] = (vd(c), lambda: S.activation(out, a, AF.Copy))
         add(al, r, w)
 
+    def lin(out, a, k, b, r, w, c=128, cs=None):
+        add({"v": (vd(c), lambda: V.tensor_scalar(out, a, k, b, A.mult, A.add)),
+             "s": (vd(cs or c), lambda: S.activation(out, a, AF.Identity, bias=b, scale=k))}, r, w)
+
+    def relu(out, x, w):
+        add({"v": (vd(512), lambda: V.tensor_scalar(out, x, 0.0, None, A.max)),
+             "s": (vd(512), lambda: S.activation(out, x, AF.Relu))}, [], w)
+
     def ms(ap, val, w, c):
         add({"v": (vd(c), lambda: V.memset(ap, val))}, [], w)
 
@@ -79,369 +94,486 @@ def build(g, T, nxt, prv, prv2, nx2):
             for (o, l, x, a, b) in lst:
                 last = P.matmul(o, l, x, a, b)
             return last
-        add({"p": (FIX + cyc * PC, run)}, r, w)
+        add({"p": (0.01 + cyc * PC, run)}, r, w)
 
-    def dma(q, out, a, r, w, nbytes):
+    def dma(pairs, r, w, us, q="y"):
         eng = g.sync if q == "y" else g.scalar
-        add({q: (0.1, lambda: eng.dma_start(out, a))}, r, w, "dma", nbytes / 450e3)
+        add({q: (0.07 * len(pairs), [lambda o=o, a=a: eng.dma_start(o, a) for (o, a) in pairs])}, r, w, "dma", us)
 
     def send(dsts, src, r, w, nbytes):
-        add({"g": (ISSUE, (dsts, src))}, r, w, "msg", HOP + nbytes / 150e3)
+        add({"g": (ISSUE, (dsts, src))}, r, w, "msg", 0.1 + nbytes / 200e3)
 
     def iota(out, pat, base, cm, w, n, small=False):
+        w = w + ["gq"]
         if small:
             add({"g": (0.15 + 2 * n * CY, lambda: g.iota(out, pat, base, cm, allow_small_or_imprecise_dtypes=True))}, [], w)
         else:
             add({"g": (0.15 + 2 * n * CY, lambda: g.iota(out, pat, base, cm))}, [], w)
 
-    gd = FIX + CH * GC * CY
-    nch = 2048 // CH
-    oc = CH // 16
-
-    def gather(kind, out, okey, win, wkeys, off, o0, okeys, d=0):
-        for j in range(nch):
-            src = win.indirect(off[:, o0 + j * oc:o0 + (j + 1) * oc])
-            dst = out[:, j * CH:(j + 1) * CH]
-            k = "%s%d" % (okey, j)
-            if kind == "cmp":
-                add({"v": (gd, lambda s=src, t=dst: V.tensor_scalar(t, s, T.taus[:, d:d + 1], 0.5, A.is_ge, A.subtract)),
-                     "s": (gd, lambda s=src, t=dst: S.activation(t, s, AF.Sign, bias=T.tw[:, 12 + d:13 + d]))},
-                    wkeys + okeys + ["tau"], [k])
-            elif kind == "copy":
-                add({"v": (gd, lambda s=src, t=dst: V.tensor_copy(t, s)),
-                     "s": (gd, lambda s=src, t=dst: S.activation(t, s, AF.Copy))}, wkeys + okeys, [k])
-            elif kind == "scopy":
-                add({"s": (gd, lambda s=src, t=dst: S.activation(t, s, AF.Copy))}, wkeys + okeys, [k])
-            else:
-                add({"v": (gd, lambda s=src, t=dst: V.tensor_tensor(t, s, t, A.mult))}, wkeys + okeys + [k], [k])
-
-    def narrow(ps, bank, M, mkey, wide, wkey, m0=0):
-        for h in range(2):
-            lst = [(ps[:, 64 * h:64 * h + 64], M[:, m0 + 32 - k:m0 + 160 - k], wide[:, 1024 * h + k:1024 * (h + 1):16], k == 0, k == 15)
-                   for k in range(16)]
-            mm(lst, [mkey] + ["%s%d" % (wkey, j) for j in range(h * nch // 2, (h + 1) * nch // 2)], [bank], 16 * 64)
-
-    def reduce(ps, bank, perm, wide, wkey):
-        for h in range(2):
-            for a in range(4):
-                lst = [(ps[:, 64 * h:64 * h + 64], perm, wide[:, 1024 * h + k:1024 * (h + 1):16], k == 0, k == 15) for k in range(4 * a, 4 * a + 4)]
-                mm(lst, ["IU"] + ["%s%d" % (wkey, j) for j in range(h * nch // 2, (h + 1) * nch // 2)], [bank], 4 * 256)
-
     def act(out, a, f, bias, scale, r, w, c=128):
         add({"s": (vd(c), lambda: S.activation(out, a, f, bias=bias, scale=scale))}, r, w)
 
-    col = T.col
-    c_k, c_g, c_kh, c_k5, c_k4, c_k0, c_nk, c_cap, c_32p, c_p, c_k16, c_u1, c_u2, c_ks = [col[:, i:i + 1] for i in range(14)]
-    ps = [T["ps%d" % b] for b in range(8)]
-    W = [T.WA, T.WB, T.WA]
-    wk = [["W%s%d" % ("ABA"[t], j) for j in range(8)] for t in range(EP)]
-    fwk = ["FW%d" % j for j in range(8)]
+    nch = 2048 // CH // NH
 
+    def chunks(h):
+        return range(h * nch, (h + 1) * nch)
+
+    def keys(k, h=None):
+        return ["%s%d" % (k, j) for j in (range(nch * NH) if h is None else chunks(h))]
+
+    def pick(dst, src, r, w, n, can=None):
+        u = 0.06 + n * GC * CY
+        add({"v": (u, lambda: V.tensor_copy(dst, src)), "s": (u, lambda: S.activation(dst, src, AF.Copy))}, r, w, slow=1.85, can=can)
+
+    def gather(h, out, okey, win, wkeys, off, o0, okeys, by=None, bkey=None):
+        for j in chunks(h):
+            k = "%s%d" % (okey, j)
+            if by is None:
+                pick(out[:, j * CH:(j + 1) * CH], win.indirect(off[:, o0 + j * CH // 16:o0 + (j + 1) * CH // 16]), wkeys + okeys, [k], CH)
+                continue
+            for u in range(SUB):
+                c0, c1 = j * CH + u * CH // SUB, j * CH + (u + 1) * CH // SUB
+                add({"v": (0.05 + CH // SUB * GC * CY, lambda s=win.indirect(off[:, o0 + c0 // 16:o0 + c1 // 16]), t=out[:, c0:c1], x=by[:, c0:c1]:
+                           V.tensor_tensor(t, s, x, A.mult))}, wkeys + okeys + ["%s%d" % (bkey, j)], [k], slow=1.85)
+
+    def times(h, out, okey, x, xkey, Wg, wkey):
+        for j in chunks(h):
+            bk, sl = 4 + j % 2, slice(CH * j, CH * (j + 1))
+            mm([(ps[bk][:], I1, Wg[:, sl], True, True)], ["Ib", "%s%d" % (wkey, j)], ["ps%d" % bk], CH)
+            tt(out[:, sl], ps[bk][:], x[:, sl], A.mult, ["%s%d" % (xkey, j)], ["ps%d" % bk, "%s%d" % (okey, j)], CH)
+
+    def narrow(h, o, bank, M, mkey, wide, wkey):
+        a, b = 16 * HE * h, 16 * HE * (h + 1)
+        mm([(o, M[:, 32 - k:160 - k], wide[:, a + k:b:16], k == 0, k == 15) for k in range(16)], [mkey] + keys(wkey, h), [bank], 16 * max(64, HE))
+
+    def reduce(h, wide, wkey, last):
+        a, b = 16 * HE * h, 16 * HE * (h + 1)
+        for u in range(8):
+            mm([(ps[3][:, HE * h:HE * (h + 1)], T.IU[:], wide[:, a + k:b:16], False, last and k == 15) for k in (2 * u, 2 * u + 1)],
+               ["IU"] + keys(wkey, h), ["ps3"], 2 * 4 * max(64, HE))
+
+    def heap(x, xkey):
+        add({"g": (1.0, [lambda: g.dma_start(T.X1[:], x[:], accum_op=A.add)])}, keys(xkey), keys("X1"), "dma", 4.0)
+
+    col = T.col
+    (c_k, c_g, c_cap, c_x, c_a2, c_b2, c_a3, c_r0, c_r5, c_r4, c_e2, c_e3, c_e4, c_ul, c_p, c_32p, c_kq, c_p4, c_u, c_v,
+     c_xe, c_31) = [col[:, i:i + 1] for i in range(22)]
+    c_w = col[:, 24:28]
+    ps = [T["ps%d" % b] for b in range(8)]
+    W = [0, 3 * NW, 0]
+    wk = [["W%s%d" % ("ABA"[t], j) for j in range(8)] for t in range(EP)]
+    I384, I3200, Im1, I9, I2304, Im8, I65, I2k, Im4k = [T.Iw[:, 128 * i:128 * (i + 1)] for i in range(9)]
+    I1 = T.Ib[:, 0:128]
+    nqk = ["NQ%d" % q for q in range(4)]
+
+    def spread(t, far):
+        for x in range(2):
+            sl, a, r = slice(2048 * x, 2048 * (x + 1)), W[t] + 2048 * x, wk[t][4 * x:4 * x + 4]
+            if not far:
+                send([(prv, T.W2[:, sl])], T.WA[:, a:a + 2048], r, ["W2%d" % x], 524e3)
+            else:
+                D = T["D%d" % x]
+                dma([(D[0:128, :], T.WA[:, a:a + 2048]), (D[128:144, :], T.WA[0:16, a:a + 2048])], r, ["D%d" % x], 1.4)
+                send([(prv2, T.W3[:, sl])], D[16:144, :], ["D%d" % x], ["W3%d" % x], 524e3)
+
+    boost[0] = 40.0
+    dma([(T.bni[:], T.bn[:])], [], ["bni"], 0.5)
     boost[0] = 20.0
-    dma("y", T.bni[:], T.bn[:], [], ["bni"], 196e3)
+    dma([(T.taus[:, 0:3], T.tau[:])], [], ["taus"], 0.1, "s")
+    dma([(T.ST[96:128, 768:2048], T.ft[0:32, 0:1280])], [], ["STz"], 0.3)
+    dma([(T.WA[:, 0:NW], T.wt[:])], [], wk[0], 2.3)
     boost[0] = 0.0
-    dma("s", T.taus[:, 0:3], T.tau[:], [], ["taus"], 2e3)
-    dma("y", T.WA[:, 0:NW], T.wt[:], [], wk[0], 1048e3)
-    dma("y", T.F[:], T.ft[:], [], ["F"], 1048e3)
-    iota(T.LA[:], [[0, 512]], 0, 0, ["LA0", "LA1"], 512)
-    dma("y", T.LA[0::16, 0:256], T.lab[:], [], ["LA0"], 8e3)
-    dma("y", T.LA[0::16, 256:512], T.ask[:], [], ["LA1"], 8e3)
+    dma([(T.T2[r::8, 0:E2], T.ft[32 * x:32 * x + 32, 0:E2 // 2]) for x, r in enumerate((2, 3, 7))], [], ["T2x"], 1.29)
     iota(T.IP[:, 0:1], [[0, 1]], 0, 1, ["IP"], 1)
+    iota(T.DM[:], [[0, 8], [1, 16]], 0, 0, ["DM"], 128, True)
+    iota(T.Ia[:], [[1, 144]], -64, -1, ["Ia"], 144, True)
+    for q, pat in enumerate(([[0, 64], [8, 4]], [[0, 16], [8, 4], [0, 4]], [[0, 4], [8, 4], [0, 16]], [[8, 4], [0, 64]])):
+        iota(T.NQ[32 * q:32 * q + 32, :], pat, 1, 0, ["NQ%d" % q], 256, True)
     iota(T.IX[:], [[1, 176]], 0, 0, ["IX"], 176)
-    ms(T.TB[:], 0.0, ["TB%d" % i for i in range(6)], 1024)
-    ts(T.IP[:, 1:2], T.IP[:, 0:1], 15, None, A.bitwise_and, None, ["IP"], ["IP1"], 1)
-    ts(T.IP[:, 2:3], T.IP[:, 0:1], 14, None, A.bitwise_and, None, ["IP"], ["IP2"], 1)
-    ts(T.IP[:, 3:4], T.IP[:, 0:1], 112, None, A.bitwise_and, None, ["IP"], ["IP3"], 1)
-    cp(c_k, T.IP[:, 1:2], ["IP1"], ["c_k"], 1)
-    ts(c_g, T.IP[:, 3:4], -1.0, 96.0, A.mult, A.add, ["IP3"], ["c_g"], 1)
-    ts(c_u1, T.IP[:, 1:2], 15.0, -16.0, A.is_equal, A.mult, ["IP1"], ["c_u1"], 1)
-    ts(c_u2, T.IP[:, 1:2], 15.0, 1536.0, A.is_equal, A.mult, ["IP1"], ["c_u2"], 1)
-    ts(c_ks, T.IP[:, 1:2], 1.0, 1.0 / 16, A.add, A.mult, ["IP1"], ["c_ks"], 1)
-    ts(c_kh, T.IP[:, 2:3], 500.0, None, A.mult, None, ["IP2"], ["c_kh"], 1)
-    ts(c_k5, T.IP[:, 1:2], 5.0, None, A.add, None, ["IP1"], ["c_k5"], 1)
-    ts(c_k4, T.IP[:, 1:2], 4.0, None, A.add, None, ["IP1"], ["c_k4"], 1)
-    ts(c_k0, T.IP[:, 1:2], 0.0, None, A.is_equal, None, ["IP1"], ["c_k0"], 1)
-    ts(c_nk, T.IP[:, 1:2], -1.0, None, A.mult, None, ["IP1"], ["c_nk"], 1)
-    ts(c_cap, T.IP[:, 1:2], 12.0, 15.0, A.max, A.subtract, ["IP1"], ["c_cap"], 1)
-    ts(c_32p, T.IP[:, 0:1], 32.0, None, A.mult, None, ["IP"], ["c_32p"], 1)
-    ts(c_p, T.IP[:, 0:1], -1.0, 128.0, A.mult, A.add, ["IP"], ["c_p"], 1)
+    ms(T.zero[:], 0.0, ["zero"], 128)
+    ms(T.tau1[:], 0.0, ["tau0"], 8)
+    ts(T.ti[:, 0:3], T.taus[:, 0:3], 512.0, None, A.mult, None, ["taus"], ["ti"], 3)
+    lin(T.tw[:, 0:3], T.taus[:, 0:3], 512.0, 0.0, ["taus"], ["tw0"], 3)
+    tt(T.tw[:, 4:7], T.ti[:, 0:3], T.tw[:, 0:3], A.is_lt, ["ti", "tw0"], ["tw1"], 3)
+    tt(T.tw[:, 8:11], T.tw[:, 4:7], T.ti[:, 0:3], A.add, ["ti", "tw1"], ["tw2"], 3)
+    lin(T.tau1[:, 0:3], T.tw[:, 8:11], 1.0 / 512, -1.0 / 1024, ["tw2"], ["tau0"], 3)
+    lin(T.tau1[:, 4:7], T.tw[:, 8:11], -1.0 / 512, 1.0 / 1024, ["tw2"], ["tau0"], 3)
+    send([(prv, T.tau2[:]), (prv2, T.taur[:])], T.tau1[:], ["tau0"], ["tau1", "taur"], 4e3)
+    dma([(T.tau3[0:112, :], T.taur[16:128, :]), (T.tau3[112:128, :], T.taur[0:16, :])], ["taur"], ["tau2"], 0.1)
+    masks = (15, 7, 112, 31, 96, 12, 1, 2, 6)
+    for i, m in enumerate(masks):
+        ts(T.IP[:, i + 1:i + 2], T.IP[:, 0:1], m, None, A.bitwise_and, None, ["IP"], ["IP%d" % m], 1)
+    i15, i7, i112, i31, i96, i12, i1, i2, i6 = [T.IP[:, i + 1:i + 2] for i in range(9)]
+    cp(c_k, i15, ["IP15"], ["c_k"], 1)
+    ts(c_g, i112, -1.0, 96.0, A.mult, A.add, ["IP112"], ["c_g"], 1)
+    ts(c_p, i31, -1.0, 0.5, A.mult, A.add, ["IP31"], ["c_p"], 1)
+    ts(c_u, i96, 1.0 / 256, 0.625, A.mult, A.add, ["IP96"], ["c_u"], 1)
+    tt(c_xe, c_u, c_p, A.subtract, ["c_u", "c_p"], ["c_xe"], 1)
+    ts(c_31, i31, 31.0, None, A.is_equal, None, ["IP31"], ["c_31"], 1)
+    ms(T.Tri[:], 0.0, ["Tri"], 64)
+    for q in range(4):
+        ms(T.Tri[32 * q:32 * q + 32, 32 * q:128], 1.0 / 256, ["Tri"], 64)
+    mm([(ps[4][:, 0:256], T.Tri[:], T.NQ[:], True, True)], ["Tri"] + nqk, ["ps4"], 256)
+    ts(ps[4][:, 256:512], ps[4][:, 0:256], c_xe, c_31, A.is_equal, A.subtract, ["c_xe", "c_31"], ["ps4"], 256)
+    tt(T.U[:], ps[4][:, 256:512], T.NQ[:], A.mult, nqk, ["ps4", "U"], 256)
+    if TDMA:
+        act(T.C[:, 0:128], T.DM[:], AF.Sign, c_p, 1.0, ["DM", "c_p"], ["C0"])
+        mm([(ps[5][:, 0:256], T.C[:, 0:128], T.U[:], True, True)], ["U", "C0"], ["ps5"], 256)
+        lin(T.U2[:], ps[5][:, 0:256], 0.5, 0.0, [], ["ps5", "U2"], 256)
+        dma([(T.DT[h::4, 0:4096 - 1024 * h], T.zero[0:128 - 32 * h, :]) for h in range(4)], ["zero"], ["DT0"], 0.4)
+        dma([(T.DT[h::4, 4096 - 1024 * h:8192 - 1024 * h], T.U2[:]) for h in range(4)], ["U2"], ["DT1"], 0.6)
+        dma([(T.TT[m::4, :], T.DT[:, 256 * m:256 * m + 4352]) for m in range(4)], ["DT0", "DT1"], ["TT0"], 2.6)
+        ttk = ["TT0"]
+    else:
+        lin(T.bs[:], T.DM[:, 0:16], -1.0, c_p, ["DM", "c_p"], ["bs"], 16)
+        for s in range(16):
+            act(T.C[:, 128 * s:128 * (s + 1)], T.DM[:], AF.Sign, T.bs[:, 15 - s:16 - s], 1.0, ["DM", "bs"], ["Sh%d" % s, "C%d" % (s * 128 // CH)])
+        for s in range(8):
+            b = 4 + s % 4
+            mm([(ps[b][:, 256 * x:256 * (x + 1)], T.C[:, 128 * (2 * s + x):128 * (2 * s + x + 1)], T.U[:], True, True) for x in range(2)],
+               ["U", "Sh%d" % (2 * s), "Sh%d" % (2 * s + 1), "C%d" % (s * 256 // CH)], ["ps%d" % b], 512)
+            lin(T.TT[:, 256 + 512 * s:768 + 512 * s], ps[b][:], 0.5, 0.0, [], ["ps%d" % b, "TT%d" % s], 512)
+        lin(T.TT[:, 0:256], T.zero[:], 1.0, 0.0, ["zero"], ["TT8"], 128, 256)
+        ttk = ["TT%d" % s for s in range(9)]
+    lin(T.ones[:], T.DM[:], 0.0, 1.0, ["DM"], ["ones"], 64, 128)
     ts(T.Yj[:], T.IX[:], c_g, None, A.add, None, ["IX", "c_g"], ["Yj"], 176)
     ts(T.Yi[:], T.Yj[:], 127, None, A.bitwise_and, None, ["Yj"], ["Yi"], 176)
     ts(T.MM[:], T.Yi[:], 0.0, -4.0, A.is_equal, A.mult, ["Yi"], ["MM"], 176)
-    ts(T.MF[:], T.Yi[:], 0.0, 1.0 / 4096, A.is_equal, A.mult, ["Yi"], ["MF"], 176)
-    ms(T.cst[:, 0:128], -0.5 / 128, ["cst"], 64)
-    ms(T.cst[:, 128:256], 864.0 / 4096 / 128, ["cst"], 64)
-    ts(T.M16[:], T.Yi[:], 0.0, None, A.is_equal, None, ["Yi"], ["M16"], 176)
-    ts(T.Ms[:], T.Yi[:], 0.0, 1.0 / 16, A.is_equal, A.mult, ["Yi"], ["Ms"], 176)
-    for r in range(3):
-        ts(T.Mr[:, 176 * r:176 * (r + 1)], T.Yi[:], c_kh, 1000.0 * r, A.add, A.is_equal, ["Yi", "c_kh"], ["Mr%d" % r], 176)
-    ts(T.Ym[:], T.Yi[:], 15.0, None, A.is_le, None, ["Yi"], ["Ym"], 176)
-    ts(T.Yj[:], T.Yi[:], 5.0, None, A.add, None, ["Yi"], ["Yj"], 176)
-    tt(T.Y5[:], T.Yj[:], T.Ym[:], A.mult, ["Yj", "Ym"], ["Y5"], 352)
-    cp(T.Blk[:], T.Ym[:], ["Ym"], ["Blk"], 176)
-    ts(T.B0F[:], T.Ym[:], c_k0, 1.0 / 4096, A.mult, A.mult, ["Ym", "c_k0"], ["B0F"], 176)
-    ts(T.B0[:], T.Ym[:], c_k0, 1.0 / 16, A.mult, A.mult, ["Ym", "c_k0"], ["B0"], 176)
-    ts(T.TriL[:], T.Y5[:, 32:160], c_k5, 16384.0, A.is_ge, A.mult, ["Y5", "c_k5"], ["TriL"])
-    ts(T.TriB[:], T.Y5[:, 32:160], c_k5, 32.0, A.is_ge, A.mult, ["Y5", "c_k5"], ["TriB"])
-    ts(T.I16[:], T.Y5[:, 32:160], c_k5, None, A.is_equal, None, ["Y5", "c_k5"], ["I16"])
-    ts(T.ShI[:], T.Y5[:, 32:160], c_k4, None, A.is_equal, None, ["Y5", "c_k4"], ["ShI"])
-    tt(T.TriB[:], T.TriB[:], T.I16[:], A.add, ["TriB", "I16"], ["TriB"])
-    tt(T.ShF[:], T.ShI[:], T.I16[:], A.subtract, ["ShI", "I16"], ["ShF"])
-    cp(T.ShI[:], T.ShF[:], ["ShF"], ["ShI"])
-    ts(T.CE2[:], T.IX[:, 0:128], 1.0 / 2048, None, A.mult, None, ["IX"], ["CE2"])
-    ts(T.CE1[:], T.CE2[:], 0.0, c_ks, A.mult, A.add, ["CE2", "c_ks"], ["CE1"])
-    ts(T.Yj[:, 0:144], T.IX[:, 0:144], c_p, None, A.add, None, ["IX", "c_p"], ["Yj"], 144)
-    ts(T.Yj[:, 0:144], T.Yj[:, 0:144], 127, None, A.bitwise_and, None, ["Yj"], ["Yj"], 144)
-    ts(T.IU[:], T.Yj[:, 0:144], 0.0, None, A.is_equal, None, ["Yj"], ["IU"], 144)
-    cp(T.Ibf[:], T.IU[:, 0:128], ["IU"], ["Ibf"], 128, True)
-    ts(T.ti[:, 0:3], T.taus[:, 0:3], 512.0, None, A.mult, None, ["taus"], ["ti"], 3)
-    ts(T.tw[:, 0:3], T.taus[:, 0:3], 512.0, None, A.mult, None, ["taus"], ["tw0"], 3)
-    tt(T.tw[:, 4:7], T.ti[:, 0:3], T.tw[:, 0:3], A.is_lt, ["ti", "tw0"], ["tw1"], 3)
-    tt(T.tw[:, 8:11], T.tw[:, 4:7], T.ti[:, 0:3], A.add, ["ti", "tw1"], ["tw2"], 3)
-    ts(T.tw[:, 12:15], T.tw[:, 8:11], -0.5, -1.0 / 512, A.add, A.mult, ["tw2"], ["tau"], 3)
+    act(T.Ib[:], T.Ia[:], AF.Abs, 0.0, 1.0, ["Ia"], ["Ib"], 144)
+    act(T.Ia[:], T.Ib[:], AF.Abs, -64.0, 1.0, ["Ib"], ["Ia"], 144)
+    act(T.Ib[:], T.Ia[:], AF.Relu, 1.0, -1.0, ["Ia"], ["Ib"], 144)
+    ts(c_cap, i15, 12.0, 15.0, A.max, A.subtract, ["IP15"], ["c_cap0"], 1)
+    lin(c_cap, c_cap, -1.0, 0.0, ["c_cap0"], ["c_cap", "c_cap0"], 1)
+    lin(c_a2, c_k, 128.0, 3200.0 * 512, ["c_k"], ["c_a2"], 1)
+    lin(c_b2, c_k, -1.0, 14.0 - 9 * 512, ["c_k"], ["c_b2"], 1)
+    lin(c_a3, c_k, float(BETA), (BETA + 8.0) * 512, ["c_k"], ["c_a3"], 1)
+    lin(c_e2, c_k, -512.125, 4096.0, ["c_k"], ["c_e2"], 1)
+    lin(c_ul, c_k, 1.0, 2048.0, ["c_k"], ["c_ul"], 1)
+    ts(c_e3, i15, 5.0, -940.0, A.is_equal, A.mult, ["IP15"], ["c_e3"], 1)
+    ts(c_e4, i15, 13.0, -1.0, A.is_equal, A.mult, ["IP15"], ["c_e4"], 1)
+    for c, M, r in ((c_r0, T.ML, 0), (c_r5, T.MB, 5), (c_r4, T.MP, 4)):
+        ts(c, i7, float(r), -0.25, A.is_equal, A.mult, ["IP7"], ["c_r%d" % r], 1)
+        lin(M[:], T.MM[:], c, 0.0, ["MM", "c_r%d" % r], ["M%d" % r], 88, 176)
+    lin(T.M16[:], T.MM[:], -0.25, 0.0, ["MM"], ["M16"], 88, 176)
+    ts(T.Blk[:], T.Yi[:], 15.0, None, A.is_le, None, ["Yi"], ["Blk"], 176)
+    ts(c_kq, i12, 0.25, None, A.mult, None, ["IP12"], ["c_kq"], 1)
+    ts(c_x, i1, 3.0, 1.0, A.mult, A.add, ["IP1"], ["c_x"], 1)
+    ts(c_v, i2, 7.5, 1.0, A.mult, A.add, ["IP2"], ["c_v"], 1)
+    tt(c_p4, c_x, c_v, A.mult, ["c_x", "c_v"], ["c_p4"], 1)
+    ts(col[:, 28:32], T.DM[:, 0:4], c_kq, c_p4, A.is_equal, A.mult, ["DM", "c_kq", "c_p4"], ["c_w0"], 4)
+    ts(col[:, 32:36], T.DM[:, 0:4], c_kq, -256.0, A.is_gt, A.mult, ["DM", "c_kq"], ["c_w1"], 4)
+    tt(c_w, col[:, 28:32], col[:, 32:36], A.add, ["c_w0", "c_w1"], ["c_w"], 4)
+    lin(T.OW[:], T.zero[:, 0:176], 1.0, 0.0, ["zero"], ["OW"], 88, 176)
+    for q in range(4):
+        ts(T.OW[:, q::16], T.Yi[:, q::16], float(q), c_w[:, q:q + 1], A.is_equal, A.mult, ["Yi", "c_w"], ["OW"], 11)
+    lin(T.OW1[:], T.OW[:], c_cap, 0.0, ["OW", "c_cap"], ["OW1"], 88, 176)
+    for I, x in ((I384, 384), (I3200, -3200), (Im1, -1), (I9, 9), (I2304, -BETA - 8), (Im8, -8), (I65, 65), (I2k, 2048), (Im4k, -4096)):
+        lin(I, I1, float(x), 0.0, ["Ib"], ["I%d" % x], 64, 128)
+    cp(T.CE[:, 0:128], T.IX[:, 0:128], ["IX"], ["CE0"])
+    lin(T.CE[:, 128:256], T.CE[:, 0:128], 16.0, 0.0, ["CE0"], ["CE1"], 64, 128)
+    lin(T.T2[:, E2:E2 + 16], T.zero[:, 0:16], 1.0, c_e2, ["zero", "c_e2"], ["T2e"], 16)
+    ts(T.T3[:, E3:E3 + 8], T.zero[:, 0:8], c_e3, c_e4, A.add, A.add, ["zero", "c_e3", "c_e4"], ["T3e"], 8)
+    cp(T.IU[:], I1, ["Ib"], ["IU"], 128, True)
+    boost[0] = 6.0
     cp(T.L1[:], T.bni[:], ["bni"], ["L1"], 384)
     ts(T.bf[:], T.bni[:], -2048.0, None, A.add, None, ["bni"], ["bf"], 384)
-    cp(T.dig[:, 0:384], T.bf[:], ["bf"], ["dighi"], 384, True)
-    tt(T.dig[:, 384:768], T.bf[:], T.dig[:, 0:384], A.subtract, ["bf", "dighi"], ["diglo"], 768)
-    for p in range(2):
-        dma("y", T.TB[p::16, :], T.dig[:, 384 * p:384 * p + 128], ["dighi", "diglo"], ["TB%d" % p], 60e3)
-    send([(nxt, T.digl[:])], T.dig[:], ["dighi", "diglo"], ["digl"], 196e3)
-    send([(nx2, T.LAl[:])], T.LA[:], ["LA0", "LA1"], ["LAl"], 262e3)
+    cp(T.dig[:, 0:384], T.bf[:], ["bf"], ["hi"], 384, True)
+    mm([(ps[3][:, 0:384], Im1, T.dig[:, 0:384], True, True)], ["hi", "I-1"], ["ps3"], 384)
+    tt(T.dig[:, 384:768], ps[3][:, 0:384], T.bf[:], A.add, ["bf"], ["ps3", "lo"], 384)
+    lin(T.Lp1[:], T.bf[:], 1.0, 3232.0, ["bf"], ["Lp1"], 384)
 
-    def prevtable(t):
-        for p in range(2):
-            row = 2 * t + p
-            a = 384 * p + 128 * t
-            dma("y", T.TP[16 + row::16, :], T.digl[0:112, a:a + 128], ["digl"], ["TP%d" % row], 60e3)
-            dma("y", T.TP[row:row + 1, :], T.digl[112:128, a:a + 128], ["digl"], ["TP%d" % (row + 6)], 20e3)
+    def candidates(t):
+        a, b = 128 * t, 128 * (t + 1)
+        part = [T.dig[:, a:b], T.dig[:, 384 + a:384 + b]]
+        pk = ["hi", "lo", "Ib"]
+        dma([(T.ST[:, 2048 + 384 * x + 128 * j:2048 + 384 * x + 128 * (j + 1)], part[x]) for x in range(2) for j in range(3)]
+            + [(T.ST[0:128 - s, 512 + 640 * x + 128 * s:640 + 640 * x + 128 * s], T.dig[s:128, 384 * x + a:384 * x + b])
+               for x in range(2) for s in range(2, 7)], ["hi", "lo", "STz"], ["STp"], 1.2)
+        mm([(ps[6][:, 128 * j:128 * (j + 1)], T.Ib[:, j + 1:j + 129], part[x], x == 0, x == 1) for j in range(3) for x in range(2)],
+           pk, ["ps6"], 768)
+        mm([(ps[7][:, 128 * j:128 * (j + 1)], I65, part[x], x == 0, x == 1) for j in range(3) for x in range(2)], pk + ["I65"], ["ps7"], 768)
+        for j in range(3):
+            tt(T.na[:, 128 * j:128 * (j + 1)], ps[6][:, 128 * j:128 * (j + 1)], T.Lp1[:, a:b], A.mult, ["Lp1"], ["ps6", "na%d" % j], 128)
+        nak = ["na0", "na1", "na2"]
+        ts(T.nb[:], T.na[:], 5, None, A.arith_shift_right, None, nak, ["nb"], 384)
+        tt(T.na[:], ps[7][:, 0:384], T.nb[:], A.add, ["nb"], ["ps7"] + nak, 384)
+        ts(T.nb[:], T.na[:], 4095, None, A.bitwise_and, None, nak, ["nb"], 384)
+        cp(T.ST[:, 0:384], T.nb[:], ["nb"], ["STh"], 384)
+        mm([(ps[7][:, 0:384], Im1, T.ST[:, 0:384], True, True)], ["STh", "I-1"], ["ps7"], 384)
+        tt(T.ST[:, 384:768], ps[7][:, 0:384], T.nb[:], A.add, ["nb"], ["ps7", "STl"], 384)
+        rows = [(r + 8 * x, 768 + 640 * x + 128 * i) for i, r in enumerate((5, 1, 6)) for x in range(2)] + [(4 + 8 * x, 2048 + 384 * x) for x in range(2)]
+        dma([(T.T2[r::16, 0:E2], T.ST[:, c:c + 384]) for r, c in rows], ["STp"], ["T2b"], 3.0)
+        dma([(T.T2[8 * x::16, 0:E2], T.ST[:, 384 * x:384 * (x + 1)]) for x in range(2)], ["STh", "STl"], ["T2a"], 1.0)
 
-    for t in (1, 2):
-        for p in range(2):
-            dma("y", T.TB[2 * t + p::16, :], T.dig[:, 384 * p + 128 * t:384 * p + 128 * (t + 1)], ["dighi", "diglo"],
-                ["TB%d" % (2 * t + p)], 60e3)
-    for j in range(4):
-        iota(T.TP[:, 512 * j:512 * (j + 1)], [[0, 512]], 0, 0, ["TP%d" % i for i in range(12)], 512, True)
-    for t in range(EP):
-        prevtable(t)
-    dma("y", T.Fr[16:128, :], T.ft[0:112, :], [], ["Fr0"], 917e3)
-    dma("y", T.Fr[0:16, :], T.ft[112:128, :], [], ["Fr1"], 300e3)
-    dma("y", T.xvs[:], T.xv[:], [], ["xvs"], 98e3)
-    tbk = ["TB%d" % i for i in range(6)]
-    tpk = ["TP%d" % i for i in range(12)]
-    iota(T.SCi[:], [[16, 8], [1, 2]], 0, -1, ["SCi"], 16)
-    iota(T.SAi[:, 0:512], [[16, 8], [1, 2], [0, 32]], 0, -1, ["SAi"], 512)
-    iota(T.AL[:], [[0, 16], [1, 16], [16, 2]], -51200, 0, ["AL"], 512, True)
-    iota(T.SelW[:], [[0, 576]], 0, 0, ["SelW"], 576, True)
-    for base in (-16, 112):
-        add({"g": (0.2 + 1152 * CY, lambda x=base: g.affine_select(T.SelW[:], T.SelW[:], [[16, 9], [0, 64]], A.not_equal, 1.0, x, -1))},
-            ["SelW"], ["SelW"])
-    ts(T.SelC[:], T.SCi[:], 0.0, None, A.is_equal, None, ["SCi"], ["SelC"], 16)
-    ts(T.SelA[:], T.SAi[:, 0:512], 0.0, None, A.is_equal, None, ["SAi"], ["SelA"], 512)
-    ts(T.SelN[:], T.SelA[:], -32.0, None, A.mult, None, ["SelA"], ["SelN"], 256)
-    ms(T.zero[:], 0.0, ["zero"], 128)
-    ts(T.I4k[:], T.IU[:, 0:128], 2048.0, None, A.mult, None, ["IU"], ["I4k"])
-    ts(T.Dg[:], T.IU[:, 0:128], c_32p, None, A.mult, None, ["IU", "c_32p"], ["Dg"])
-    ms(T.ones[:], 1.0, ["ones"], 64)
-    ts(T.IB[:], T.IX[:, 0:128], 1536.0, None, A.add, None, ["IX"], ["IB"])
-    ms(T.WA[:, 2 * NW - 1:2 * NW], 0.0, ["HzA"], 1)
-    ms(T.WB[:, 2 * NW - 1:2 * NW], 0.0, ["HzB"], 1)
-    ts(T.nask[:], T.LAl[:, 256:512], -1.0, 0.5, A.mult, A.add, ["LAl"], ["nask"], 256)
-    ts(T.sig[:], T.LAl[:, 0:256], -262146.0, 2.0, A.mult, A.add, ["LAl"], ["sig"], 256)
-
-    def fwtable(t):
-        for j in range(8):
-            b = 6 + j % 2
-            sl = slice(512 * j, 512 * (j + 1))
-            mm([(ps[b][:], T.Ibf[:], W[t][:, sl], True, True)], ["Ibf", wk[t][j]], ["ps%d" % b], 512)
-            tt(T.FW[:, sl], ps[b][:], T.F[:, sl], A.mult, ["F", "ps%d" % b], [fwk[j], "ps%d" % b], 512)
+    boost[0] = 3.0
+    candidates(0)
+    boost[0] = 10.0
+    spread(0, False)
+    boost[0] = 0.0
+    dma([(T.F[:], T.ft[:])], [], ["F"], 2.3)
+    spread(0, True)
+    dma([(T.Fr[0:112, :], T.ft[16:128, :]), (T.Fr[112:128, :], T.ft[0:16, :])], [], ["Fr"], 2.5)
+    for j in range(5):
+        iota(T.T3[:, 2048 + 968 * j:3016 + 968 * j], [[0, 968]], 0, 0, ["T3x", "T3b"], 968, True)
+    dma([(T.xvs[:], T.xv[:])], [], ["xvs"], 0.3)
+    iota(T.LA[:], [[0, 512]], 0, 0, ["LA"], 512)
+    dma([(T.LA[0::16, 0:256], T.lab[:]), (T.LA[0::16, 256:512], T.ask[:])], [], ["LA"], 0.2)
+    iota(T.YY[:, 0:128], [[1, 16], [0, 8]], -8, 0, ["YY"], 128, True)
+    iota(T.YY[:, 128:256], [[0, 16], [1, 8]], -4, 0, ["YY"], 128, True)
+    iota(T.YY[:, 256:288], [[1, 16], [16, 2]], -16, 0, ["YY"], 32, True)
+    for j in range(2):
+        iota(T.SF[:, 1280 * j:1280 * (j + 1)], [[0, 1280]], 0, 0, ["SF"], 1280, True)
+    iota(T.SelW[:], [[0, 512]], 0, 0, ["SelW"], 512, True)
+    add({"g": (0.2 + 1024 * CY, lambda: g.affine_select(T.SelW[:], T.SelW[:], [[16, 8], [0, 64]], A.not_equal, 1.0, 0, -1))}, [], ["SelW", "gq"])
+    kc = [T.cl2[:, i:i + 1] for i in range(20)]
+    ts(kc[0], i1, 2.0, -1.0, A.mult, A.add, ["IP1"], ["k0"], 1)
+    lin(kc[1], kc[0], 0.5, -0.5, ["k0"], ["k1"], 1)
+    for i, v in enumerate((-1544.0, 10748.0, 51184.0, 1.0)):
+        ts(kc[2 + i], i6, 2.0 * i, v, A.is_equal, A.mult, ["IP6"], ["k%d" % (2 + i)], 1)
+    ts(kc[6], i1, kc[2], kc[3], A.add, A.add, ["IP1", "k2", "k3"], ["k6"], 1)
+    ts(kc[7], kc[6], kc[4], kc[5], A.add, A.add, ["k6", "k4", "k5"], ["k7"], 1)
+    for i in range(3):
+        ts(kc[8 + i], i6, 2.0 * i, kc[0], A.is_equal, A.mult, ["IP6", "k0"], ["k%d" % (8 + i)], 1)
+    lin(kc[10], kc[10], BIG, 0.0, ["k10"], ["k10"], 1)
+    ts(kc[11], i6, 2.0, kc[1], A.is_le, A.mult, ["IP6", "k1"], ["k11"], 1)
+    ts(kc[12], i7, 4.0, -BIG, A.is_equal, A.mult, ["IP7"], ["k12"], 1)
+    ts(kc[13], i7, 6.0, -1.0, A.is_equal, A.mult, ["IP7"], ["k13"], 1)
+    lin(kc[14], kc[13], -1.5, 0.0, ["k13"], ["k14"], 1)
+    lin(kc[15], kc[13], BIG, 0.0, ["k13"], ["k15"], 1)
+    lin(kc[16], kc[13], -0.25 * BIG, 0.0, ["k13"], ["k16"], 1)
+    ts(kc[17], i15, 2.0, 1000.0, A.is_ge, A.mult, ["IP15"], ["k17"], 1)
+    lin(kc[18], c_k, 8.0, kc[17], ["c_k", "k17"], ["k18"], 1)
+    act(T.YQ[:], T.YY[:], AF.Square, 0.5, 1.0, ["YY"], ["YQ"], 288)
+    terms = ((T.YY[:, 0:128], kc[8], kc[11], 0), (T.YY[:, 128:256], kc[9], 0.0, 0), (T.YQ[:, 0:128], kc[13], kc[14], 0),
+             (T.YQ[:, 128:256], kc[13], 0.0, 0), (T.YY[:, 256:288], kc[10], kc[12], 128), (T.YQ[:, 256:288], kc[15], kc[16], 128))
+    lst = []
+    for i, (x, m, v, o) in enumerate(terms):
+        w = 32 if o else 128
+        y = T.OH[:, 128 * i:128 * i + w]
+        lin(y, x, m, v, ["YY", "YQ"] + ["k%d" % j for j in range(8, 17)], ["OH%d" % (i // 4)], w)
+        lst.append((ps[5][:, o:o + w], I1, y, i in (0, 4), i in (3, 5)))
+    mm(lst, ["Ib", "OH0", "OH1"], ["ps5"], 640)
+    cp(T.VV[:], ps[5][:, 0:160], [], ["ps5", "VV"], 160, True)
+    dma([(T.SF[8 * c:8 * c + 8, 128 * c:128 * (c + 1)], T.VV[8 * c:8 * c + 8, 0:128]) for c in range(16)], ["VV", "SF"], ["SFb"], 0.8)
+    dma([(T.SF[8 * c:8 * c + 8, 2048 + 32 * c:2080 + 32 * c], T.VV[8 * c:8 * c + 8, 128:160]) for c in range(16)], ["VV", "SF"], ["SFa"], 0.8)
+    ts(T.Yj[:, 0:128], T.Yi[:, 32:160], 126, None, A.bitwise_and, None, ["Yi"], ["Yj"])
+    for i in range(3):
+        ts(T.RT[:, 128 * i:128 * (i + 1)], T.Yj[:, 0:128], kc[18], 2.0 * i, A.subtract, A.is_equal, ["Yj", "k18"], ["RT%d" % i])
+    ts(T.RT[:, 384:512], T.RT[:, 128:256], -8.0, None, A.mult, None, ["RT1"], ["RT3"], 64)
+    ts(T.RT[:, 512:640], T.RT[:, 256:384], -32.0, None, A.mult, None, ["RT2"], ["RT4"], 64)
+    ts(c_32p, T.IP[:, 0:1], 32.0, None, A.mult, None, ["IP"], ["c_32p"], 1)
+    lin(T.Dg[:, 0::2], I1, c_32p, 0.0, ["Ib", "c_32p"], ["Dg0"], 64, 128)
+    lin(c_32p, c_32p, 1.0, 16.0, ["c_32p"], ["c_32p"], 1)
+    lin(T.Dg[:, 1::2], I1, c_32p, 0.0, ["Ib", "c_32p"], ["Dg1"], 64, 128)
+    ms(T.WA[:, 2 * NW - 1:2 * NW], 0.0, ["Hz"], 1)
+    ts(T.nask[:], T.LA[:, 256:512], -1.0, 0.5, A.mult, A.add, ["LA"], ["nask"], 256)
+    ts(T.sig[:], T.LA[:, 0:256], -FNW - 2.0, 2.0, A.mult, A.add, ["LA"], ["sig"], 256)
+    cp(T.nm1[:], T.bf[:, 0:256], ["bf"], ["nm1"], 256)
 
     def halves(t):
-        n = "AB"[t]
         for j in range(4):
             a, b = 1024 * j, 1024 * (j + 1)
             src = wk[t][2 * j:2 * j + 2]
             e = b - 1 if j == 3 else b
-            ts(W[t][:, NW + a:NW + e], W[t][:, a:e], 0.5, 0.25, A.mult, A.max, src, ["H%s%d" % (n, j)], 512)
-            ts(W[t][:, 2 * NW + a:2 * NW + b], W[t][:, a:b], 2.0, 4.0, A.mult, A.min, src, ["D%s%d" % (n, j)], 512)
+            ts(T.WA[:, NW + a:NW + e], T.WA[:, W[t] + a:W[t] + e], 0.5, 0.25, A.mult, A.max, src, ["Hf%d" % j], 512)
+            ts(T.WA[:, 2 * NW + a:2 * NW + b], T.WA[:, W[t] + a:W[t] + b], 2.0, 4.0, A.mult, A.min, src, ["Db%d" % j], 512)
 
-    def names(Pm, pk, roll, off, out, okey, xb, xk):
-        c0 = 16 if roll else 32
-        u = ps[5][:, 0:128]
-        mm([(u, T.ShF[:], Pm, True, False)], pk + ["ShF"], ["ps5"], 512)
-        mm([(u, T.TriL[:], T.nn[:], False, True)], ["TriL", "nn"], ["ps5"], 128)
-        o = ps[3][:, 0:128]
-        lst = [(o, Pm, T.B0F[:, c0:c0 + 128], True, False)]
-        if off:
-            lst.append((o, T.ones[:], T.cst[:, 128 * off - 128:128 * off], False, False))
-        mm(lst, pk + ["B0F", "ones", "cst"], ["ps3"], 640)
-        for v in range(16):
-            act(T.RL[:, 128 * v:128 * (v + 1)], u, AF.Relu, 8192.0 + 16384.0 * v, 1.0, ["ps5"], ["RL%d" % v])
-            if v % 2 == 1:
-                mm([(ps[3][:, x:128:16], T.RL[:, 128 * x:128 * (x + 1)], T.MF[:, c0:c0 + 128:16], False, x == 15) for x in (v - 1, v)],
-                   ["RL%d" % (v - 1), "RL%d" % v, "MF"], ["ps3"], 512)
-        ts(xb, o, 2.0 ** -13, None, A.add, None, ["ps3"], ["ps3", xk])
-        tt(T.xt[:], o, xb, A.subtract, ["ps3", xk], ["ps3", "xt"], 128)
-        if xk == "xi":
-            mm([(ps[3][:, 128:256], T.I16[:], T.flag[:], True, False), (ps[3][:, 128:256], T.xt[:], T.I16[:], False, True)],
-               ["xt", "I16", "flag"], ["ps3"], 256)
-        else:
-            mm([(ps[3][:, 128:256], T.xt[:], T.I16[:], True, True)], ["xt", "I16"], ["ps3"], 128)
-        ts(out, ps[3][:, 128:256], 4096.0, 2048.0, A.mult, A.add, ["ps3"], ["ps3", okey])
+    def strong(h, d, Wg, win, wkeys, off, o0, okeys):
+        k, tau = "Wg%d" % d, (T.tau1, T.tau2, T.tau3)[d]
+        gather(h, Wg, k, win, wkeys, off, o0, okeys)
+        for j in chunks(h):
+            x, y = Wg[:, CH * j:CH * (j + 1)], T.C[:, CH * j:CH * (j + 1)]
+            add({"v": (vd(CH // 2), lambda x=x, y=y: V.tensor_scalar(y, x, tau[:, d:d + 1], 0.5, A.is_ge, A.subtract)),
+                 "s": (vd(CH), lambda x=x, y=y: S.activation(y, x, AF.Sign, bias=tau[:, 4 + d:5 + d]))},
+                ["%s%d" % (k, j), "tau%d" % d], ["C%d" % j], can="v")
+        o, bk = ps[h][:, 0:HE], "ps%d" % h
+        narrow(h, o, bk, T.MM, "MM", T.C, "C")
+        ts(T.st[:, 128 * d + HE * h:128 * d + HE * (h + 1)], o, -0.5, None, A.is_lt, None, [], [bk, "st%d%d" % (d, h)], HE)
 
-    def children(last, lk, Pm, pk, off, roll, tab, tk, t, outL, outP, okey, Lp, pkey, Ln, nkey):
-        c0 = 16 if roll else 32
-        u, o = ps[1][:, 0:128], ps[2][:, 0:128]
-        boost[0] = UP
-        lst = [(o, T.I16[:], T.CE1[:], True, False), (o, T.I16[:], T.CE2[:], False, False)]
-        if last is not None:
-            mm([(u, T.ShI[:], last, True, False)], lk + ["ShI"], ["ps1"], 128)
-            lst.append((o, T.B0[:, c0:c0 + 128], last, False, False))
-        mm(lst, lk + ["I16", "CE1", "CE2", "B0"], ["ps2"], 384)
-        mm([(u, T.TriB[:], T.nn[:], last is None, True)], ["TriB", "nn"], ["ps1"], 128)
-        if last is None:
-            ts(T.ua[:], u, c_u1, 17.0, A.add, A.add, ["ps1", "c_u1"], ["ps1", "ua"])
-        else:
-            ts(T.ua[:], u, c_u2, 16.0, A.add, A.add, ["ps1", "c_u2"], ["ps1", "ua"])
-        for v in range(16):
-            ts(T.R[:, 128 * v:128 * (v + 1)], T.ua[:], 32.0 * v, 0.0, A.add, A.max, ["ua"], ["R%d" % v], 64)
-            if v % 4 == 3:
-                mm([(o, T.Ms[:, c0 - x:c0 + 128 - x], T.R[:, 128 * x:128 * (x + 1)], False, x == 15) for x in range(v - 3, v + 1)],
-                   ["R%d" % x for x in range(v - 3, v + 1)] + ["Ms"], ["ps2"], 512)
-        ts(T.qi[:], o, -0.5 + 2.0 ** -12, None, A.add, None, ["ps2"], ["ps2", "qi"])
-        tt(T.fr[:], o, T.qi[:], A.subtract, ["ps2", "qi"], ["ps2", "fr"], 128)
-        ts(T.IDX[:], T.fr[:], 2048.0, None, A.mult, None, ["fr"], ["IDX"])
-        boost[0] = 0.0
-        mm([(ps[1][:, 128:256], T.Blk[:, c0:c0 + 128], T.nn[:], True, True)], ["Blk", "nn"], ["ps1"], 128)
-        ts(T.flag[:], ps[1][:, 128:256], c_nk, -8.0, A.is_ge, A.mult, ["ps1", "c_nk"], ["ps1", "flag"])
-        names(Pm, pk, roll, off, outP, okey + "P", T.xi[:], "xi")
-        gather("copy", T.GB, "GB", tab, tk, T.IDX, 0, ["IDX"])
-        act(Lp, ps[3][:, 128:256], AF.Relu, 3232.0, 4096.0, ["ps3"], ["ps3", pkey])
-        act(T.lin[:], ps[3][:, 128:256], AF.Relu, 65.0 * 2048 + 2048 + 4096 * 110 - 4095, 65.0 * 4096, ["ps3"], ["ps3", "lin"])
-        act(T.lin[:], T.lin[:], AF.Identity, 4095.0, 1.0, ["lin"], ["lin"])
-        narrow(ps[0], "ps0", T.Mr, "Mr%d" % t, T.GB, "GB", 176 * t)
-        tt(T.pa[:], ps[0][:, 0:128], Lp, A.mult, ["ps0", pkey], ["ps0", "pa"], 128)
-        ts(T.pb[:], T.pa[:], 5, None, A.arith_shift_right, None, ["pa"], ["pb"])
-        tt(T.pa[:], T.pb[:], T.lin[:], A.add, ["pb", "lin"], ["pa"])
-        ts(T.pb[:], T.pa[:], 4095, None, A.bitwise_and, None, ["pa"], ["pb"])
-        cp(outL, T.pb[:], ["pb"], [okey + "L"])
-        if Ln is not None:
-            cp(Ln, T.pb[:], ["pb"], [nkey])
+    def lookup(h, M, x, ks):
+        bk, e0 = "ps%d" % h, HE * h
+        o = ps[h][:, 128:128 + HE // 4]
+        mm([(o, M[:, 32 - 4 * r:160 - 4 * r], x[:, e0 + r:e0 + HE:4], r == 0, r == 3) for r in range(4)], ks, [bk], 256)
+        of = T.OF[:, e0 // 4:(e0 + HE) // 4]
+        ts(of, o, 4096.0, None, A.add, None, [], [bk, "OF%d" % h], 32)
+        u = 0.06 + 4 * HE * GC * CY
+        src = T.TT[:, :].indirect(of)
+        sl = slice(4 * e0, 4 * (e0 + HE))
+        pick(T.GA[:, sl], src, ttk + ["OF%d" % h], ["GA%d" % h], 4 * HE)
+        add({"v": (u, lambda: V.tensor_scalar(T.GB[:, sl], src, 0.125, 127.75, A.mult, A.add)),
+             "s": (u, lambda: S.activation(T.GB[:, sl], src, AF.Identity, bias=127.75, scale=0.125))},
+            ttk + ["OF%d" % h], ["GB%d" % h], slow=1.85, can="v")
 
-    def onehots(d, names, nk):
-        ts(T.ndb[:, 0:128], names, 1.0 / 32, 1536.0 - 31.0 / 64, A.mult, A.add, nk, ["nd0"])
-        ts(T.ndb[:, 128:256], names, -2048.0, None, A.add, None, nk, ["nd1"])
-        mm([(ps[6][:, 0:16], T.ndb[:, 0:128], T.SelC[:], True, True)], ["nd0", "SelC"], ["ps6"], 64)
-        cp(T.bT[:, 16 * d:16 * (d + 1)], ps[6][:, 0:16], ["ps6"], ["ps6", "bT%d" % d], 16, True)
-        mm([(ps[7][:], T.ndb[:, 128:256], T.SelA[:], True, False), (ps[7][:], T.ndb[:, 0:128], T.SelN[:], False, True)],
-           ["nd0", "nd1", "SelA", "SelN"], ["ps7"], 1024)
-        tt(T.AA[:, 512 * d:512 * (d + 1)], ps[7][:], T.AL[:], A.is_equal, ["ps7", "AL"], ["ps7", "AA%d" % d], 512)
-        for c in range(16 * d, 16 * (d + 1)):
-            ts(T.OH[:, 128 * c:128 * (c + 1)], T.IB[:], T.bT[:, c:c + 1], None, A.is_equal, None, ["IB", "bT%d" % d], ["OH%d" % c], 64)
+    def combine(h, o, bank, Ia, Ib, ks, more):
+        e0 = HE * h
+        lst = [(o, I1, x, i == 0, False) for i, x in enumerate(more)]
+        lst += [(o, Ia, T.GA[:, 4 * e0 + q:4 * (e0 + HE):4], q == 0 and not more, False) for q in range(4)]
+        lst += [(o, Ib, T.GB[:, 4 * e0 + q:4 * (e0 + HE):4], False, q == 3) for q in range(4)]
+        mm(lst, ks + ["Ib", "GA%d" % h, "GB%d" % h], [bank], len(lst) * max(64, HE))
+
+    def onehots(d, nm, nk):
+        n5, n8, ft = T.nd[:, 0:128], T.nd[:, 128:256], T.fe[:, 128 * d:128 * (d + 1)]
+        ts(n5, nm, 1.0 / 32, 1600.0 - 31.0 / 64, A.mult, A.add, nk, ["n5"], 64)
+        ts(n8, nm, 1.0 / 256, 1544.0 - 255.0 / 512, A.mult, A.add, nk, ["n8"], 64)
+        o = ps[5][:, 0:128]
+        mm([(o, T.RT[:, 128 * i:128 * (i + 1)], x, i == 0, i == 4) for i, x in enumerate((n8, n5, nm, n8, n5))],
+           nk + ["n5", "n8"] + ["RT%d" % i for i in range(5)], ["ps5"], 640)
+        act(ft, o, AF.Square, kc[7], 1.0, ["k7"], ["ps5", "fe%d" % d])
+        for x in range(4):
+            b = 4 + x % 2
+            mm([(ps[b][:], ft, T.SF[:, 512 * x:512 * (x + 1)], True, True)], ["fe%d" % d, "SFb"], ["ps%d" % b], 512)
+            relu(T.OH[:, 2048 * d + 512 * x:2048 * d + 512 * (x + 1)], ps[b][:], ["ps%d" % b, "OH%d" % (4 * d + x)])
+
+    def prime(b, d):
+        mm([(ps[b][:], T.fe[:, 128 * d:128 * (d + 1)], T.SF[:, 2048:2560], True, False)], ["fe%d" % d, "SFa"], ["ps%d" % b], 512)
 
     def weigh(d, wgt, k, b):
-        o = 0 if d == 2 else 64
-        mm([(ps[b][:], wgt, T.SelW[:, o:o + 512], True, True)], [k, "SelW"], ["ps%d" % b], 512)
-        tt(T.Aw[:, 512 * d:512 * (d + 1)], ps[b][:], T.AA[:, 512 * d:512 * (d + 1)], A.mult, ["ps%d" % b, "AA%d" % d],
-           ["ps%d" % b, "Aw%d" % d], 512)
+        mm([(ps[b][:], wgt, T.SelW[:], False, True)], [k, "SelW"], ["ps%d" % b], 512)
+        relu(T.Aw[:, 512 * d:512 * (d + 1)], ps[b][:], ["ps%d" % b, "Aw%d" % d])
 
+    hs = range(NH)
+    part = [slice(HE * h, HE * (h + 1)) for h in hs]
+    e16 = [T.CE[:, 128 + HE * h:128 + HE * (h + 1)] for h in hs]
     for t in range(EP):
         n = str(t)
         up = t < EP - 1
-        Wt = W[t][:, 0:NW]
         a, b = 128 * t, 128 * (t + 1)
-        gather("cmp", T.C, "C", Wt, wk[t], T.L1, a, ["L1"], 0)
-        narrow(ps[0], "ps0", T.MM, "MM", T.C, "C")
-        ts(T.nn[:], ps[0][:, 0:128], c_cap, 0.0, A.max, A.min, ["ps0", "c_cap"], ["ps0", "nn"])
-        o1 = 384 * t
-        ts(T.s1c[:, o1 + 256:o1 + 384], ps[0][:, 0:128], -0.5, None, A.is_lt, None, ["ps0"], ["ps0", "s1c2" + n])
-        children(None, [], T.bf[:, a:b], ["bf"], 0, False, T.TB[:, :], tbk, t, T.s1a[:, 2 * a:2 * a + 128], T.s1a[:, 2 * a + 128:2 * b],
-                 "s1a" + n, T.s1b[:, 2 * a + 128:2 * b], "s1bP" + n, T.s1b[:, 2 * a:2 * a + 128], "s1bL" + n)
-        send([(nxt, T.l1a[:, 2 * a:2 * b])], T.s1a[:, 2 * a:2 * b], ["s1a" + n + "L", "s1a" + n + "P"], ["l1a" + n], 65e3)
-        send([(nxt, T.l1b[:, 2 * a:2 * b])], T.s1b[:, 2 * a:2 * b], ["s1bL" + n, "s1bP" + n, "s1a" + n + "L"], ["l1b" + n], 131e3)
-        ts(T.s1c[:, o1:o1 + 128], T.fr[:], 16.0, 1535.504, A.mult, A.add, ["fr"], ["s1c0" + n])
-        ts(T.s1c[:, o1 + 128:o1 + 256], T.s1c[:, o1:o1 + 128], 1548.0, 1551.0, A.max, A.subtract, ["s1c0" + n], ["s1c1" + n], 64)
-        send([(nxt, T.l1c[:, o1:o1 + 384])], T.s1c[:, o1:o1 + 384], ["s1c%d%s" % (i, n) for i in range(3)], ["l1c" + n], 98e3)
-        fwtable(t)
-        gather("scopy", T.X1, "X1", T.FW[:, :], fwk, T.L1, a, ["L1"])
+        for h in hs:
+            bk = "ps%d" % h
+            strong(h, 0, T.Wg1, T.WA[:, W[t]:W[t] + NW], wk[t], T.L1, a, ["L1"])
+            lookup(h, T.OW1, T.st, ["OW1", "st0%d" % h])
+            o = ps[h][:, 192:192 + HE]
+            combine(h, o, bk, I384, I3200, ["I384", "I-3200", "CE0"], [T.CE[:, part[h]]])
+            ts(T.AD[:, part[h]], o, c_a2, float(E2), A.add, A.min, ["c_a2"], [bk, "AD%d" % h], HE)
+        for h in hs:
+            bk, o = "ps%d" % h, ps[h][:, 0:HE]
+            gather(h, T.T3, "G2", T.T2[:, :], ["T2a", "T2b", "T2x", "T2e"], T.AD, 0, ["AD%d" % h])
+            narrow(h, o, bk, T.ML, "M0", T.T3, "G2")
+            cp(T.L2[:, part[h]], o, [], [bk, "L2%d" % h], HE)
+            if up:
+                ts(T.sn2[:, a + HE * h:a + HE * (h + 1)], o, -2048.0, None, A.add, None, [], [bk, "sn2%d" % h + n], HE)
+            o = ps[2][:, part[h]]
+            combine(h, o, "ps2", Im1, I9, ["I-1", "I9"], [])
+            ts(T.cap[:, part[h]], o, c_b2, 3.0, A.add, A.min, ["c_b2"], ["ps2", "cap%d" % h], HE)
+        for h in hs:
+            narrow(h, ps[2][:, 128 + HE * h:128 + HE * (h + 1)], "ps2", T.MP, "M4", T.T3, "G2")
+        ts(T.Pn[:], ps[2][:, 128:256], 2048.0, None, A.add, None, [], ["ps2"] + ["Pn%d" % h for h in hs], 128)
+        dma([(T.T3[r::8, BETA * j:BETA * j + 2048], T.T3[s::8, 0:2048]) for j, r, s in ((1, 0, 0), (1, 5, 1), (2, 0, 0), (2, 5, 6))],
+            keys("G2"), ["T3b"], 1.0)
         if up:
-            onehots(0, T.L1[:, a:b], ["L1"])
-        gather("cmp", T.C, "C", Wt, wk[t], T.l1a, 2 * a, ["l1a" + n], 1)
-        narrow(ps[0], "ps0", T.MM, "MM", T.C, "C")
-        tt(T.nt[:], ps[0][:, 0:128], T.l1c[:, o1 + 128:o1 + 256], A.max, ["ps0", "l1c" + n], ["ps0", "nt"], 128)
-        ts(T.nn[:], T.nt[:], 0.0, None, A.min, None, ["nt"], ["nn"], 64)
-        ts(T.st[:], ps[0][:, 0:128], -0.5, None, A.is_lt, None, ["ps0"], ["ps0", "st"])
-        tt(T.s2c[:, a:b], T.st[:], T.l1c[:, o1 + 256:o1 + 384], A.add, ["st", "l1c" + n], ["s2c" + n])
-        send([(nxt, T.l2c[:, a:b])], T.s2c[:, a:b], ["s2c" + n], ["l2c" + n], 32e3)
-        children(T.l1c[:, o1:o1 + 128], ["l1c" + n], T.l1b[:, 2 * a:2 * a + 128], ["l1b" + n], 1, True, T.TP[:, :], tpk, t,
-                 T.s2a[:, 2 * a:2 * a + 128], T.s2a[:, 2 * a + 128:2 * b], "s2a" + n, T.Lp[:], "Lp", None, None)
-        send([(nxt, T.l2a[:, 2 * a:2 * b])], T.s2a[:, 2 * a:2 * b], ["s2a" + n + "L", "s2a" + n + "P"], ["l2a" + n], 65e3)
-        names(T.l1b[:, 2 * a + 128:2 * b], ["l1b" + n], True, 2, T.s2b[:, a:b], "s2b" + n, T.xj[:], "xj")
-        send([(nxt, T.l2b[:, a:b])], T.s2b[:, a:b], ["s2b" + n], ["l2b" + n], 32e3)
-        b1, b2 = (4, 4) if up else (6, 7)
-        reduce(ps[b1], "ps%d" % b1, T.IU[:, 0:128], T.X1, "X1")
-        cp(T.S1[:], ps[b1][:, 0:128], ["ps%d" % b1], ["ps%d" % b1, "S1"], 128, True)
-        gather("scopy", T.X2, "X2", T.FW[:, :], fwk, T.l1a, 2 * a, ["l1a" + n])
-        gather("mult", T.X2, "X2", T.F[:, :], ["F"], T.l1a, 2 * a + 128, ["l1a" + n])
-        reduce(ps[b2], "ps%d" % b2, T.IU[:, 0:128], T.X2, "X2")
-        cp(T.s4[:, a:b], ps[b2][:, 0:128], ["ps%d" % b2], ["ps%d" % b2, "s4" + n], 128, True)
-        send([(prv, T.l4[:, a:b])], T.s4[:, a:b], ["s4" + n], ["l4" + n], 65e3)
+            send([(nxt, T.ln2[:, a:b])], T.sn2[:, a:b], ["sn2%d" % h + n for h in hs], ["ln2" + n], 32e3)
+            onehots(0, T.nm1[:, a:b], ["nm1"])
+        for h in hs:
+            gather(h, T.X1, "X1", T.F[:, :], ["F"], T.L1, a, ["L1"], T.Wg1, "Wg0")
+        mm([(ps[3][:, 0:128], T.zero[:, 0:128], T.zero[:, 0:128], True, False)], ["zero"], ["ps3"], 128)
+        if t not in ACC:
+            for h in hs:
+                reduce(h, T.X1, "X1", False)
+        for h in hs:
+            bk = "ps%d" % h
+            strong(h, 1, T.Wg2, T.W2[:, :], ["W20", "W21"], T.L2, 0, ["L2%d" % h])
+            tt(T.nn[:, part[h]], T.st[:, 128 + HE * h:128 + HE * (h + 1)], T.cap[:, part[h]], A.mult, ["st1%d" % h, "cap%d" % h], ["nn%d" % h], 2 * HE)
+            lookup(h, T.OW, T.nn, ["OW", "nn%d" % h])
+            o = ps[h][:, 320:320 + HE]
+            mm([(o, T.Blk[:, 32:160], T.nn[:, part[h]], True, True)], ["Blk", "nn%d" % h], [bk], max(64, HE))
+            ts(T.flag[:, part[h]], o, c_k, 8192.0, A.is_le, A.mult, ["c_k"], [bk, "flag%d" % h], HE)
+            o = ps[h][:, 192:192 + HE]
+            combine(h, o, bk, I1, I2304, ["I%d" % (-BETA - 8), "CE1", "flag%d" % h], [e16[h], T.flag[:, part[h]]])
+            ts(T.AD[:, part[h]], o, c_a3, float(E3), A.add, A.min, ["c_a3"], [bk, "AD%d" % h], HE)
+            combine(h, ps[2][:, 384 + HE * h:384 + HE * (h + 1)], "ps2", I1, Im8, ["I-8", "CE1"], [e16[h]])
+        ts(T.pos[:], ps[2][:, 384:512], 4096.0, 2047.0, A.add, A.min, [], ["ps2"] + ["pos%d" % h for h in hs], 128)
+        for h in hs:
+            gather(h, T.V2, "V2", T.F[:, :], ["F"], T.Pn, 0, ["Pn%d" % h])
+            gather(h, T.V2, "V2", T.F[:, :], ["F"], T.L2, 0, ["L2%d" % h], T.V2, "V2")
         if up:
+            candidates(t + 1)
+        for h in hs:
+            bk = "ps%d" % h
+            gather(h, T.G3, "G3", T.T3[:, :], keys("G2") + ["T3b", "T3x", "T3e"], T.AD, 0, ["AD%d" % h])
+            o = ps[h][:, 256:256 + HE]
+            narrow(h, o, bk, T.ML, "M0", T.G3, "G3")
+            lin(T.Lp[:, part[h]], o, 1.0, 1184.0, [], [bk, "Lp%d" % h], HE)
+            lin(T.lin[:, part[h]], T.Lp[:, part[h]], 65.0, 2048.0 - 65.0 * 1184, ["Lp%d" % h], ["lin%d" % h], HE)
+            o = ps[h][:, 0:HE]
+            narrow(h, o, bk, T.MB, "M5", T.G3, "G3")
+            pa, pb = T.pa[:, part[h]], T.pb[:, part[h]]
+            tt(pa, o, T.Lp[:, part[h]], A.mult, ["Lp%d" % h], [bk, "pa%d" % h], HE)
+            ts(pb, pa, 5, None, A.arith_shift_right, None, ["pa%d" % h], ["pb%d" % h], HE)
+            tt(pa, pb, T.lin[:, part[h]], A.add, ["pb%d" % h, "lin%d" % h], ["pa%d" % h], 2 * HE)
+            ts(pb, pa, 4095, None, A.bitwise_and, None, ["pa%d" % h], ["pb%d" % h], HE)
+            cp(T.L3[:, part[h]], pb, ["pb%d" % h], ["L3%d" % h], HE)
+            if up:
+                ts(T.sn3[:, a + HE * h:a + HE * (h + 1)], pb, -2048.0, None, A.add, None, ["pb%d" % h], ["sn3%d" % h + n], HE)
+        if up:
+            send([(nx2, T.ln3[:, a:b])], T.sn3[:, a:b], ["sn3%d" % h + n for h in hs], ["ln3" + n], 32e3)
             halves(t)
-            onehots(1, T.l1a[:, 2 * a:2 * a + 128], ["l1a" + n])
-        gather("cmp", T.C, "C", Wt, wk[t], T.l2a, 2 * a, ["l2a" + n], 2)
-        narrow(ps[0], "ps0", T.MM, "MM", T.C, "C")
-        ts(T.st[:], ps[0][:, 0:128], -0.5, None, A.is_lt, None, ["ps0"], ["ps0", "st"])
+        for h in hs:
+            times(h, T.X2, "X2", T.V2, "V2", T.Wg2, "Wg1")
+            if t not in ACC:
+                reduce(h, T.X2, "X2", False)
+        if t in ACC:
+            heap(T.X2, "X2")
+            if not up:
+                for h in hs:
+                    reduce(h, T.X1, "X1", False)
         if up:
-            o = ps[2][:, 0:128]
-            mm([(o, T.M16[:, 32:160], T.l2c[:, a:b], True, False), (o, T.I16[:], T.nask[:, a:b], False, False)],
-               ["M16", "I16", "nask", "l2c" + n], ["ps2"], 256)
-            mm([(o, T.M16[:, 48:176], T.st[:], False, True)], ["M16", "st"], ["ps2"], 128)
-            tt(T.tv[:], o, T.sig[:, a:b], A.mult, ["ps2", "sig"], ["ps2", "tv"], 128)
-            ts(T.s3[:, a:b], T.tv[:], 0.0, None, A.max, None, ["tv"], ["s3" + n])
-            send([(prv, T.l3a[:, a:b]), (prv2, T.l3b[:, a:b])], T.s3[:, a:b], ["s3" + n], ["l3" + n], 65e3)
-            onehots(2, T.l2a[:, 2 * a:2 * a + 128], ["l2a" + n])
-        o = ps[0][:, 128:256]
-        mm([(o, T.M16[:, 32:160], T.l2c[:, a:b], True, False), (o, T.M16[:, 48:176], T.st[:], False, True)],
-           ["M16", "st", "l2c" + n], ["ps0"], 256)
-        cp(T.s5[:, 2 * a + 128:2 * b], o, ["ps0"], ["ps0", "s5v" + n], 128, True)
-        gather("scopy" if up else "copy", T.X3, "X3", T.FW[:, :], fwk, T.l2a, 2 * a, ["l2a" + n])
+            onehots(1, T.ln2[:, a:b], ["ln2" + n])
+            prime(6, 1)
+        o = ps[2][:, 0:128]
+        lst = [(o, T.M16[:, 32:160], T.st[:, 0:128], True, False), (o, T.M16[:, 32:160], T.st[:, 128:256], False, False)]
         if up:
-            weigh(2, T.s3[:, a:b], "s3" + n, 6)
-            weigh(1, T.l3a[:, a:b], "l3" + n, 7)
-            weigh(0, T.l3b[:, a:b], "l3" + n, 6)
-            mm([(ps[1][:, 0:256], T.ones[:], T.zero[:], True, False)], ["ones", "zero"], ["ps1"], 256)
-            for d in (2, 1, 0):
-                cs = range(16 * d, 16 * (d + 1))
-                mm([(ps[1][:, 32 * (c % 16 // 2):32 * (c % 16 // 2 + 1)], T.OH[:, 128 * c:128 * (c + 1)], T.Aw[:, 32 * c:32 * (c + 1)], False, c == 15)
-                    for c in cs], ["Aw%d" % d] + ["OH%d" % c for c in cs], ["ps1"], 16 * 64)
-            act(T.s1[:], ps[1][:, 0:256], AF.Sign, -0.5, 1.0, ["ps1"], ["s1"], 256)
-            act(T.s2[:], ps[1][:, 0:256], AF.Sign, -100000.5, 1.0, ["ps1"], ["s2"], 256)
-            lst = []
-            for x in range(2):
-                o = ps[2][:, 128 * x:128 * (x + 1)]
-                lst += [(o, T.ones[:], T.Dg[:], True, False), (o, T.s1[:, x::2], T.I4k[:], False, False), (o, T.s2[:, x::2], T.I4k[:], False, True)]
-            mm(lst, ["ones", "Dg", "s1", "s2", "I4k"], ["ps2"], 768)
-            ts(T.UL[:, 0::2], ps[2][:, 0:128], c_k, 4096.0, A.add, A.add, ["ps2", "c_k"], ["UL0"])
-            ts(T.UL[:, 1::2], ps[2][:, 128:256], c_k, 4112.0, A.add, A.add, ["ps2", "c_k"], ["UL1"])
-            nm = "AB"[t]
-            src = wk[t] + ["%s%s%d" % (x, nm, j) for x in "HD" for j in range(4)] + ["Hz" + nm, "UL0", "UL1"]
+            lst.append((o, I1, T.nask[:, a:b], False, False))
+        mm(lst, ["M16", "Ib", "nask"] + ["st%d%d" % (d, h) for d in range(2) for h in hs], ["ps2"], 384)
+        for h in hs:
+            strong(h, 2, T.Wg3, T.W3[:, :], ["W30", "W31"], T.L3, 0, ["L3%d" % h])
+            mm([(ps[2][:, part[h]], T.M16[:, 32:160], T.st[:, 256 + HE * h:256 + HE * (h + 1)], False, h == NH - 1)],
+               ["M16", "st2%d" % h], ["ps2"], max(64, HE))
+        if up:
+            tt(T.sw[:, a:b], o, T.sig[:, a:b], A.mult, ["sig"], ["ps2", "sw" + n], 128)
+            send([(nxt, T.lw2[:, a:b]), (nx2, T.lw3[:, a:b])], T.sw[:, a:b], ["sw" + n], ["lw" + n], 65e3)
+            tt(T.cvs[:, a:b], o, T.nask[:, a:b], A.subtract, ["nask"], ["ps2", "cvs" + n], 128)
+            onehots(2, T.ln3[:, a:b], ["ln3" + n])
+            prime(7, 2)
+            prime(1, 0)
+            weigh(0, T.sw[:, a:b], "sw" + n, 1)
+            weigh(1, T.lw2[:, a:b], "lw" + n, 6)
+            weigh(2, T.lw3[:, a:b], "lw" + n, 7)
+            mm([(ps[0][:, 0:256], T.zero[:, 0:128], T.zero[:], True, False)], ["zero"], ["ps0"], 256)
+            mm([(ps[1][:, 0:256], T.ones[:], T.Dg[:], True, False)], ["ones", "Dg0", "Dg1"], ["ps1"], 256)
+            for d in range(3):
+                mm([(ps[0][:, 32 * ((c // 2 + d // 2) % 8):32 * ((c // 2 + d // 2) % 8 + 1)], T.OH[:, 128 * (16 * d + c):128 * (16 * d + c + 1)],
+                     T.Aw[:, 32 * (16 * d + c):32 * (16 * d + c + 1)], False, d == 2 and c == 15) for c in range(16)],
+                   ["Aw%d" % d] + ["OH%d" % (4 * d + x) for x in range(4)], ["ps0"], 16 * 64)
+            act(T.s1[:], ps[0][:, 0:256], AF.Sign, -0.5, 1.0, [], ["ps0", "s1"], 256)
+            ts(T.s2[:], ps[0][:, 0:256], 73300.0, 2.0, A.is_gt, A.mult, [], ["ps0", "s2"], 256)
+            for s, k, I in ((T.s1, "s1", Im4k if t else I2k), (T.s2, "s2", I2k)):
+                mm([(ps[1][:, x:256:2], s[:, x::2], I, False, k == "s2" and x == 1) for x in range(2)], [k, "I2048", "I-4096"], ["ps1"], 256)
+            ts(T.UL[:], ps[1][:, 0:256], c_ul, 2048.0 * t, A.add, A.add, ["c_ul"], ["ps1", "UL"], 256)
+            src = wk[t] + ["%s%d" % (x, j) for x in ("Hf", "Db") for j in range(4)] + ["Hz", "UL"]
             for j in range(8):
-                s_ = W[t][:, :].indirect(T.UL[:, 32 * j:32 * (j + 1)])
-                d_ = W[t + 1][:, 512 * j:512 * (j + 1)]
-                u = FIX + 512 * GC * CY
-                add({"v": (u, lambda s=s_, x=d_: V.tensor_copy(x, s)), "s": (u, lambda s=s_, x=d_: S.activation(x, s, AF.Copy))},
-                    src, [wk[t + 1][j]])
-        gather("mult", T.X3, "X3", T.Fr[:, :], ["Fr0", "Fr1"], T.l2a, 2 * a + 128, ["l2a" + n])
-        gather("mult", T.X3, "X3", T.Fr[:, :], ["Fr0", "Fr1"], T.l2b, a, ["l2b" + n])
-        reduce(ps[4], "ps4", T.IU[:, 16:144], T.X3, "X3")
-        cp(T.s5[:, 2 * a:2 * a + 128], ps[4][:, 0:128], ["ps4"], ["ps4", "s5s" + n], 128, True)
-        send([(prv2, T.l5[:, 2 * a:2 * b])], T.s5[:, 2 * a:2 * b], ["s5s" + n, "s5v" + n], ["l5" + n], 131e3)
-        o, bk = ps[b1][:, 128:256], "ps%d" % b1
-        mm([(o, T.IU[:, 0:128], T.S1[:], True, False), (o, T.IU[:, 0:128], T.l4[:, a:b], False, False)], ["IU", "S1", "l4" + n], [bk], 1024)
-        mm([(o, T.IU[:, 0:128], T.l5[:, 2 * a:2 * a + 128], False, True)], ["IU", "l5" + n], [bk], 512)
-        tt(T.ys[:, a:b], o, T.xvs[:, a:b], A.mult, [bk, "xvs"], [bk, "ys" + n], 128)
-        dma("y", T.cv[:, a:b], T.l5[0::16, 2 * a + 128:2 * b], ["l5" + n], ["cv" + n], 8e3)
-        dma("y", T.y[:, a:b], T.ys[:, a:b], ["ys" + n], ["y" + n], 65e3)
+                pick(T.WA[:, W[t + 1] + 512 * j:W[t + 1] + 512 * (j + 1)], T.WA[:, NW * t:NW * (t + 3)].indirect(T.UL[:, 32 * j:32 * (j + 1)]),
+                     src, [wk[t + 1][j]], 512, "vs")
+            spread(t + 1, False)
+            spread(t + 1, True)
+        else:
+            cp(T.cvs[:, a:b], o, [], ["ps2", "cvs" + n], 128, True)
+        for h in hs:
+            if t in EARLY:
+                gather(h, T.X3, "X3", T.V2[:, :], keys("V2"), T.pos, 0, ["pos%d" % h])
+                gather(h, T.X3, "X3", T.Fr[:, :], ["Fr"], T.L3, 0, ["L3%d" % h], T.X3, "X3")
+                times(h, T.X3, "X3", T.X3, "X3", T.Wg3, "Wg2")
+            else:
+                gather(h, T.X3, "X3", T.V2[:, :], keys("V2"), T.pos, 0, ["pos%d" % h], T.Wg3, "Wg2")
+                gather(h, T.X3, "X3", T.Fr[:, :], ["Fr"], T.L3, 0, ["L3%d" % h], T.X3, "X3")
+            if not (up and t in ACC):
+                reduce(h, T.X3, "X3", h == NH - 1)
+        if up and t in ACC:
+            heap(T.X3, "X3")
+            for h in hs:
+                reduce(h, T.X1, "X1", h == NH - 1)
+        tt(T.ys[:, a:b], ps[3][:, 0:128], T.xvs[:, a:b], A.mult, ["xvs"], ["ps3", "ys" + n], 128)
+        dma([(T.cv[:, a:b], T.cvs[0::16, a:b])], ["cvs" + n], ["cv" + n], 0.1)
+        dma([(T.y[:, a:b], T.ys[:, a:b])], ["ys" + n], ["y" + n], 0.2)
     return ops
 
 
@@ -464,128 +596,156 @@ def depends(ops):
     return deps
 
 
+def gap(busy, t, dur):
+    lo, hi = 0, len(busy)
+    while lo < hi:
+        mid = (lo + hi) // 2
+        if busy[mid][1] <= t:
+            lo = mid + 1
+        else:
+            hi = mid
+    while lo < len(busy) and busy[lo][0] < t + dur - 1e-9:
+        t = max(t, busy[lo][1])
+        lo += 1
+    return t, lo
+
+
+def place(ops, seq, before, can, back):
+    n = len(ops)
+    busy = {q: [] for q in "vspgyw"}
+    where, start, fin = [None] * n, [0.0] * n, [0.0] * n
+    for c in seq:
+        o = ops[c]
+        t0, pe = 0.0, can[c] == "p"
+        for d in before[c]:
+            t = fin[d] if pe and where[d] == "p" else fin[d] + WAKE
+            if t > t0:
+                t0 = t
+        if o["kind"] != "c":
+            q = can[c]
+            dur = o["alts"][q][0]
+            if back:
+                w, j = gap(busy["w"], t0 + 0.8, o["lat"])
+                busy["w"].insert(j, (w, w + o["lat"]))
+                t, j = gap(busy[q], w + o["lat"] + 1.0, dur)
+                end = t + dur
+            else:
+                t, j = gap(busy[q], t0, dur)
+                w, i = gap(busy["w"], t + dur + 1.0, o["lat"])
+                busy["w"].insert(i, (w, w + o["lat"]))
+                t, j = gap(busy[q], max(t, w - 1.0 - dur), dur)
+                end = max(w + o["lat"], t + dur + 1.0) + 0.8
+        else:
+            end = 1e9
+            for x in can[c]:
+                u = o["alts"][x][0]
+                s, i = gap(busy[x], t0, u)
+                if s + u + (LEAN if x == "v" else 0.0) < end:
+                    q, t, j, dur, end = x, s, i, u, s + u + (LEAN if x == "v" else 0.0)
+            end = t + dur
+        busy[q].insert(j, (t, t + dur))
+        where[c], start[c], fin[c] = q, t, end
+    return where, start, fin
+
+
+def replay(cost, deps, seq, where):
+    n = len(seq)
+    free, last, end, by, held = dict.fromkeys("vspgyw", 0.0), dict.fromkeys("vspgyw"), [0.0] * n, [None] * n, [False] * n
+    seen = [0.0] * n
+    total, tail = 0.0, None
+    for c in seq:
+        q = where[c]
+        t0, p = 0.0, None
+        if q == "p":
+            for d in deps[c]:
+                t = end[d] if where[d] == "p" else seen[d]
+                if t > t0:
+                    t0, p = t, d
+        else:
+            for d in deps[c]:
+                if seen[d] > t0:
+                    t0, p = seen[d], d
+        if free[q] > t0:
+            t0, p, held[c] = free[q], last[q], True
+        dur, wire = cost[c][q]
+        e = free[q] = t0 + dur
+        last[q] = c
+        if wire:
+            if free["w"] > e + 1.0:
+                p, held[c] = last["w"], True
+                e = free["w"] - 1.0
+            free["w"] = e + 1.0 + wire
+            last["w"] = c
+            e += 1.8 + wire
+        end[c], seen[c], by[c] = e, e + WAKE, p
+        if e > total:
+            total, tail = e, c
+    pairs = []
+    while by[tail] is not None:
+        if held[tail]:
+            pairs.append((by[tail], tail))
+        tail = by[tail]
+    return total + MEAN * sum(end) / n, pairs, end
+
+
 def schedule(ops, deps):
     n = len(ops)
     succ = [[] for _ in range(n)]
     for i in range(n):
         for d in deps[i]:
             succ[d].append(i)
-    full = [min(a[0] for a in o["alts"].values()) + o["lat"] + (1.6 if o["kind"] == "dma" else 0.0) + WAKE for o in ops]
-    prio = [0.0] * n
+    key = [0.0] * n
     for i in range(n - 1, -1, -1):
-        prio[i] = full[i] + max([prio[s] for s in succ[i]] + [0.0])
-    prio = [prio[i] + ops[i]["up"] for i in range(n)]
+        o = ops[i]
+        key[i] = (min(a[0] for a in o["alts"].values()) + o["lat"] + WAKE + (1.8 if o["kind"] != "c" else 0.0)
+                  + max([key[s] for s in succ[i]] + [0.0]) + o["up"])
+    can = [ops[i]["can"] or "".join(ops[i]["alts"]) for i in range(n)]
+    cost = [{q: (o["alts"][q][0] * (1 + SLOWER * (o["slow"] - 1) if o["kind"] == "c" else 1.0), o["lat"]) for q in o["alts"]} for o in ops]
     best = None
-    rng = np.random.default_rng(1)
-    lean = [LEAN] * n
-    keep = prio
-    head = {}
-    run = []
-    for i, o in enumerate(ops):
-        k = o["w"][0].rstrip("0123456789")
-        if k not in head or i - head[k][1] > 2 or k == "ps":
-            head[k] = [i, i]
-        head[k][1] = i
-        run.append(head[k][0])
+    for rnd in range(TURN):
+        where, start, fin = place(ops, sorted(range(n), key=lambda i: (-key[i], i)), deps, can, False)
+        seq = sorted(range(n), key=lambda i: (start[i], fin[i]))
+        m, pairs, end = replay(cost, deps, seq, where)
+        if best is None or m < best[0]:
+            best = (m, seq, where, pairs)
+        key = place(ops, sorted(range(n), key=lambda i: -fin[i]), succ, where, True)[2]
+    dice = np.random.default_rng(SEED).random((ROUNDS, 4))
+    now = best
     for rnd in range(ROUNDS):
-        plan = forward(ops, deps, succ, prio, lean)
-        if best is None or max(plan[3]) < max(best[3]):
-            best, keep = plan, prio
-        if rnd % 4 == 3:
-            plan = best
-        late = backward(ops, deps, succ, plan)
-        noise = rng.random(n)[run] * (NOISE if rnd % 4 == 3 else 0.0)
-        prio = [MIX * prio[i] + (1 - MIX) * (late[i] + ops[i]["up"]) + float(noise[i]) for i in range(n)]
-    for rnd in range(CLIMB):
-        step = (rng.normal(0.0, NOISE, n) * (rng.random(n) < 0.06))[run]
-        flip = rng.random(n) < 0.03
-        prio = [keep[i] + float(step[i]) for i in range(n)]
-        trial = [LEAN - lean[i] if flip[i] else lean[i] for i in range(n)]
-        plan = forward(ops, deps, succ, prio, trial)
-        if max(plan[3]) <= max(best[3]):
-            best, keep, lean = plan, prio, trial
-    return best
-
-
-def backward(ops, deps, succ, plan):
-    order, where, start, fin = plan
-    n = len(ops)
-    left = [len(s) for s in succ]
-    ready = [0.0] * n
-    late = [0.0] * n
-    pool = {q: [] for q in order}
-    free = {q: 0.0 for q in order}
-    lag = [o["lat"] + (1.6 if o["kind"] == "dma" else 0.0) for o in ops]
-    for i in range(n):
-        if left[i] == 0:
-            ready[i] = lag[i]
-            pool[where[i]].append(i)
-    for _ in range(n):
-        pick = None
-        for q in pool:
-            if pool[q]:
-                t0 = max(free[q], min(ready[i] for i in pool[q]))
-                if pick is None or t0 < pick[0]:
-                    pick = (t0, q)
-        t0, q = pick
-        c = max([i for i in pool[q] if ready[i] <= t0 + 1e-9], key=lambda i: fin[i])
-        pool[q].remove(c)
-        free[q] = late[c] = t0 + ops[c]["alts"][q][0]
-        for d in deps[c]:
-            ready[d] = max(ready[d], late[c] + lag[d] + (0.0 if q == "p" and where[d] == "p" else WAKE))
-            left[d] -= 1
-            if left[d] == 0:
-                pool[where[d]].append(d)
-    return late
-
-
-def forward(ops, deps, succ, prio, lean):
-    n = len(ops)
-    left = [len(d) for d in deps]
-    ready = [0.0] * n
-    pool = [i for i in range(n) if left[i] == 0]
-    free = {q: 0.0 for q in "vspgy"}
-    order = {q: [] for q in "vspgy"}
-    where, fin, start = [None] * n, [0.0] * n, [0.0] * n
-    wire = 0.0
-    done = 0
-    while done < n:
-        best = None
-        for q in "vspgy":
-            cand = [i for i in pool if q in ops[i]["alts"]]
-            if not cand:
+        level, seq, where, pairs = now
+        u = dice[rnd]
+        b, c = pairs[int(u[0] * len(pairs))]
+        x = b if u[1] < 0.5 else c
+        if len(ops[x]["alts"]) > 1 and u[2] < FLIP:
+            where = list(where)
+            where[x] = "s" if where[x] == "v" else "v"
+        else:
+            i, j = seq.index(b), seq.index(c)
+            span = seq[i:j + 1] if x == b else seq[i:j + 1][::-1]
+            moved = {x}
+            for y in span[1:]:
+                if any(z in moved for z in (deps if x == b else succ)[y]):
+                    moved.add(y)
+            if b in moved and c in moved:
                 continue
-            t0 = max(free[q], min(ready[i] for i in cand))
-            now = [i for i in cand if ready[i] <= t0 + 1e-9]
-            c = max(now, key=lambda i: (prio[i] - (lean[i] if len(ops[i]["alts"]) > 1 and q == "v" else 0.0), -i))
-            dur = ops[c]["alts"][q][0]
-            soon = [i for i in cand if t0 < ready[i] < t0 + LOOK * dur and prio[i] > prio[c] + MARGIN]
-            if soon:
-                c = min(soon, key=lambda i: ready[i])
-                t0 = ready[c]
-            if best is None or t0 < best[0]:
-                best = (t0, q, c)
-        t0, q, c = best
-        o = ops[c]
-        dur = o["alts"][q][0]
-        free[q] = t0 + dur
-        end = t0 + dur
-        if o["kind"] == "dma":
-            wire = max(wire, end + 1.0) + o["lat"]
-            end = wire + 0.6
-        elif o["kind"] == "msg":
-            end += o["lat"]
-        where[c], start[c], fin[c] = q, t0, end
-        order[q].append(c)
-        pool.remove(c)
-        done += 1
-        for s in succ[c]:
-            same = q == "p" and "p" in ops[s]["alts"]
-            ready[s] = max(ready[s], end + (0.0 if same else WAKE))
-            left[s] -= 1
-            if left[s] == 0:
-                pool.append(s)
-    return order, where, start, fin
+            stay, go = [y for y in seq[i:j + 1] if y not in moved], [y for y in seq[i:j + 1] if y in moved]
+            seq = seq[:i] + (stay + go if x == b else go + stay) + seq[j + 1:]
+        m, pairs, end = replay(cost, deps, seq, where)
+        if m <= level - HEAT * (1.0 - rnd / ROUNDS) * math.log(u[3] + 1e-12):
+            now = (m, seq, where, pairs)
+            if m < best[0]:
+                best = now
+    m, seq, where, pairs = best
+    fin = replay(cost, deps, seq, where)[2]
+    start = [fin[i] - cost[i][where[i]][0] - (1.8 + ops[i]["lat"] if ops[i]["lat"] else 0.0) for i in range(n)]
+    vec = [i for i in seq if where[i] == "v"]
+    at = {i: j for j, i in enumerate(seq)}
+    for i in seq:
+        if ops[i]["lat"] > 1.3 and ops[i]["up"] < 20.0 and start[i] > max([fin[d] for d in deps[i]] + [0.0]) + 1.0:
+            d = [j for j in vec if fin[j] < start[i] - 0.3 and at[j] < at[i]]
+            if d:
+                deps[i] = sorted(set(deps[i] + [d[-1]]))
+    return {q: [i for i in seq if where[i] == q] for q in "vspgy"}, where, start, fin
 
 
 PLAN = {}
@@ -635,7 +795,7 @@ def rank_program(g, core, T, topo):
                 mark[i] = (T.sem["q" + q], c)
     for i in range(n):
         if ops[i]["kind"] == "dma":
-            mark[i] = (T.sem["d%d" % nd], 16)
+            mark[i] = (T.sem["d%d" % nd], 16 * len(ops[i]["alts"][where[i]][1]))
             nd += 1
         elif ops[i]["kind"] == "msg":
             mark[i] = (T.sem["a%d" % nm], len(topo.engines(core, peer[0])))
@@ -664,11 +824,12 @@ def rank_program(g, core, T, topo):
                                                      remote_sem=mark[i][0], src=src, dst=ap))
                         sent += len(en)
                     g.remote_dma_fused(trs, local_sem=T.sem.sent)
+            elif o["kind"] == "dma":
+                for f in o["alts"][q][1]:
+                    f().then_inc(mark[i][0], 16)
             else:
                 ins = o["alts"][q][1]()
-                if o["kind"] == "dma":
-                    ins.then_inc(mark[i][0], 16)
-                elif need[i]:
+                if need[i]:
                     ins.then_inc(mark[i][0], 1)
     for i in range(n):
         if ops[i]["kind"] != "c" and i not in waited:

@@ -18,7 +18,7 @@ def _sb(n, d):
 
 SCRATCH = {
     "WA": _sb(4 * NW, BF), "W2": _sb(NW, BF), "W3": _sb(NW, BF), "F": _sb(NW, BF), "Fr": _sb(NW, BF),
-    "D0": ("dram", [144, 2048], BF), "D1": ("dram", [144, 2048], BF), "DT": ("dram", [32, 8192], BF),
+    "D0": ("dram", [144, 2048], BF), "D1": ("dram", [144, 2048], BF),
     "TT": _sb(4352, BF), "T2": _sb(E2 + 16, BF), "T3": _sb(E3 + 8, BF), "G3": _sb(2048, BF),
     "Wg1": _sb(2048, BF), "Wg2": _sb(2048, BF), "Wg3": _sb(2048, BF), "C": _sb(2048, BF),
     "X1": _sb(2048, F32), "X2": _sb(2048, F32), "X3": _sb(2048, F32), "V2": _sb(2048, F32),
@@ -32,10 +32,10 @@ SCRATCH = {
     "MM": _sb(176, BF), "M16": _sb(176, BF), "ML": _sb(176, BF), "MB": _sb(176, BF), "MP": _sb(176, BF), "OW": _sb(176, BF),
     "OW1": _sb(176, BF), "Blk": _sb(176, BF), "IU": _sb(128, F32), "Ib": _sb(144, BF), "Ia": _sb(144, BF), "Iw": _sb(9 * 128, BF),
     "CE": _sb(256, BF), "Dg": _sb(256, BF), "ones": _sb(128, BF), "zero": _sb(256, BF), "bs": _sb(16, F32),
-    "NQ": _sb(256, BF), "Tri": _sb(128, BF), "U": _sb(256, BF), "U2": _sb(256, BF), "DM": _sb(128, BF), "SelW": _sb(512, BF),
+    "NQ": _sb(256, BF), "Tri": _sb(128, BF), "U": _sb(256, BF), "DM": _sb(128, BF), "SelW": _sb(512, BF), "keep": _sb(512, BF),
     "nn": _sb(128, BF), "st": _sb(384, BF), "cap": _sb(128, BF), "flag": _sb(128, BF), "OF": _sb(32, U16), "AD": _sb(128, U16),
     "L2": _sb(128, U16), "Pn": _sb(128, U16), "L3": _sb(128, U16), "pos": _sb(128, U16),
-    "Lp": _sb(128, F32), "lin": _sb(128, F32), "pa": _sb(128, I32), "pb": _sb(128, I32),
+    "Lp": _sb(128, F32), "pa": _sb(128, I32), "pb": _sb(128, I32),
     "nd": _sb(256, F16), "s1": _sb(256, BF), "s2": _sb(256, BF), "UL": _sb(256, U16), "ys": _sb(384, F32), "cvs": _sb(384, F32),
     "sn2": _sb(256, F16), "ln2": _sb(256, F16), "sn3": _sb(256, F16), "ln3": _sb(256, F16),
     "sw": _sb(256, BF), "lw2": _sb(256, BF), "lw3": _sb(256, BF),
@@ -45,10 +45,11 @@ for _b in range(8):
 NDMA, NMSG = 60, 32
 SEMAPHORES = ["qv", "qs", "qp", "qg", "sent"] + ["d%d" % i for i in range(NDMA)] + ["a%d" % i for i in range(NMSG)]
 
-CY, PC, GC, FIX, WAKE, ISSUE = 0.00088, 0.00044, 1.56, 0.035, 0.12, 0.35
-CH, SUB = 512, 2
-EARLY, ACC, TDMA = (2,), (), False
-LEAN, ROUNDS, TURN, FLIP, HEAT, SLOWER, MEAN, SEED = 0.5, 40000, 6, 0.4, 0.1, 0.15, 0.3, 1
+CH = 512
+EARLY = (2,)
+CY, PC, GC, FIX, WAKE, ISSUE, LATE = 0.00085, 0.00044, 1.56, 0.05, 0.22, 0.35, 5.0
+PACES = ((0.05, 0.9, 1.1, 0.6), (1.0, 0.9, 1.0, 0.45))
+LEAN, ROUNDS, TURN, FLIP, HEAT, MEAN, SEED = 0.5, 72000, 6, 0.4, 0.22, 0.2, 2
 
 
 def build(g, T, nxt, prv, prv2, nx2):
@@ -77,9 +78,9 @@ def build(g, T, nxt, prv, prv2, nx2):
             al["s"] = (vd(c), lambda: S.activation(out, a, AF.Copy))
         add(al, r, w)
 
-    def lin(out, a, k, b, r, w, c=128, cs=None):
+    def lin(out, a, k, b, r, w, c=128, cs=None, can=None):
         add({"v": (vd(c), lambda: V.tensor_scalar(out, a, k, b, A.mult, A.add)),
-             "s": (vd(cs or c), lambda: S.activation(out, a, AF.Identity, bias=b, scale=k))}, r, w)
+             "s": (vd(cs or c) + 0.015, lambda: S.activation(out, a, AF.Identity, bias=b, scale=k))}, r, w, can=can)
 
     def relu(out, x, w):
         add({"v": (vd(512), lambda: V.tensor_scalar(out, x, 0.0, None, A.max)),
@@ -103,15 +104,15 @@ def build(g, T, nxt, prv, prv2, nx2):
     def send(dsts, src, r, w, nbytes):
         add({"g": (ISSUE, (dsts, src))}, r, w, "msg", 0.1 + nbytes / 200e3)
 
-    def iota(out, pat, base, cm, w, n, small=False):
+    def iota(out, pat, base, cm, w, n, small=False, r=()):
         w = w + ["gq"]
         if small:
-            add({"g": (0.15 + 2 * n * CY, lambda: g.iota(out, pat, base, cm, allow_small_or_imprecise_dtypes=True))}, [], w)
+            add({"g": (0.15 + 2 * n * CY, lambda: g.iota(out, pat, base, cm, allow_small_or_imprecise_dtypes=True))}, r, w)
         else:
-            add({"g": (0.15 + 2 * n * CY, lambda: g.iota(out, pat, base, cm))}, [], w)
+            add({"g": (0.15 + 2 * n * CY, lambda: g.iota(out, pat, base, cm))}, r, w)
 
     def act(out, a, f, bias, scale, r, w, c=128):
-        add({"s": (vd(c), lambda: S.activation(out, a, f, bias=bias, scale=scale))}, r, w)
+        add({"s": (vd(c) + 0.015, lambda: S.activation(out, a, f, bias=bias, scale=scale))}, r, w)
 
     nch = 2048 // CH // NH
 
@@ -127,14 +128,13 @@ def build(g, T, nxt, prv, prv2, nx2):
 
     def gather(h, out, okey, win, wkeys, off, o0, okeys, by=None, bkey=None):
         for j in chunks(h):
-            k = "%s%d" % (okey, j)
+            k, sl = "%s%d" % (okey, j), slice(j * CH, (j + 1) * CH)
+            src = win.indirect(off[:, o0 + j * CH // 16:o0 + (j + 1) * CH // 16])
             if by is None:
-                pick(out[:, j * CH:(j + 1) * CH], win.indirect(off[:, o0 + j * CH // 16:o0 + (j + 1) * CH // 16]), wkeys + okeys, [k], CH)
-                continue
-            for u in range(SUB):
-                c0, c1 = j * CH + u * CH // SUB, j * CH + (u + 1) * CH // SUB
-                add({"v": (0.05 + CH // SUB * GC * CY, lambda s=win.indirect(off[:, o0 + c0 // 16:o0 + c1 // 16]), t=out[:, c0:c1], x=by[:, c0:c1]:
-                           V.tensor_tensor(t, s, x, A.mult))}, wkeys + okeys + ["%s%d" % (bkey, j)], [k], slow=1.85)
+                pick(out[:, sl], src, wkeys + okeys, [k], CH)
+            else:
+                add({"v": (0.05 + CH * GC * CY, lambda s=src, t=out[:, sl], x=by[:, sl]: V.tensor_tensor(t, s, x, A.mult))},
+                    wkeys + okeys + ["%s%d" % (bkey, j)], [k], slow=1.85)
 
     def times(h, out, okey, x, xkey, Wg, wkey):
         for j in chunks(h):
@@ -152,17 +152,14 @@ def build(g, T, nxt, prv, prv2, nx2):
             mm([(ps[3][:, HE * h:HE * (h + 1)], T.IU[:], wide[:, a + k:b:16], False, last and k == 15) for k in (2 * u, 2 * u + 1)],
                ["IU"] + keys(wkey, h), ["ps3"], 2 * 4 * max(64, HE))
 
-    def heap(x, xkey):
-        add({"g": (1.0, [lambda: g.dma_start(T.X1[:], x[:], accum_op=A.add)])}, keys(xkey), keys("X1"), "dma", 4.0)
-
     col = T.col
     (c_k, c_g, c_cap, c_x, c_a2, c_b2, c_a3, c_r0, c_r5, c_r4, c_e2, c_e3, c_e4, c_ul, c_p, c_32p, c_kq, c_p4, c_u, c_v,
-     c_xe, c_31) = [col[:, i:i + 1] for i in range(22)]
+     c_xe, c_31, c_hi, c_um) = [col[:, i:i + 1] for i in range(24)]
     c_w = col[:, 24:28]
     ps = [T["ps%d" % b] for b in range(8)]
     W = [0, 3 * NW, 0]
     wk = [["W%s%d" % ("ABA"[t], j) for j in range(8)] for t in range(EP)]
-    I384, I3200, Im1, I9, I2304, Im8, I65, I2k, Im4k = [T.Iw[:, 128 * i:128 * (i + 1)] for i in range(9)]
+    I384, I3200, Im1, I9, I2304, Im8, I2080, I2k, Im4k = [T.Iw[:, 128 * i:128 * (i + 1)] for i in range(9)]
     I1 = T.Ib[:, 0:128]
     nqk = ["NQ%d" % q for q in range(4)]
 
@@ -170,10 +167,10 @@ def build(g, T, nxt, prv, prv2, nx2):
         for x in range(2):
             sl, a, r = slice(2048 * x, 2048 * (x + 1)), W[t] + 2048 * x, wk[t][4 * x:4 * x + 4]
             if not far:
-                send([(prv, T.W2[:, sl])], T.WA[:, a:a + 2048], r, ["W2%d" % x], 524e3)
+                send([(prv, T.W2[:, sl])], T.WA[:, a:a + 2048], r + ([] if t else ["STl"]), ["W2%d" % x], 524e3)
             else:
                 D = T["D%d" % x]
-                dma([(D[0:128, :], T.WA[:, a:a + 2048]), (D[128:144, :], T.WA[0:16, a:a + 2048])], r, ["D%d" % x], 1.4)
+                dma([(D[0:128, :], T.WA[:, a:a + 2048]), (D[128:144, :], T.WA[0:16, a:a + 2048])], r + ([] if t else ["W20"]), ["D%d" % x], 1.4)
                 send([(prv2, T.W3[:, sl])], D[16:144, :], ["D%d" % x], ["W3%d" % x], 524e3)
 
     boost[0] = 40.0
@@ -183,7 +180,7 @@ def build(g, T, nxt, prv, prv2, nx2):
     dma([(T.ST[96:128, 768:2048], T.ft[0:32, 0:1280])], [], ["STz"], 0.3)
     dma([(T.WA[:, 0:NW], T.wt[:])], [], wk[0], 2.3)
     boost[0] = 0.0
-    dma([(T.T2[r::8, 0:E2], T.ft[32 * x:32 * x + 32, 0:E2 // 2]) for x, r in enumerate((2, 3, 7))], [], ["T2x"], 1.29)
+    dma([(T.T2[r::8, 0:E2], T.ft[32 * x:32 * x + 32, 0:E2 // 2]) for x, r in enumerate((2, 3, 7))], ["bni"], ["T2x"], 1.29)
     iota(T.IP[:, 0:1], [[0, 1]], 0, 1, ["IP"], 1)
     iota(T.DM[:], [[0, 8], [1, 16]], 0, 0, ["DM"], 128, True)
     iota(T.Ia[:], [[1, 144]], -64, -1, ["Ia"], 144, True)
@@ -199,6 +196,7 @@ def build(g, T, nxt, prv, prv2, nx2):
     lin(T.tau1[:, 0:3], T.tw[:, 8:11], 1.0 / 512, -1.0 / 1024, ["tw2"], ["tau0"], 3)
     lin(T.tau1[:, 4:7], T.tw[:, 8:11], -1.0 / 512, 1.0 / 1024, ["tw2"], ["tau0"], 3)
     send([(prv, T.tau2[:]), (prv2, T.taur[:])], T.tau1[:], ["tau0"], ["tau1", "taur"], 4e3)
+    tausent = len(ops) - 1
     dma([(T.tau3[0:112, :], T.taur[16:128, :]), (T.tau3[112:128, :], T.taur[0:16, :])], ["taur"], ["tau2"], 0.1)
     masks = (15, 7, 112, 31, 96, 12, 1, 2, 6)
     for i, m in enumerate(masks):
@@ -214,27 +212,18 @@ def build(g, T, nxt, prv, prv2, nx2):
     for q in range(4):
         ms(T.Tri[32 * q:32 * q + 32, 32 * q:128], 1.0 / 256, ["Tri"], 64)
     mm([(ps[4][:, 0:256], T.Tri[:], T.NQ[:], True, True)], ["Tri"] + nqk, ["ps4"], 256)
-    ts(ps[4][:, 256:512], ps[4][:, 0:256], c_xe, c_31, A.is_equal, A.subtract, ["c_xe", "c_31"], ["ps4"], 256)
-    tt(T.U[:], ps[4][:, 256:512], T.NQ[:], A.mult, nqk, ["ps4", "U"], 256)
-    if TDMA:
-        act(T.C[:, 0:128], T.DM[:], AF.Sign, c_p, 1.0, ["DM", "c_p"], ["C0"])
-        mm([(ps[5][:, 0:256], T.C[:, 0:128], T.U[:], True, True)], ["U", "C0"], ["ps5"], 256)
-        lin(T.U2[:], ps[5][:, 0:256], 0.5, 0.0, [], ["ps5", "U2"], 256)
-        dma([(T.DT[h::4, 0:4096 - 1024 * h], T.zero[0:128 - 32 * h, :]) for h in range(4)], ["zero"], ["DT0"], 0.4)
-        dma([(T.DT[h::4, 4096 - 1024 * h:8192 - 1024 * h], T.U2[:]) for h in range(4)], ["U2"], ["DT1"], 0.6)
-        dma([(T.TT[m::4, :], T.DT[:, 256 * m:256 * m + 4352]) for m in range(4)], ["DT0", "DT1"], ["TT0"], 2.6)
-        ttk = ["TT0"]
-    else:
-        lin(T.bs[:], T.DM[:, 0:16], -1.0, c_p, ["DM", "c_p"], ["bs"], 16)
-        for s in range(16):
-            act(T.C[:, 128 * s:128 * (s + 1)], T.DM[:], AF.Sign, T.bs[:, 15 - s:16 - s], 1.0, ["DM", "bs"], ["Sh%d" % s, "C%d" % (s * 128 // CH)])
-        for s in range(8):
-            b = 4 + s % 4
-            mm([(ps[b][:, 256 * x:256 * (x + 1)], T.C[:, 128 * (2 * s + x):128 * (2 * s + x + 1)], T.U[:], True, True) for x in range(2)],
-               ["U", "Sh%d" % (2 * s), "Sh%d" % (2 * s + 1), "C%d" % (s * 256 // CH)], ["ps%d" % b], 512)
-            lin(T.TT[:, 256 + 512 * s:768 + 512 * s], ps[b][:], 0.5, 0.0, [], ["ps%d" % b, "TT%d" % s], 512)
-        lin(T.TT[:, 0:256], T.zero[:], 1.0, 0.0, ["zero"], ["TT8"], 128, 256)
-        ttk = ["TT%d" % s for s in range(9)]
+    ts(ps[4][:, 256:512], ps[4][:, 0:256], c_xe, c_31, A.is_equal, A.subtract, ["c_xe", "c_31"], ["ps4", "PW"], 256)
+    tt(T.U[:], ps[4][:, 256:512], T.NQ[:], A.mult, nqk + ["PW"], ["ps4", "U"], 256)
+    lin(T.bs[:], T.DM[:, 0:16], -1.0, c_p, ["DM", "c_p"], ["bs"], 16)
+    for s in range(16):
+        act(T.C[:, 128 * s:128 * (s + 1)], T.DM[:], AF.Sign, T.bs[:, 15 - s:16 - s], 1.0, ["DM", "bs"], ["Sh%d" % s, "C%d" % (s * 128 // CH)])
+    for s in range(8):
+        b = (4, 5, 2, 0)[s % 4]
+        mm([(ps[b][:, 256 * x:256 * (x + 1)], T.C[:, 128 * (2 * s + x):128 * (2 * s + x + 1)], T.U[:], True, True) for x in range(2)],
+           ["U", "Sh%d" % (2 * s), "Sh%d" % (2 * s + 1), "C%d" % (s * 256 // CH)], ["ps%d" % b], 512)
+        lin(T.TT[:, 256 + 512 * s:768 + 512 * s], ps[b][:], 0.5, 0.0, [], ["ps%d" % b, "TT%d" % s], 512)
+    lin(T.TT[:, 0:256], T.zero[:], 1.0, 0.0, ["zero"], ["TT8"], 128, 256)
+    ttk = ["TT%d" % s for s in range(9)]
     lin(T.ones[:], T.DM[:], 0.0, 1.0, ["DM"], ["ones"], 64, 128)
     ts(T.Yj[:], T.IX[:], c_g, None, A.add, None, ["IX", "c_g"], ["Yj"], 176)
     ts(T.Yi[:], T.Yj[:], 127, None, A.bitwise_and, None, ["Yj"], ["Yi"], 176)
@@ -248,7 +237,9 @@ def build(g, T, nxt, prv, prv2, nx2):
     lin(c_b2, c_k, -1.0, 14.0 - 9 * 512, ["c_k"], ["c_b2"], 1)
     lin(c_a3, c_k, float(BETA), (BETA + 8.0) * 512, ["c_k"], ["c_a3"], 1)
     lin(c_e2, c_k, -512.125, 4096.0, ["c_k"], ["c_e2"], 1)
-    lin(c_ul, c_k, 1.0, 2048.0, ["c_k"], ["c_ul"], 1)
+    ts(c_hi, i112, 64.0, 2048.0, A.is_ge, A.mult, ["IP112"], ["c_hi"], 1)
+    lin(c_ul, c_hi, 2.0, c_k, ["c_k", "c_hi"], ["c_ul"], 1)
+    ts(c_um, c_k, 8192.0, c_hi, A.add, A.subtract, ["c_k", "c_hi"], ["c_um"], 1)
     ts(c_e3, i15, 5.0, -940.0, A.is_equal, A.mult, ["IP15"], ["c_e3"], 1)
     ts(c_e4, i15, 13.0, -1.0, A.is_equal, A.mult, ["IP15"], ["c_e4"], 1)
     for c, M, r in ((c_r0, T.ML, 0), (c_r5, T.MB, 5), (c_r4, T.MP, 4)):
@@ -267,7 +258,7 @@ def build(g, T, nxt, prv, prv2, nx2):
     for q in range(4):
         ts(T.OW[:, q::16], T.Yi[:, q::16], float(q), c_w[:, q:q + 1], A.is_equal, A.mult, ["Yi", "c_w"], ["OW"], 11)
     lin(T.OW1[:], T.OW[:], c_cap, 0.0, ["OW", "c_cap"], ["OW1"], 88, 176)
-    for I, x in ((I384, 384), (I3200, -3200), (Im1, -1), (I9, 9), (I2304, -BETA - 8), (Im8, -8), (I65, 65), (I2k, 2048), (Im4k, -4096)):
+    for I, x in ((I384, 384), (I3200, -3200), (Im1, -1), (I9, 9), (I2304, -BETA - 8), (Im8, -8), (I2080, 2080), (I2k, 2048), (Im4k, -4096)):
         lin(I, I1, float(x), 0.0, ["Ib"], ["I%d" % x], 64, 128)
     cp(T.CE[:, 0:128], T.IX[:, 0:128], ["IX"], ["CE0"])
     lin(T.CE[:, 128:256], T.CE[:, 0:128], 16.0, 0.0, ["CE0"], ["CE1"], 64, 128)
@@ -287,35 +278,38 @@ def build(g, T, nxt, prv, prv2, nx2):
         part = [T.dig[:, a:b], T.dig[:, 384 + a:384 + b]]
         pk = ["hi", "lo", "Ib"]
         dma([(T.ST[:, 2048 + 384 * x + 128 * j:2048 + 384 * x + 128 * (j + 1)], part[x]) for x in range(2) for j in range(3)]
-            + [(T.ST[0:128 - s, 512 + 640 * x + 128 * s:640 + 640 * x + 128 * s], T.dig[s:128, 384 * x + a:384 * x + b])
-               for x in range(2) for s in range(2, 7)], ["hi", "lo", "STz"], ["STp"], 1.2)
+            + [(T.ST[p:q, 512 + 640 * x + 128 * s:640 + 640 * x + 128 * s], T.dig[p + s:q + s, 384 * x + a:384 * x + b])
+               for x in range(2) for s in range(2, 7) for p, q in ((0, 112), (112, 128 - s))], ["hi", "lo", "STz"], ["STp"], 1.2)
         mm([(ps[6][:, 128 * j:128 * (j + 1)], T.Ib[:, j + 1:j + 129], part[x], x == 0, x == 1) for j in range(3) for x in range(2)],
            pk, ["ps6"], 768)
-        mm([(ps[7][:, 128 * j:128 * (j + 1)], I65, part[x], x == 0, x == 1) for j in range(3) for x in range(2)], pk + ["I65"], ["ps7"], 768)
+        mm([(ps[7][:, 128 * j:128 * (j + 1)], I2080, part[x], x == 0, x == 1) for j in range(3) for x in range(2)], pk + ["I2080"], ["ps7"], 768)
         for j in range(3):
             tt(T.na[:, 128 * j:128 * (j + 1)], ps[6][:, 128 * j:128 * (j + 1)], T.Lp1[:, a:b], A.mult, ["Lp1"], ["ps6", "na%d" % j], 128)
         nak = ["na0", "na1", "na2"]
-        ts(T.nb[:], T.na[:], 5, None, A.arith_shift_right, None, nak, ["nb"], 384)
-        tt(T.na[:], ps[7][:, 0:384], T.nb[:], A.add, ["nb"], ["ps7"] + nak, 384)
-        ts(T.nb[:], T.na[:], 4095, None, A.bitwise_and, None, nak, ["nb"], 384)
+        tt(T.na[:], ps[7][:, 0:384], T.na[:], A.add, [], ["ps7"] + nak, 384)
+        ts(T.nb[:], T.na[:], 5, 4095, A.arith_shift_right, A.bitwise_and, nak, ["nb"], 384)
         cp(T.ST[:, 0:384], T.nb[:], ["nb"], ["STh"], 384)
         mm([(ps[7][:, 0:384], Im1, T.ST[:, 0:384], True, True)], ["STh", "I-1"], ["ps7"], 384)
         tt(T.ST[:, 384:768], ps[7][:, 0:384], T.nb[:], A.add, ["nb"], ["ps7", "STl"], 384)
         rows = [(r + 8 * x, 768 + 640 * x + 128 * i) for i, r in enumerate((5, 1, 6)) for x in range(2)] + [(4 + 8 * x, 2048 + 384 * x) for x in range(2)]
-        dma([(T.T2[r::16, 0:E2], T.ST[:, c:c + 384]) for r, c in rows], ["STp"], ["T2b"], 3.0)
+        dma([(T.T2[r::16, 0:E2], T.ST[:, c:c + 384]) for r, c in rows], ["STp"] + (["W31"] if t else []), ["T2b"], 3.0)
         dma([(T.T2[8 * x::16, 0:E2], T.ST[:, 384 * x:384 * (x + 1)]) for x in range(2)], ["STh", "STl"], ["T2a"], 1.0)
+        ops[-1]["after"] = len(ops) - 2
 
-    boost[0] = 3.0
+    boost[0] = 8.0
     candidates(0)
-    boost[0] = 10.0
+    boost[0] = 12.0
     spread(0, False)
+    ops[-2]["after"], ops[-1]["after"], sent0 = tausent, len(ops) - 2, len(ops) - 1
     boost[0] = 0.0
-    dma([(T.F[:], T.ft[:])], [], ["F"], 2.3)
+    dma([(T.F[:], T.ft[:])], ["T2a"], ["F"], 2.3)
     spread(0, True)
-    dma([(T.Fr[0:112, :], T.ft[16:128, :]), (T.Fr[112:128, :], T.ft[0:16, :])], [], ["Fr"], 2.5)
+    dma([(T.Fr[0:112, :], T.ft[16:128, :]), (T.Fr[112:128, :], T.ft[0:16, :])], ["W30"], ["Fr"], 2.5)
     for j in range(5):
         iota(T.T3[:, 2048 + 968 * j:3016 + 968 * j], [[0, 968]], 0, 0, ["T3x", "T3b"], 968, True)
-    dma([(T.xvs[:], T.xv[:])], [], ["xvs"], 0.3)
+        if j == 2:
+            ops[-1]["after"] = sent0
+    dma([(T.xvs[:], T.xv[:])], ["W21"], ["xvs"], 0.3)
     iota(T.LA[:], [[0, 512]], 0, 0, ["LA"], 512)
     dma([(T.LA[0::16, 0:256], T.lab[:]), (T.LA[0::16, 256:512], T.ask[:])], [], ["LA"], 0.2)
     iota(T.YY[:, 0:128], [[1, 16], [0, 8]], -8, 0, ["YY"], 128, True)
@@ -323,9 +317,12 @@ def build(g, T, nxt, prv, prv2, nx2):
     iota(T.YY[:, 256:288], [[1, 16], [16, 2]], -16, 0, ["YY"], 32, True)
     for j in range(2):
         iota(T.SF[:, 1280 * j:1280 * (j + 1)], [[0, 1280]], 0, 0, ["SF"], 1280, True)
+    iota(T.keep[:], [[0, 32], [1, 16]], 0, 0, ["keep"], 512, True)
+    ts(T.keep[:], T.keep[:], 1.0, None, A.min, None, [], ["keep"], 256)
     iota(T.SelW[:], [[0, 512]], 0, 0, ["SelW"], 512, True)
     add({"g": (0.2 + 1024 * CY, lambda: g.affine_select(T.SelW[:], T.SelW[:], [[16, 8], [0, 64]], A.not_equal, 1.0, 0, -1))}, [], ["SelW", "gq"])
     kc = [T.cl2[:, i:i + 1] for i in range(20)]
+    boost[0] = -LATE
     ts(kc[0], i1, 2.0, -1.0, A.mult, A.add, ["IP1"], ["k0"], 1)
     lin(kc[1], kc[0], 0.5, -0.5, ["k0"], ["k1"], 1)
     for i, v in enumerate((-1544.0, 10748.0, 51184.0, 1.0)):
@@ -369,6 +366,7 @@ def build(g, T, nxt, prv, prv2, nx2):
     ts(T.nask[:], T.LA[:, 256:512], -1.0, 0.5, A.mult, A.add, ["LA"], ["nask"], 256)
     ts(T.sig[:], T.LA[:, 0:256], -FNW - 2.0, 2.0, A.mult, A.add, ["LA"], ["sig"], 256)
     cp(T.nm1[:], T.bf[:, 0:256], ["bf"], ["nm1"], 256)
+    boost[0] = 0.0
 
     def halves(t):
         for j in range(4):
@@ -396,13 +394,9 @@ def build(g, T, nxt, prv, prv2, nx2):
         mm([(o, M[:, 32 - 4 * r:160 - 4 * r], x[:, e0 + r:e0 + HE:4], r == 0, r == 3) for r in range(4)], ks, [bk], 256)
         of = T.OF[:, e0 // 4:(e0 + HE) // 4]
         ts(of, o, 4096.0, None, A.add, None, [], [bk, "OF%d" % h], 32)
-        u = 0.06 + 4 * HE * GC * CY
-        src = T.TT[:, :].indirect(of)
         sl = slice(4 * e0, 4 * (e0 + HE))
-        pick(T.GA[:, sl], src, ttk + ["OF%d" % h], ["GA%d" % h], 4 * HE)
-        add({"v": (u, lambda: V.tensor_scalar(T.GB[:, sl], src, 0.125, 127.75, A.mult, A.add)),
-             "s": (u, lambda: S.activation(T.GB[:, sl], src, AF.Identity, bias=127.75, scale=0.125))},
-            ttk + ["OF%d" % h], ["GB%d" % h], slow=1.85, can="v")
+        pick(T.GA[:, sl], T.TT[:, :].indirect(of), ttk + ["OF%d" % h], ["GA%d" % h], 4 * HE)
+        lin(T.GB[:, sl], T.GA[:, sl], 0.125, 127.75, ["GA%d" % h], ["GB%d" % h], 2 * HE, 4 * HE, "v")
 
     def combine(h, o, bank, Ia, Ib, ks, more):
         e0 = HE * h
@@ -450,25 +444,22 @@ def build(g, T, nxt, prv, prv2, nx2):
             gather(h, T.T3, "G2", T.T2[:, :], ["T2a", "T2b", "T2x", "T2e"], T.AD, 0, ["AD%d" % h])
             narrow(h, o, bk, T.ML, "M0", T.T3, "G2")
             cp(T.L2[:, part[h]], o, [], [bk, "L2%d" % h], HE)
-            if up:
-                ts(T.sn2[:, a + HE * h:a + HE * (h + 1)], o, -2048.0, None, A.add, None, [], [bk, "sn2%d" % h + n], HE)
-            o = ps[2][:, part[h]]
-            combine(h, o, "ps2", Im1, I9, ["I-1", "I9"], [])
-            ts(T.cap[:, part[h]], o, c_b2, 3.0, A.add, A.min, ["c_b2"], ["ps2", "cap%d" % h], HE)
+            combine(h, ps[2][:, part[h]], "ps2", Im1, I9, ["I-1", "I9"], [])
+        ts(T.cap[:], ps[2][:, 0:128], c_b2, 3.0, A.add, A.min, ["c_b2"], ["ps2"] + ["cap%d" % h for h in hs], 128)
         for h in hs:
             narrow(h, ps[2][:, 128 + HE * h:128 + HE * (h + 1)], "ps2", T.MP, "M4", T.T3, "G2")
         ts(T.Pn[:], ps[2][:, 128:256], 2048.0, None, A.add, None, [], ["ps2"] + ["Pn%d" % h for h in hs], 128)
         dma([(T.T3[r::8, BETA * j:BETA * j + 2048], T.T3[s::8, 0:2048]) for j, r, s in ((1, 0, 0), (1, 5, 1), (2, 0, 0), (2, 5, 6))],
             keys("G2"), ["T3b"], 1.0)
         if up:
-            send([(nxt, T.ln2[:, a:b])], T.sn2[:, a:b], ["sn2%d" % h + n for h in hs], ["ln2" + n], 32e3)
+            ts(T.sn2[:, a:b], T.L2[:], -2048.0, None, A.add, None, ["L2%d" % h for h in hs], ["sn2" + n], 64)
+            send([(nxt, T.ln2[:, a:b])], T.sn2[:, a:b], ["sn2" + n], ["ln2" + n], 32e3)
             onehots(0, T.nm1[:, a:b], ["nm1"])
         for h in hs:
             gather(h, T.X1, "X1", T.F[:, :], ["F"], T.L1, a, ["L1"], T.Wg1, "Wg0")
         mm([(ps[3][:, 0:128], T.zero[:, 0:128], T.zero[:, 0:128], True, False)], ["zero"], ["ps3"], 128)
-        if t not in ACC:
-            for h in hs:
-                reduce(h, T.X1, "X1", False)
+        for h in hs:
+            reduce(h, T.X1, "X1", False)
         for h in hs:
             bk = "ps%d" % h
             strong(h, 1, T.Wg2, T.W2[:, :], ["W20", "W21"], T.L2, 0, ["L2%d" % h])
@@ -488,34 +479,26 @@ def build(g, T, nxt, prv, prv2, nx2):
         if up:
             candidates(t + 1)
         for h in hs:
-            bk = "ps%d" % h
+            bk, lk, lo = "ps%d" % h, "ps%d" % (6 + h), ps[6 + h][:, 448:448 + HE]
             gather(h, T.G3, "G3", T.T3[:, :], keys("G2") + ["T3b", "T3x", "T3e"], T.AD, 0, ["AD%d" % h])
             o = ps[h][:, 256:256 + HE]
             narrow(h, o, bk, T.ML, "M0", T.G3, "G3")
             lin(T.Lp[:, part[h]], o, 1.0, 1184.0, [], [bk, "Lp%d" % h], HE)
-            lin(T.lin[:, part[h]], T.Lp[:, part[h]], 65.0, 2048.0 - 65.0 * 1184, ["Lp%d" % h], ["lin%d" % h], HE)
+            lin(lo, T.Lp[:, part[h]], 2080.0, -2080.0 * 3232, ["Lp%d" % h], [lk, "PW%d" % h], HE)
             o = ps[h][:, 0:HE]
             narrow(h, o, bk, T.MB, "M5", T.G3, "G3")
             pa, pb = T.pa[:, part[h]], T.pb[:, part[h]]
             tt(pa, o, T.Lp[:, part[h]], A.mult, ["Lp%d" % h], [bk, "pa%d" % h], HE)
-            ts(pb, pa, 5, None, A.arith_shift_right, None, ["pa%d" % h], ["pb%d" % h], HE)
-            tt(pa, pb, T.lin[:, part[h]], A.add, ["pb%d" % h, "lin%d" % h], ["pa%d" % h], 2 * HE)
-            ts(pb, pa, 4095, None, A.bitwise_and, None, ["pa%d" % h], ["pb%d" % h], HE)
+            tt(pa, lo, pa, A.add, ["PW%d" % h], [lk, "pa%d" % h], HE)
+            ts(pb, pa, 5, 4095, A.arith_shift_right, A.bitwise_and, ["pa%d" % h], ["pb%d" % h], HE)
             cp(T.L3[:, part[h]], pb, ["pb%d" % h], ["L3%d" % h], HE)
-            if up:
-                ts(T.sn3[:, a + HE * h:a + HE * (h + 1)], pb, -2048.0, None, A.add, None, ["pb%d" % h], ["sn3%d" % h + n], HE)
         if up:
-            send([(nx2, T.ln3[:, a:b])], T.sn3[:, a:b], ["sn3%d" % h + n for h in hs], ["ln3" + n], 32e3)
+            ts(T.sn3[:, a:b], T.pb[:], -2048.0, None, A.add, None, ["pb%d" % h for h in hs], ["sn3" + n], 128)
+            send([(nx2, T.ln3[:, a:b])], T.sn3[:, a:b], ["sn3" + n], ["ln3" + n], 32e3)
             halves(t)
         for h in hs:
             times(h, T.X2, "X2", T.V2, "V2", T.Wg2, "Wg1")
-            if t not in ACC:
-                reduce(h, T.X2, "X2", False)
-        if t in ACC:
-            heap(T.X2, "X2")
-            if not up:
-                for h in hs:
-                    reduce(h, T.X1, "X1", False)
+            reduce(h, T.X2, "X2", False)
         if up:
             onehots(1, T.ln2[:, a:b], ["ln2" + n])
             prime(6, 1)
@@ -538,17 +521,21 @@ def build(g, T, nxt, prv, prv2, nx2):
             weigh(0, T.sw[:, a:b], "sw" + n, 1)
             weigh(1, T.lw2[:, a:b], "lw" + n, 6)
             weigh(2, T.lw3[:, a:b], "lw" + n, 7)
-            mm([(ps[0][:, 0:256], T.zero[:, 0:128], T.zero[:], True, False)], ["zero"], ["ps0"], 256)
+            for x in (0, 2):
+                mm([(ps[x][:, 0:128], T.zero[:, 0:128], T.zero[:, 0:128], True, False)], ["zero"], ["ps%d" % x], 128)
             mm([(ps[1][:, 0:256], T.ones[:], T.Dg[:], True, False)], ["ones", "Dg0", "Dg1"], ["ps1"], 256)
             for d in range(3):
-                mm([(ps[0][:, 32 * ((c // 2 + d // 2) % 8):32 * ((c // 2 + d // 2) % 8 + 1)], T.OH[:, 128 * (16 * d + c):128 * (16 * d + c + 1)],
-                     T.Aw[:, 32 * (16 * d + c):32 * (16 * d + c + 1)], False, d == 2 and c == 15) for c in range(16)],
-                   ["Aw%d" % d] + ["OH%d" % (4 * d + x) for x in range(4)], ["ps0"], 16 * 64)
-            act(T.s1[:], ps[0][:, 0:256], AF.Sign, -0.5, 1.0, [], ["ps0", "s1"], 256)
-            ts(T.s2[:], ps[0][:, 0:256], 73300.0, 2.0, A.is_gt, A.mult, [], ["ps0", "s2"], 256)
+                for x in range(2):
+                    cs = [c for c in range(16) if (c // 2 + d // 2) % 8 // 4 == x]
+                    mm([(ps[2 * x][:, 32 * ((c // 2 + d // 2) % 4):32 * ((c // 2 + d // 2) % 4 + 1)], T.OH[:, 128 * (16 * d + c):128 * (16 * d + c + 1)],
+                         T.Aw[:, 32 * (16 * d + c):32 * (16 * d + c + 1)], False, d == 2 and c == cs[-1]) for c in cs],
+                       ["Aw%d" % d] + ["OH%d" % (4 * d + y) for y in range(4)], ["ps%d" % (2 * x)], 8 * 64)
+            for s, k, x in ((T.s1, "s1", 0.5), (T.s2, "s2", 73300.5)):
+                ts(s[:, 0:128], ps[0][:, 0:128], x, 2.0, A.is_gt, A.mult, [], ["ps0", k])
+                act(s[:, 128:256], ps[2][:, 0:128], AF.Sign, -x, 1.0, [], ["ps2", k + "b"])
             for s, k, I in ((T.s1, "s1", Im4k if t else I2k), (T.s2, "s2", I2k)):
-                mm([(ps[1][:, x:256:2], s[:, x::2], I, False, k == "s2" and x == 1) for x in range(2)], [k, "I2048", "I-4096"], ["ps1"], 256)
-            ts(T.UL[:], ps[1][:, 0:256], c_ul, 2048.0 * t, A.add, A.add, ["c_ul"], ["ps1", "UL"], 256)
+                mm([(ps[1][:, x:256:2], s[:, x::2], I, False, k == "s2" and x == 1) for x in range(2)], [k, k + "b", "I2048", "I-4096"], ["ps1"], 256)
+            ts(T.UL[:], ps[1][:, 0:256], (c_ul, c_um)[t], None, A.add, None, ["c_ul", "c_um"], ["ps1", "UL"], 256)
             src = wk[t] + ["%s%d" % (x, j) for x in ("Hf", "Db") for j in range(4)] + ["Hz", "UL"]
             for j in range(8):
                 pick(T.WA[:, W[t + 1] + 512 * j:W[t + 1] + 512 * (j + 1)], T.WA[:, NW * t:NW * (t + 3)].indirect(T.UL[:, 32 * j:32 * (j + 1)]),
@@ -565,12 +552,14 @@ def build(g, T, nxt, prv, prv2, nx2):
             else:
                 gather(h, T.X3, "X3", T.V2[:, :], keys("V2"), T.pos, 0, ["pos%d" % h], T.Wg3, "Wg2")
                 gather(h, T.X3, "X3", T.Fr[:, :], ["Fr"], T.L3, 0, ["L3%d" % h], T.X3, "X3")
-            if not (up and t in ACC):
+            if up:
                 reduce(h, T.X3, "X3", h == NH - 1)
-        if up and t in ACC:
-            heap(T.X3, "X3")
-            for h in hs:
-                reduce(h, T.X1, "X1", h == NH - 1)
+                continue
+            for j in chunks(h):
+                sl = slice(CH * j, CH * (j + 1))
+                add({"v": (vd(CH), lambda sl=sl: V.tensor_tensor_scan(T.X2[:, sl], T.keep[:], T.X3[:, sl], 0.0, A.mult, A.add))},
+                    ["keep", "X3%d" % j], ["X2%d" % j])
+                mm([(ps[3][:, 32 * j:32 * (j + 1)], T.IU[:], T.X2[:, CH * j + 15:CH * (j + 1):16], False, j == 3)], ["IU", "X2%d" % j], ["ps3"], 256)
         tt(T.ys[:, a:b], ps[3][:, 0:128], T.xvs[:, a:b], A.mult, ["xvs"], ["ps3", "ys" + n], 128)
         dma([(T.cv[:, a:b], T.cvs[0::16, a:b])], ["cvs" + n], ["cv" + n], 0.1)
         dma([(T.y[:, a:b], T.ys[:, a:b])], ["ys" + n], ["y" + n], 0.2)
@@ -587,6 +576,11 @@ def depends(ops):
         for k in o["w"]:
             d.update(readers.get(k, []))
         d.discard(i)
+        o["soft"] = {j for j in d if "p" not in o["alts"] and "p" not in ops[j]["alts"] and not any(k[:2] == "PW" for k in o["w"] + ops[j]["w"])
+                     and all(k[:2] == "ps" for k in (set(o["r"]) | set(o["w"])) & set(ops[j]["w"]) | set(o["w"]) & set(ops[j]["r"]))}
+        if "after" in o:
+            d.add(o["after"])
+            o["soft"].add(o["after"])
         deps.append(sorted(d))
         for k in o["r"]:
             readers.setdefault(k, []).append(i)
@@ -619,6 +613,8 @@ def place(ops, seq, before, can, back):
         t0, pe = 0.0, can[c] == "p"
         for d in before[c]:
             t = fin[d] if pe and where[d] == "p" else fin[d] + WAKE
+            if not back and d == o.get("after"):
+                t = start[d] + 1e-3
             if t > t0:
                 t0 = t
         if o["kind"] != "c":
@@ -648,44 +644,59 @@ def place(ops, seq, before, can, back):
     return where, start, fin
 
 
-def replay(cost, deps, seq, where):
+def replay(cost, seq, where, old=None, first=0, again=3):
     n = len(seq)
-    free, last, end, by, held = dict.fromkeys("vspgyw", 0.0), dict.fromkeys("vspgyw"), [0.0] * n, [None] * n, [False] * n
-    seen = [0.0] * n
-    total, tail = 0.0, None
-    for c in seq:
+    free, last = dict.fromkeys("vspgyw", 0.0), dict.fromkeys("vspgyw")
+    issued, turned, lead = 0.0, False, cost[n]
+    if old is None:
+        end, off, by, held, first = [0.0] * n, [0.0] * n, [None] * n, [False] * n, 0
+    else:
+        end, off, by, held = [list(x) for x in old]
+        for j in range(first - 1, -1, -1):
+            c = seq[j]
+            q = where[c]
+            if last[q] is None:
+                last[q], free[q] = c, off[c]
+            if last["w"] is None and cost[c][q][1]:
+                last["w"], free["w"], issued = c, end[c] - 0.7 * lead, off[c]
+            if None not in last.values():
+                break
+    for j in range(first, n):
+        c = seq[j]
         q = where[c]
-        t0, p = 0.0, None
-        if q == "p":
-            for d in deps[c]:
-                t = end[d] if where[d] == "p" else seen[d]
-                if t > t0:
-                    t0, p = t, d
-        else:
-            for d in deps[c]:
-                if seen[d] > t0:
-                    t0, p = seen[d], d
-        if free[q] > t0:
-            t0, p, held[c] = free[q], last[q], True
-        dur, wire = cost[c][q]
-        e = free[q] = t0 + dur
+        dur, wire, hard, soft = cost[c][q]
+        t0, p = -1.0, None
+        for d in hard:
+            if end[d] > t0:
+                t0, p = end[d], d
+        t0 += WAKE
+        for d in soft:
+            if where[d] != q and end[d] + WAKE > t0:
+                t0, p = end[d] + WAKE, d
+        held[c] = free[q] > t0
+        if held[c]:
+            t0, p = free[q], last[q]
+        e = off[c] = free[q] = t0 + dur
         last[q] = c
         if wire:
-            if free["w"] > e + 1.0:
+            turned, issued = turned or e < issued - 0.3, max(e, issued)
+            if free["w"] > e + lead:
                 p, held[c] = last["w"], True
-                e = free["w"] - 1.0
-            free["w"] = e + 1.0 + wire
+                e = free["w"] - lead
+            free["w"] = e + lead + wire
             last["w"] = c
-            e += 1.8 + wire
-        end[c], seen[c], by[c] = e, e + WAKE, p
-        if e > total:
-            total, tail = e, c
-    pairs = []
+            e += 1.7 * lead + wire
+        end[c], by[c] = e, p
+    if turned and again:
+        seq.sort(key=lambda i: off[i] - 0.5 * cost[i][where[i]][0])
+        return replay(cost, seq, where, None, 0, again - 1)
+    total = max(end)
+    tail, pairs = end.index(total), []
     while by[tail] is not None:
         if held[tail]:
             pairs.append((by[tail], tail))
         tail = by[tail]
-    return total + MEAN * sum(end) / n, pairs, end
+    return total + MEAN * sum(end) / n, pairs, (end, off, by, held), again < 3
 
 
 def schedule(ops, deps):
@@ -698,29 +709,47 @@ def schedule(ops, deps):
     for i in range(n - 1, -1, -1):
         o = ops[i]
         key[i] = (min(a[0] for a in o["alts"].values()) + o["lat"] + WAKE + (1.8 if o["kind"] != "c" else 0.0)
-                  + max([key[s] for s in succ[i]] + [0.0]) + o["up"])
+                  + max([key[s] for s in succ[i]] + [0.0]))
     can = [ops[i]["can"] or "".join(ops[i]["alts"]) for i in range(n)]
-    cost = [{q: (o["alts"][q][0] * (1 + SLOWER * (o["slow"] - 1) if o["kind"] == "c" else 1.0), o["lat"]) for q in o["alts"]} for o in ops]
+    soft = [[d for d in deps[i] if d in ops[i]["soft"] or ("p" in ops[i]["alts"] and "p" in ops[d]["alts"])] for i in range(n)]
+    hard = [[d for d in deps[i] if d not in soft[i]] for i in range(n)]
+    costs = [[{q: (o["alts"][q][0] * (1 + slow * (o["slow"] - 1) if o["kind"] == "c" else 1.0), o["lat"] * wire, hard[i], soft[i])
+               for q in o["alts"]} for i, o in enumerate(ops)] + [lead] for slow, wire, lead, share in PACES]
+
+    def judge(seq, where, old=None, first=0):
+        m, pairs, keep = 0.0, [], []
+        for x, pace in enumerate(PACES):
+            y = replay(costs[x], seq, where, old and old[x], first, 0 if x else 3)
+            if y[3] and x == 0:
+                old = None
+            m, pairs = m + pace[3] * y[0], pairs + y[1]
+            keep.append(y[2])
+        return m, seq, where, pairs, keep
+
     best = None
     for rnd in range(TURN):
+        for i in range(n - 1, -1, -1):
+            key[i] = max([key[i] + ops[i]["up"]] + [key[s] + 1e-6 for s in succ[i]])
         where, start, fin = place(ops, sorted(range(n), key=lambda i: (-key[i], i)), deps, can, False)
-        seq = sorted(range(n), key=lambda i: (start[i], fin[i]))
-        m, pairs, end = replay(cost, deps, seq, where)
-        if best is None or m < best[0]:
-            best = (m, seq, where, pairs)
+        now = judge(sorted(range(n), key=lambda i: (start[i], fin[i])), where)
+        if best is None or now[0] < best[0]:
+            best = now
         key = place(ops, sorted(range(n), key=lambda i: -fin[i]), succ, where, True)[2]
-    dice = np.random.default_rng(SEED).random((ROUNDS, 4))
+    dice = np.random.default_rng(SEED).random((ROUNDS, 4)).tolist()
     now = best
     for rnd in range(ROUNDS):
-        level, seq, where, pairs = now
+        level, seq, where, pairs, old = now
         u = dice[rnd]
         b, c = pairs[int(u[0] * len(pairs))]
         x = b if u[1] < 0.5 else c
         if len(ops[x]["alts"]) > 1 and u[2] < FLIP:
-            where = list(where)
+            where, seq = list(where), list(seq)
             where[x] = "s" if where[x] == "v" else "v"
+            i = seq.index(x)
         else:
             i, j = seq.index(b), seq.index(c)
+            if i > j:
+                continue
             span = seq[i:j + 1] if x == b else seq[i:j + 1][::-1]
             moved = {x}
             for y in span[1:]:
@@ -730,22 +759,13 @@ def schedule(ops, deps):
                 continue
             stay, go = [y for y in seq[i:j + 1] if y not in moved], [y for y in seq[i:j + 1] if y in moved]
             seq = seq[:i] + (stay + go if x == b else go + stay) + seq[j + 1:]
-        m, pairs, end = replay(cost, deps, seq, where)
-        if m <= level - HEAT * (1.0 - rnd / ROUNDS) * math.log(u[3] + 1e-12):
-            now = (m, seq, where, pairs)
-            if m < best[0]:
-                best = now
-    m, seq, where, pairs = best
-    fin = replay(cost, deps, seq, where)[2]
-    start = [fin[i] - cost[i][where[i]][0] - (1.8 + ops[i]["lat"] if ops[i]["lat"] else 0.0) for i in range(n)]
-    vec = [i for i in seq if where[i] == "v"]
-    at = {i: j for j, i in enumerate(seq)}
-    for i in seq:
-        if ops[i]["lat"] > 1.3 and ops[i]["up"] < 20.0 and start[i] > max([fin[d] for d in deps[i]] + [0.0]) + 1.0:
-            d = [j for j in vec if fin[j] < start[i] - 0.3 and at[j] < at[i]]
-            if d:
-                deps[i] = sorted(set(deps[i] + [d[-1]]))
-    return {q: [i for i in seq if where[i] == q] for q in "vspgy"}, where, start, fin
+        new = judge(seq, where, old, i)
+        if new[0] <= level - HEAT * (1.0 - rnd / ROUNDS) * math.log(u[3] + 1e-12):
+            now = new
+            if new[0] < best[0]:
+                best = new
+    seq, where = best[1:3]
+    return {q: [i for i in seq if where[i] == q] for q in "vspgy"}, where, best[4][0][1], best[4][0][0]
 
 
 PLAN = {}
@@ -761,7 +781,9 @@ def rank_program(g, core, T, topo):
     if "p" not in PLAN:
         deps = depends(ops)
         PLAN["p"] = (deps, schedule(ops, deps))
+        PLAN["soft"] = [o["soft"] for o in ops]
     deps, (order, where, start, fin) = PLAN["p"]
+    soft = PLAN["soft"]
     queue = {"v": g.vector, "s": g.scalar, "p": g.tensor, "g": g, "y": g.sync}
     n = len(ops)
     pos = [0] * n
@@ -775,10 +797,10 @@ def rank_program(g, core, T, topo):
             top = {}
             for d in deps[i]:
                 if ops[d]["kind"] != "c":
-                    if d not in got:
+                    if d not in got and d not in soft[i]:
                         got.add(d)
                         waits[i].append(d)
-                elif not (q == "p" and where[d] == "p"):
+                elif not (q == where[d] and (q == "p" or d in soft[i])):
                     e = where[d]
                     if pos[d] > seen.get(e, -1) and (e not in top or pos[d] > pos[top[e]]):
                         top[e] = d

import math
import numpy as np
from concourse.bass import DstId, RemoteDMATransfer
from concourse.mybir import AluOpType as A, ActivationFunctionType as AF

NW, E, EP = 4096, 128, 3
BF, F16, F32, I32, U16 = "bfloat16", "float16", "float32", "int32", "uint16"
NH = 2
HE = E // NH
BETA = 2296
E2, E3 = 6144, 3 * BETA
BIG, FNW = 2.0 ** 23, 147456.0


def _sb(n, d):
    return ("sbuf", [128, n], d)


SCRATCH = {
    "WA": _sb(4 * NW, BF), "W2": _sb(NW, BF), "W3": _sb(NW, BF), "F": _sb(NW, BF), "Fr": _sb(NW, BF),
    "D0": ("dram", [144, 2048], BF), "D1": ("dram", [144, 2048], BF),
    "TT": _sb(4352, BF), "T2": _sb(E2 + 16, BF), "T3": _sb(E3 + 8, BF), "G3": _sb(2048, BF),
    "Wg1": _sb(2048, BF), "Wg2": _sb(2048, BF), "Wg3": _sb(2048, BF), "C": _sb(2048, BF),
    "X1": _sb(2048, F32), "X2": _sb(2048, F32), "X3": _sb(2048, F32), "V2": _sb(2048, F32),
    "OH": _sb(48 * 128, BF), "Aw": _sb(1536, BF), "GA": _sb(512, BF), "GB": _sb(512, BF),
    "SF": _sb(2560, BF), "VV": _sb(160, BF), "YY": _sb(288, BF), "YQ": _sb(288, F32), "RT": _sb(640, F16), "fe": _sb(384, BF),
    "ST": _sb(2816, BF), "na": _sb(384, I32), "nb": _sb(384, I32), "bni": _sb(384, I32),
    "taus": _sb(4, F32), "tau1": _sb(8, F32), "tau2": _sb(8, F32), "tau3": _sb(8, F32), "taur": _sb(8, F32),
    "tw": _sb(16, F32), "ti": _sb(4, I32), "xvs": _sb(384, BF), "LA": _sb(512, I32), "nask": _sb(256, BF), "sig": _sb(256, F32),
    "dig": _sb(768, BF), "L1": _sb(384, U16), "bf": _sb(384, F32), "Lp1": _sb(384, F32), "nm1": _sb(256, F16),
    "IX": _sb(176, I32), "IP": _sb(12, I32), "col": _sb(40, F32), "cl2": _sb(20, F32), "Yi": _sb(176, I32), "Yj": _sb(176, I32),
    "MM": _sb(176, BF), "M16": _sb(176, BF), "ML": _sb(176, BF), "MB": _sb(176, BF), "MP": _sb(176, BF), "OW": _sb(176, BF),
    "OW1": _sb(176, BF), "Blk": _sb(176, BF), "IU": _sb(128, F32), "Ib": _sb(144, BF), "Ia": _sb(144, BF), "Iw": _sb(9 * 128, BF),
    "CE": _sb(256, BF), "Dg": _sb(256, BF), "ones": _sb(128, BF), "zero": _sb(256, BF), "bs": _sb(16, F32),
    "NQ": _sb(256, BF), "Tri": _sb(128, BF), "U": _sb(256, BF), "DM": _sb(128, BF), "SelW": _sb(512, BF), "keep": _sb(512, BF),
    "nn": _sb(128, BF), "st": _sb(384, BF), "cap": _sb(128, BF), "flag": _sb(128, BF), "OF": _sb(32, U16), "AD": _sb(128, U16),
    "L2": _sb(128, U16), "Pn": _sb(128, U16), "L3": _sb(128, U16), "pos": _sb(128, U16),
    "Lp": _sb(128, F32), "pa": _sb(128, I32), "pb": _sb(128, I32),
    "nd": _sb(256, F16), "s1": _sb(256, BF), "s2": _sb(256, BF), "UL": _sb(256, U16), "ys": _sb(384, F32), "cvs": _sb(384, F32),
    "sn2": _sb(256, F16), "ln2": _sb(256, F16), "sn3": _sb(256, F16), "ln3": _sb(256, F16),
    "sw": _sb(256, BF), "lw2": _sb(256, BF), "lw3": _sb(256, BF),
}
for _b in range(8):
    SCRATCH["ps%d" % _b] = ("psum", [128, 512], F32)
NDMA, NMSG = 60, 32
SEMAPHORES = ["qv", "qs", "qp", "qg", "sent"] + ["d%d" % i for i in range(NDMA)] + ["a%d" % i for i in range(NMSG)]

CH = 512
EARLY = (2,)
CY, PC, GC, FIX, WAKE, ISSUE, LATE = 0.00085, 0.00044, 1.56, 0.05, 0.22, 0.35, 5.0
PACES = ((0.05, 0.9, 1.1, 0.6), (1.0, 0.9, 1.0, 0.45))
LEAN, ROUNDS, TURN, FLIP, HEAT, MEAN, SEED = 0.5, 72000, 6, 0.4, 0.22, 0.2, 2


def build(g, T, nxt, prv, prv2, nx2):
    ops, boost = [], [0.0]
    V, S, P = g.vector, g.scalar, g.tensor

    def add(alts, r, w, kind="c", lat=0.0, slow=1.4, can=None):
        ops.append({"alts": alts, "r": list(r), "w": list(w), "kind": kind, "lat": lat, "up": boost[0], "slow": slow,
                    "can": can or ("s" if len(alts) > 1 else None)})

    def vd(c):
        return FIX + max(64, c) * CY

    def ts(out, in0, s1, s2, o0, o1, r, w, c=128):
        if o1 is None:
            add({"v": (vd(c), lambda: V.tensor_scalar(out, in0, s1, None, o0))}, r, w)
        else:
            add({"v": (vd(c), lambda: V.tensor_scalar(out, in0, s1, s2, o0, o1))}, r, w)

    def tt(out, a, b, o, r, w, c=256):
        add({"v": (vd(c), lambda: V.tensor_tensor(out, a, b, o))}, r, w)

    def cp(out, a, r, w, c=128, both=False):
        al = {"v": (vd(c), lambda: V.tensor_copy(out, a))}
        if both:
            al["s"] = (vd(c), lambda: S.activation(out, a, AF.Copy))
        add(al, r, w)

    def lin(out, a, k, b, r, w, c=128, cs=None, can=None):
        add({"v": (vd(c), lambda: V.tensor_scalar(out, a, k, b, A.mult, A.add)),
             "s": (vd(cs or c) + 0.015, lambda: S.activation(out, a, AF.Identity, bias=b, scale=k))}, r, w, can=can)

    def relu(out, x, w):
        add({"v": (vd(512), lambda: V.tensor_scalar(out, x, 0.0, None, A.max)),
             "s": (vd(512), lambda: S.activation(out, x, AF.Relu))}, [], w)

    def ms(ap, val, w, c):
        add({"v": (vd(c), lambda: V.memset(ap, val))}, [], w)

    def mm(lst, r, w, cyc):
        def run():
            last = None
            for (o, l, x, a, b) in lst:
                last = P.matmul(o, l, x, a, b)
            return last
        add({"p": (0.01 + cyc * PC, run)}, r, w)

    def dma(pairs, r, w, us, q="y"):
        eng = g.sync if q == "y" else g.scalar
        add({q: (0.07 * len(pairs), [lambda o=o, a=a: eng.dma_start(o, a) for (o, a) in pairs])}, r, w, "dma", us)

    def send(dsts, src, r, w, nbytes):
        add({"g": (ISSUE, (dsts, src))}, r, w, "msg", 0.1 + nbytes / 200e3)

    def iota(out, pat, base, cm, w, n, small=False, r=()):
        w = w + ["gq"]
        if small:
            add({"g": (0.15 + 2 * n * CY, lambda: g.iota(out, pat, base, cm, allow_small_or_imprecise_dtypes=True))}, r, w)
        else:
            add({"g": (0.15 + 2 * n * CY, lambda: g.iota(out, pat, base, cm))}, r, w)

    def act(out, a, f, bias, scale, r, w, c=128):
        add({"s": (vd(c) + 0.015, lambda: S.activation(out, a, f, bias=bias, scale=scale))}, r, w)

    nch = 2048 // CH // NH

    def chunks(h):
        return range(h * nch, (h + 1) * nch)

    def keys(k, h=None):
        return ["%s%d" % (k, j) for j in (range(nch * NH) if h is None else chunks(h))]

    def pick(dst, src, r, w, n, can=None):
        u = 0.06 + n * GC * CY
        add({"v": (u, lambda: V.tensor_copy(dst, src)), "s": (u, lambda: S.activation(dst, src, AF.Copy))}, r, w, slow=1.85, can=can)

    def gather(h, out, okey, win, wkeys, off, o0, okeys, by=None, bkey=None):
        for j in chunks(h):
            k, sl = "%s%d" % (okey, j), slice(j * CH, (j + 1) * CH)
            src = win.indirect(off[:, o0 + j * CH // 16:o0 + (j + 1) * CH // 16])
            if by is None:
                pick(out[:, sl], src, wkeys + okeys, [k], CH)
            else:
                add({"v": (0.05 + CH * GC * CY, lambda s=src, t=out[:, sl], x=by[:, sl]: V.tensor_tensor(t, s, x, A.mult))},
                    wkeys + okeys + ["%s%d" % (bkey, j)], [k], slow=1.85)

    def times(h, out, okey, x, xkey, Wg, wkey):
        for j in chunks(h):
            bk, sl = 4 + j % 2, slice(CH * j, CH * (j + 1))
            mm([(ps[bk][:], I1, Wg[:, sl], True, True)], ["Ib", "%s%d" % (wkey, j)], ["ps%d" % bk], CH)
            tt(out[:, sl], ps[bk][:], x[:, sl], A.mult, ["%s%d" % (xkey, j)], ["ps%d" % bk, "%s%d" % (okey, j)], CH)

    def narrow(h, o, bank, M, mkey, wide, wkey):
        a, b = 16 * HE * h, 16 * HE * (h + 1)
        mm([(o, M[:, 32 - k:160 - k], wide[:, a + k:b:16], k == 0, k == 15) for k in range(16)], [mkey] + keys(wkey, h), [bank], 16 * max(64, HE))

    def reduce(h, wide, wkey, last):
        a, b = 16 * HE * h, 16 * HE * (h + 1)
        for u in range(8):
            mm([(ps[3][:, HE * h:HE * (h + 1)], T.IU[:], wide[:, a + k:b:16], False, last and k == 15) for k in (2 * u, 2 * u + 1)],
               ["IU"] + keys(wkey, h), ["ps3"], 2 * 4 * max(64, HE))

    col = T.col
    (c_k, c_g, c_cap, c_x, c_a2, c_b2, c_a3, c_r0, c_r5, c_r4, c_e2, c_e3, c_e4, c_ul, c_p, c_32p, c_kq, c_p4, c_u, c_v,
     c_xe, c_31, c_hi, c_um) = [col[:, i:i + 1] for i in range(24)]
    c_w = col[:, 24:28]
    ps = [T["ps%d" % b] for b in range(8)]
    W = [0, 3 * NW, 0]
    wk = [["W%s%d" % ("ABA"[t], j) for j in range(8)] for t in range(EP)]
    I384, I3200, Im1, I9, I2304, Im8, I2080, I2k, Im4k = [T.Iw[:, 128 * i:128 * (i + 1)] for i in range(9)]
    I1 = T.Ib[:, 0:128]
    nqk = ["NQ%d" % q for q in range(4)]

    def spread(t, far):
        for x in range(2):
            sl, a, r = slice(2048 * x, 2048 * (x + 1)), W[t] + 2048 * x, wk[t][4 * x:4 * x + 4]
            if not far:
                send([(prv, T.W2[:, sl])], T.WA[:, a:a + 2048], r + ([] if t else ["STl"]), ["W2%d" % x], 524e3)
            else:
                D = T["D%d" % x]
                dma([(D[0:128, :], T.WA[:, a:a + 2048]), (D[128:144, :], T.WA[0:16, a:a + 2048])], r + ([] if t else ["W20"]), ["D%d" % x], 1.4)
                send([(prv2, T.W3[:, sl])], D[16:144, :], ["D%d" % x], ["W3%d" % x], 524e3)

    boost[0] = 40.0
    dma([(T.bni[:], T.bn[:])], [], ["bni"], 0.5)
    boost[0] = 20.0
    dma([(T.taus[:, 0:3], T.tau[:])], [], ["taus"], 0.1, "s")
    dma([(T.ST[96:128, 768:2048], T.ft[0:32, 0:1280])], [], ["STz"], 0.3)
    dma([(T.WA[:, 0:NW], T.wt[:])], [], wk[0], 2.3)
    boost[0] = 0.0
    dma([(T.T2[r::8, 0:E2], T.ft[32 * x:32 * x + 32, 0:E2 // 2]) for x, r in enumerate((2, 3, 7))], ["bni"], ["T2x"], 1.29)
    iota(T.IP[:, 0:1], [[0, 1]], 0, 1, ["IP"], 1)
    iota(T.DM[:], [[0, 8], [1, 16]], 0, 0, ["DM"], 128, True)
    iota(T.Ia[:], [[1, 144]], -64, -1, ["Ia"], 144, True)
    for q, pat in enumerate(([[0, 64], [8, 4]], [[0, 16], [8, 4], [0, 4]], [[0, 4], [8, 4], [0, 16]], [[8, 4], [0, 64]])):
        iota(T.NQ[32 * q:32 * q + 32, :], pat, 1, 0, ["NQ%d" % q], 256, True)
    iota(T.IX[:], [[1, 176]], 0, 0, ["IX"], 176)
    ms(T.zero[:], 0.0, ["zero"], 128)
    ms(T.tau1[:], 0.0, ["tau0"], 8)
    ts(T.ti[:, 0:3], T.taus[:, 0:3], 512.0, None, A.mult, None, ["taus"], ["ti"], 3)
    lin(T.tw[:, 0:3], T.taus[:, 0:3], 512.0, 0.0, ["taus"], ["tw0"], 3)
    tt(T.tw[:, 4:7], T.ti[:, 0:3], T.tw[:, 0:3], A.is_lt, ["ti", "tw0"], ["tw1"], 3)
    tt(T.tw[:, 8:11], T.tw[:, 4:7], T.ti[:, 0:3], A.add, ["ti", "tw1"], ["tw2"], 3)
    lin(T.tau1[:, 0:3], T.tw[:, 8:11], 1.0 / 512, -1.0 / 1024, ["tw2"], ["tau0"], 3)
    lin(T.tau1[:, 4:7], T.tw[:, 8:11], -1.0 / 512, 1.0 / 1024, ["tw2"], ["tau0"], 3)
    send([(prv, T.tau2[:]), (prv2, T.taur[:])], T.tau1[:], ["tau0"], ["tau1", "taur"], 4e3)
    tausent = len(ops) - 1
    dma([(T.tau3[0:112, :], T.taur[16:128, :]), (T.tau3[112:128, :], T.taur[0:16, :])], ["taur"], ["tau2"], 0.1)
    masks = (15, 7, 112, 31, 96, 12, 1, 2, 6)
    for i, m in enumerate(masks):
        ts(T.IP[:, i + 1:i + 2], T.IP[:, 0:1], m, None, A.bitwise_and, None, ["IP"], ["IP%d" % m], 1)
    i15, i7, i112, i31, i96, i12, i1, i2, i6 = [T.IP[:, i + 1:i + 2] for i in range(9)]
    cp(c_k, i15, ["IP15"], ["c_k"], 1)
    ts(c_g, i112, -1.0, 96.0, A.mult, A.add, ["IP112"], ["c_g"], 1)
    ts(c_p, i31, -1.0, 0.5, A.mult, A.add, ["IP31"], ["c_p"], 1)
    ts(c_u, i96, 1.0 / 256, 0.625, A.mult, A.add, ["IP96"], ["c_u"], 1)
    tt(c_xe, c_u, c_p, A.subtract, ["c_u", "c_p"], ["c_xe"], 1)
    ts(c_31, i31, 31.0, None, A.is_equal, None, ["IP31"], ["c_31"], 1)
    ms(T.Tri[:], 0.0, ["Tri"], 64)
    for q in range(4):
        ms(T.Tri[32 * q:32 * q + 32, 32 * q:128], 1.0 / 256, ["Tri"], 64)
    mm([(ps[4][:, 0:256], T.Tri[:], T.NQ[:], True, True)], ["Tri"] + nqk, ["ps4"], 256)
    ts(ps[4][:, 256:512], ps[4][:, 0:256], c_xe, c_31, A.is_equal, A.subtract, ["c_xe", "c_31"], ["ps4", "PW"], 256)
    tt(T.U[:], ps[4][:, 256:512], T.NQ[:], A.mult, nqk + ["PW"], ["ps4", "U"], 256)
    lin(T.bs[:], T.DM[:, 0:16], -1.0, c_p, ["DM", "c_p"], ["bs"], 16)
    for s in range(16):
        act(T.C[:, 128 * s:128 * (s + 1)], T.DM[:], AF.Sign, T.bs[:, 15 - s:16 - s], 1.0, ["DM", "bs"], ["Sh%d" % s, "C%d" % (s * 128 // CH)])
    for s in range(8):
        b = (4, 5, 2, 0)[s % 4]
        mm([(ps[b][:, 256 * x:256 * (x + 1)], T.C[:, 128 * (2 * s + x):128 * (2 * s + x + 1)], T.U[:], True, True) for x in range(2)],
           ["U", "Sh%d" % (2 * s), "Sh%d" % (2 * s + 1), "C%d" % (s * 256 // CH)], ["ps%d" % b], 512)
        lin(T.TT[:, 256 + 512 * s:768 + 512 * s], ps[b][:], 0.5, 0.0, [], ["ps%d" % b, "TT%d" % s], 512)
    lin(T.TT[:, 0:256], T.zero[:], 1.0, 0.0, ["zero"], ["TT8"], 128, 256)
    ttk = ["TT%d" % s for s in range(9)]
    lin(T.ones[:], T.DM[:], 0.0, 1.0, ["DM"], ["ones"], 64, 128)
    ts(T.Yj[:], T.IX[:], c_g, None, A.add, None, ["IX", "c_g"], ["Yj"], 176)
    ts(T.Yi[:], T.Yj[:], 127, None, A.bitwise_and, None, ["Yj"], ["Yi"], 176)
    ts(T.MM[:], T.Yi[:], 0.0, -4.0, A.is_equal, A.mult, ["Yi"], ["MM"], 176)
    act(T.Ib[:], T.Ia[:], AF.Abs, 0.0, 1.0, ["Ia"], ["Ib"], 144)
    act(T.Ia[:], T.Ib[:], AF.Abs, -64.0, 1.0, ["Ib"], ["Ia"], 144)
    act(T.Ib[:], T.Ia[:], AF.Relu, 1.0, -1.0, ["Ia"], ["Ib"], 144)
    ts(c_cap, i15, 12.0, 15.0, A.max, A.subtract, ["IP15"], ["c_cap0"], 1)
    lin(c_cap, c_cap, -1.0, 0.0, ["c_cap0"], ["c_cap", "c_cap0"], 1)
    lin(c_a2, c_k, 128.0, 3200.0 * 512, ["c_k"], ["c_a2"], 1)
    lin(c_b2, c_k, -1.0, 14.0 - 9 * 512, ["c_k"], ["c_b2"], 1)
    lin(c_a3, c_k, float(BETA), (BETA + 8.0) * 512, ["c_k"], ["c_a3"], 1)
    lin(c_e2, c_k, -512.125, 4096.0, ["c_k"], ["c_e2"], 1)
    ts(c_hi, i112, 64.0, 2048.0, A.is_ge, A.mult, ["IP112"], ["c_hi"], 1)
    lin(c_ul, c_hi, 2.0, c_k, ["c_k", "c_hi"], ["c_ul"], 1)
    ts(c_um, c_k, 8192.0, c_hi, A.add, A.subtract, ["c_k", "c_hi"], ["c_um"], 1)
    ts(c_e3, i15, 5.0, -940.0, A.is_equal, A.mult, ["IP15"], ["c_e3"], 1)
    ts(c_e4, i15, 13.0, -1.0, A.is_equal, A.mult, ["IP15"], ["c_e4"], 1)
    for c, M, r in ((c_r0, T.ML, 0), (c_r5, T.MB, 5), (c_r4, T.MP, 4)):
        ts(c, i7, float(r), -0.25, A.is_equal, A.mult, ["IP7"], ["c_r%d" % r], 1)
        lin(M[:], T.MM[:], c, 0.0, ["MM", "c_r%d" % r], ["M%d" % r], 88, 176)
    lin(T.M16[:], T.MM[:], -0.25, 0.0, ["MM"], ["M16"], 88, 176)
    ts(T.Blk[:], T.Yi[:], 15.0, None, A.is_le, None, ["Yi"], ["Blk"], 176)
    ts(c_kq, i12, 0.25, None, A.mult, None, ["IP12"], ["c_kq"], 1)
    ts(c_x, i1, 3.0, 1.0, A.mult, A.add, ["IP1"], ["c_x"], 1)
    ts(c_v, i2, 7.5, 1.0, A.mult, A.add, ["IP2"], ["c_v"], 1)
    tt(c_p4, c_x, c_v, A.mult, ["c_x", "c_v"], ["c_p4"], 1)
    ts(col[:, 28:32], T.DM[:, 0:4], c_kq, c_p4, A.is_equal, A.mult, ["DM", "c_kq", "c_p4"], ["c_w0"], 4)
    ts(col[:, 32:36], T.DM[:, 0:4], c_kq, -256.0, A.is_gt, A.mult, ["DM", "c_kq"], ["c_w1"], 4)
    tt(c_w, col[:, 28:32], col[:, 32:36], A.add, ["c_w0", "c_w1"], ["c_w"], 4)
    lin(T.OW[:], T.zero[:, 0:176], 1.0, 0.0, ["zero"], ["OW"], 88, 176)
    for q in range(4):
        ts(T.OW[:, q::16], T.Yi[:, q::16], float(q), c_w[:, q:q + 1], A.is_equal, A.mult, ["Yi", "c_w"], ["OW"], 11)
    lin(T.OW1[:], T.OW[:], c_cap, 0.0, ["OW", "c_cap"], ["OW1"], 88, 176)
    for I, x in ((I384, 384), (I3200, -3200), (Im1, -1), (I9, 9), (I2304, -BETA - 8), (Im8, -8), (I2080, 2080), (I2k, 2048), (Im4k, -4096)):
        lin(I, I1, float(x), 0.0, ["Ib"], ["I%d" % x], 64, 128)
    cp(T.CE[:, 0:128], T.IX[:, 0:128], ["IX"], ["CE0"])
    lin(T.CE[:, 128:256], T.CE[:, 0:128], 16.0, 0.0, ["CE0"], ["CE1"], 64, 128)
    lin(T.T2[:, E2:E2 + 16], T.zero[:, 0:16], 1.0, c_e2, ["zero", "c_e2"], ["T2e"], 16)
    ts(T.T3[:, E3:E3 + 8], T.zero[:, 0:8], c_e3, c_e4, A.add, A.add, ["zero", "c_e3", "c_e4"], ["T3e"], 8)
    cp(T.IU[:], I1, ["Ib"], ["IU"], 128, True)
    boost[0] = 6.0
    cp(T.L1[:], T.bni[:], ["bni"], ["L1"], 384)
    ts(T.bf[:], T.bni[:], -2048.0, None, A.add, None, ["bni"], ["bf"], 384)
    cp(T.dig[:, 0:384], T.bf[:], ["bf"], ["hi"], 384, True)
    mm([(ps[3][:, 0:384], Im1, T.dig[:, 0:384], True, True)], ["hi", "I-1"], ["ps3"], 384)
    tt(T.dig[:, 384:768], ps[3][:, 0:384], T.bf[:], A.add, ["bf"], ["ps3", "lo"], 384)
    lin(T.Lp1[:], T.bf[:], 1.0, 3232.0, ["bf"], ["Lp1"], 384)

    def candidates(t):
        a, b = 128 * t, 128 * (t + 1)
        part = [T.dig[:, a:b], T.dig[:, 384 + a:384 + b]]
        pk = ["hi", "lo", "Ib"]
        dma([(T.ST[:, 2048 + 384 * x + 128 * j:2048 + 384 * x + 128 * (j + 1)], part[x]) for x in range(2) for j in range(3)]
            + [(T.ST[p:q, 512 + 640 * x + 128 * s:640 + 640 * x + 128 * s], T.dig[p + s:q + s, 384 * x + a:384 * x + b])
               for x in range(2) for s in range(2, 7) for p, q in ((0, 112), (112, 128 - s))], ["hi", "lo", "STz"], ["STp"], 1.2)
        mm([(ps[6][:, 128 * j:128 * (j + 1)], T.Ib[:, j + 1:j + 129], part[x], x == 0, x == 1) for j in range(3) for x in range(2)],
           pk, ["ps6"], 768)
        mm([(ps[7][:, 128 * j:128 * (j + 1)], I2080, part[x], x == 0, x == 1) for j in range(3) for x in range(2)], pk + ["I2080"], ["ps7"], 768)
        for j in range(3):
            tt(T.na[:, 128 * j:128 * (j + 1)], ps[6][:, 128 * j:128 * (j + 1)], T.Lp1[:, a:b], A.mult, ["Lp1"], ["ps6", "na%d" % j], 128)
        nak = ["na0", "na1", "na2"]
        tt(T.na[:], ps[7][:, 0:384], T.na[:], A.add, [], ["ps7"] + nak, 384)
        ts(T.nb[:], T.na[:], 5, 4095, A.arith_shift_right, A.bitwise_and, nak, ["nb"], 384)
        cp(T.ST[:, 0:384], T.nb[:], ["nb"], ["STh"], 384)
        mm([(ps[7][:, 0:384], Im1, T.ST[:, 0:384], True, True)], ["STh", "I-1"], ["ps7"], 384)
        tt(T.ST[:, 384:768], ps[7][:, 0:384], T.nb[:], A.add, ["nb"], ["ps7", "STl"], 384)
        rows = [(r + 8 * x, 768 + 640 * x + 128 * i) for i, r in enumerate((5, 1, 6)) for x in range(2)] + [(4 + 8 * x, 2048 + 384 * x) for x in range(2)]
        dma([(T.T2[r::16, 0:E2], T.ST[:, c:c + 384]) for r, c in rows], ["STp"] + (["W31"] if t else []), ["T2b"], 3.0)
        dma([(T.T2[8 * x::16, 0:E2], T.ST[:, 384 * x:384 * (x + 1)]) for x in range(2)], ["STh", "STl"], ["T2a"], 1.0)
        ops[-1]["after"] = len(ops) - 2

    boost[0] = 8.0
    candidates(0)
    boost[0] = 12.0
    spread(0, False)
    ops[-2]["after"], ops[-1]["after"], sent0 = tausent, len(ops) - 2, len(ops) - 1
    boost[0] = 0.0
    dma([(T.F[:], T.ft[:])], ["T2a"], ["F"], 2.3)
    spread(0, True)
    dma([(T.Fr[0:112, :], T.ft[16:128, :]), (T.Fr[112:128, :], T.ft[0:16, :])], ["W30"], ["Fr"], 2.5)
    for j in range(5):
        iota(T.T3[:, 2048 + 968 * j:3016 + 968 * j], [[0, 968]], 0, 0, ["T3x", "T3b"], 968, True)
        if j == 2:
            ops[-1]["after"] = sent0
    dma([(T.xvs[:], T.xv[:])], ["W21"], ["xvs"], 0.3)
    iota(T.LA[:], [[0, 512]], 0, 0, ["LA"], 512)
    dma([(T.LA[0::16, 0:256], T.lab[:]), (T.LA[0::16, 256:512], T.ask[:])], [], ["LA"], 0.2)
    iota(T.YY[:, 0:128], [[1, 16], [0, 8]], -8, 0, ["YY"], 128, True)
    iota(T.YY[:, 128:256], [[0, 16], [1, 8]], -4, 0, ["YY"], 128, True)
    iota(T.YY[:, 256:288], [[1, 16], [16, 2]], -16, 0, ["YY"], 32, True)
    for j in range(2):
        iota(T.SF[:, 1280 * j:1280 * (j + 1)], [[0, 1280]], 0, 0, ["SF"], 1280, True)
    iota(T.keep[:], [[0, 32], [1, 16]], 0, 0, ["keep"], 512, True)
    ts(T.keep[:], T.keep[:], 1.0, None, A.min, None, [], ["keep"], 256)
    iota(T.SelW[:], [[0, 512]], 0, 0, ["SelW"], 512, True)
    add({"g": (0.2 + 1024 * CY, lambda: g.affine_select(T.SelW[:], T.SelW[:], [[16, 8], [0, 64]], A.not_equal, 1.0, 0, -1))}, [], ["SelW", "gq"])
    kc = [T.cl2[:, i:i + 1] for i in range(20)]
    boost[0] = -LATE
    ts(kc[0], i1, 2.0, -1.0, A.mult, A.add, ["IP1"], ["k0"], 1)
    lin(kc[1], kc[0], 0.5, -0.5, ["k0"], ["k1"], 1)
    for i, v in enumerate((-1544.0, 10748.0, 51184.0, 1.0)):
        ts(kc[2 + i], i6, 2.0 * i, v, A.is_equal, A.mult, ["IP6"], ["k%d" % (2 + i)], 1)
    ts(kc[6], i1, kc[2], kc[3], A.add, A.add, ["IP1", "k2", "k3"], ["k6"], 1)
    ts(kc[7], kc[6], kc[4], kc[5], A.add, A.add, ["k6", "k4", "k5"], ["k7"], 1)
    for i in range(3):
        ts(kc[8 + i], i6, 2.0 * i, kc[0], A.is_equal, A.mult, ["IP6", "k0"], ["k%d" % (8 + i)], 1)
    lin(kc[10], kc[10], BIG, 0.0, ["k10"], ["k10"], 1)
    ts(kc[11], i6, 2.0, kc[1], A.is_le, A.mult, ["IP6", "k1"], ["k11"], 1)
    ts(kc[12], i7, 4.0, -BIG, A.is_equal, A.mult, ["IP7"], ["k12"], 1)
    ts(kc[13], i7, 6.0, -1.0, A.is_equal, A.mult, ["IP7"], ["k13"], 1)
    lin(kc[14], kc[13], -1.5, 0.0, ["k13"], ["k14"], 1)
    lin(kc[15], kc[13], BIG, 0.0, ["k13"], ["k15"], 1)
    lin(kc[16], kc[13], -0.25 * BIG, 0.0, ["k13"], ["k16"], 1)
    ts(kc[17], i15, 2.0, 1000.0, A.is_ge, A.mult, ["IP15"], ["k17"], 1)
    lin(kc[18], c_k, 8.0, kc[17], ["c_k", "k17"], ["k18"], 1)
    act(T.YQ[:], T.YY[:], AF.Square, 0.5, 1.0, ["YY"], ["YQ"], 288)
    terms = ((T.YY[:, 0:128], kc[8], kc[11], 0), (T.YY[:, 128:256], kc[9], 0.0, 0), (T.YQ[:, 0:128], kc[13], kc[14], 0),
             (T.YQ[:, 128:256], kc[13], 0.0, 0), (T.YY[:, 256:288], kc[10], kc[12], 128), (T.YQ[:, 256:288], kc[15], kc[16], 128))
    lst = []
    for i, (x, m, v, o) in enumerate(terms):
        w = 32 if o else 128
        y = T.OH[:, 128 * i:128 * i + w]
        lin(y, x, m, v, ["YY", "YQ"] + ["k%d" % j for j in range(8, 17)], ["OH%d" % (i // 4)], w)
        lst.append((ps[5][:, o:o + w], I1, y, i in (0, 4), i in (3, 5)))
    mm(lst, ["Ib", "OH0", "OH1"], ["ps5"], 640)
    cp(T.VV[:], ps[5][:, 0:160], [], ["ps5", "VV"], 160, True)
    dma([(T.SF[8 * c:8 * c + 8, 128 * c:128 * (c + 1)], T.VV[8 * c:8 * c + 8, 0:128]) for c in range(16)], ["VV", "SF"], ["SFb"], 0.8)
    dma([(T.SF[8 * c:8 * c + 8, 2048 + 32 * c:2080 + 32 * c], T.VV[8 * c:8 * c + 8, 128:160]) for c in range(16)], ["VV", "SF"], ["SFa"], 0.8)
    ts(T.Yj[:, 0:128], T.Yi[:, 32:160], 126, None, A.bitwise_and, None, ["Yi"], ["Yj"])
    for i in range(3):
        ts(T.RT[:, 128 * i:128 * (i + 1)], T.Yj[:, 0:128], kc[18], 2.0 * i, A.subtract, A.is_equal, ["Yj", "k18"], ["RT%d" % i])
    ts(T.RT[:, 384:512], T.RT[:, 128:256], -8.0, None, A.mult, None, ["RT1"], ["RT3"], 64)
    ts(T.RT[:, 512:640], T.RT[:, 256:384], -32.0, None, A.mult, None, ["RT2"], ["RT4"], 64)
    ts(c_32p, T.IP[:, 0:1], 32.0, None, A.mult, None, ["IP"], ["c_32p"], 1)
    lin(T.Dg[:, 0::2], I1, c_32p, 0.0, ["Ib", "c_32p"], ["Dg0"], 64, 128)
    lin(c_32p, c_32p, 1.0, 16.0, ["c_32p"], ["c_32p"], 1)
    lin(T.Dg[:, 1::2], I1, c_32p, 0.0, ["Ib", "c_32p"], ["Dg1"], 64, 128)
    ms(T.WA[:, 2 * NW - 1:2 * NW], 0.0, ["Hz"], 1)
    ts(T.nask[:], T.LA[:, 256:512], -1.0, 0.5, A.mult, A.add, ["LA"], ["nask"], 256)
    ts(T.sig[:], T.LA[:, 0:256], -FNW - 2.0, 2.0, A.mult, A.add, ["LA"], ["sig"], 256)
    cp(T.nm1[:], T.bf[:, 0:256], ["bf"], ["nm1"], 256)
    boost[0] = 0.0

    def halves(t):
        for j in range(4):
            a, b = 1024 * j, 1024 * (j + 1)
            src = wk[t][2 * j:2 * j + 2]
            e = b - 1 if j == 3 else b
            ts(T.WA[:, NW + a:NW + e], T.WA[:, W[t] + a:W[t] + e], 0.5, 0.25, A.mult, A.max, src, ["Hf%d" % j], 512)
            ts(T.WA[:, 2 * NW + a:2 * NW + b], T.WA[:, W[t] + a:W[t] + b], 2.0, 4.0, A.mult, A.min, src, ["Db%d" % j], 512)

    def strong(h, d, Wg, win, wkeys, off, o0, okeys):
        k, tau = "Wg%d" % d, (T.tau1, T.tau2, T.tau3)[d]
        gather(h, Wg, k, win, wkeys, off, o0, okeys)
        for j in chunks(h):
            x, y = Wg[:, CH * j:CH * (j + 1)], T.C[:, CH * j:CH * (j + 1)]
            add({"v": (vd(CH // 2), lambda x=x, y=y: V.tensor_scalar(y, x, tau[:, d:d + 1], 0.5, A.is_ge, A.subtract)),
                 "s": (vd(CH), lambda x=x, y=y: S.activation(y, x, AF.Sign, bias=tau[:, 4 + d:5 + d]))},
                ["%s%d" % (k, j), "tau%d" % d], ["C%d" % j], can="v")
        o, bk = ps[h][:, 0:HE], "ps%d" % h
        narrow(h, o, bk, T.MM, "MM", T.C, "C")
        ts(T.st[:, 128 * d + HE * h:128 * d + HE * (h + 1)], o, -0.5, None, A.is_lt, None, [], [bk, "st%d%d" % (d, h)], HE)

    def lookup(h, M, x, ks):
        bk, e0 = "ps%d" % h, HE * h
        o = ps[h][:, 128:128 + HE // 4]
        mm([(o, M[:, 32 - 4 * r:160 - 4 * r], x[:, e0 + r:e0 + HE:4], r == 0, r == 3) for r in range(4)], ks, [bk], 256)
        of = T.OF[:, e0 // 4:(e0 + HE) // 4]
        ts(of, o, 4096.0, None, A.add, None, [], [bk, "OF%d" % h], 32)
        sl = slice(4 * e0, 4 * (e0 + HE))
        pick(T.GA[:, sl], T.TT[:, :].indirect(of), ttk + ["OF%d" % h], ["GA%d" % h], 4 * HE)
        lin(T.GB[:, sl], T.GA[:, sl], 0.125, 127.75, ["GA%d" % h], ["GB%d" % h], 2 * HE, 4 * HE, "v")

    def combine(h, o, bank, Ia, Ib, ks, more):
        e0 = HE * h
        lst = [(o, I1, x, i == 0, False) for i, x in enumerate(more)]
        lst += [(o, Ia, T.GA[:, 4 * e0 + q:4 * (e0 + HE):4], q == 0 and not more, False) for q in range(4)]
        lst += [(o, Ib, T.GB[:, 4 * e0 + q:4 * (e0 + HE):4], False, q == 3) for q in range(4)]
        mm(lst, ks + ["Ib", "GA%d" % h, "GB%d" % h], [bank], len(lst) * max(64, HE))

    def onehots(d, nm, nk):
        n5, n8, ft = T.nd[:, 0:128], T.nd[:, 128:256], T.fe[:, 128 * d:128 * (d + 1)]
        ts(n5, nm, 1.0 / 32, 1600.0 - 31.0 / 64, A.mult, A.add, nk, ["n5"], 64)
        ts(n8, nm, 1.0 / 256, 1544.0 - 255.0 / 512, A.mult, A.add, nk, ["n8"], 64)
        o = ps[5][:, 0:128]
        mm([(o, T.RT[:, 128 * i:128 * (i + 1)], x, i == 0, i == 4) for i, x in enumerate((n8, n5, nm, n8, n5))],
           nk + ["n5", "n8"] + ["RT%d" % i for i in range(5)], ["ps5"], 640)
        act(ft, o, AF.Square, kc[7], 1.0, ["k7"], ["ps5", "fe%d" % d])
        for x in range(4):
            b = 4 + x % 2
            mm([(ps[b][:], ft, T.SF[:, 512 * x:512 * (x + 1)], True, True)], ["fe%d" % d, "SFb"], ["ps%d" % b], 512)
            relu(T.OH[:, 2048 * d + 512 * x:2048 * d + 512 * (x + 1)], ps[b][:], ["ps%d" % b, "OH%d" % (4 * d + x)])

    def prime(b, d):
        mm([(ps[b][:], T.fe[:, 128 * d:128 * (d + 1)], T.SF[:, 2048:2560], True, False)], ["fe%d" % d, "SFa"], ["ps%d" % b], 512)

    def weigh(d, wgt, k, b):
        mm([(ps[b][:], wgt, T.SelW[:], False, True)], [k, "SelW"], ["ps%d" % b], 512)
        relu(T.Aw[:, 512 * d:512 * (d + 1)], ps[b][:], ["ps%d" % b, "Aw%d" % d])

    hs = range(NH)
    part = [slice(HE * h, HE * (h + 1)) for h in hs]
    e16 = [T.CE[:, 128 + HE * h:128 + HE * (h + 1)] for h in hs]
    for t in range(EP):
        n = str(t)
        up = t < EP - 1
        a, b = 128 * t, 128 * (t + 1)
        for h in hs:
            bk = "ps%d" % h
            strong(h, 0, T.Wg1, T.WA[:, W[t]:W[t] + NW], wk[t], T.L1, a, ["L1"])
            lookup(h, T.OW1, T.st, ["OW1", "st0%d" % h])
            o = ps[h][:, 192:192 + HE]
            combine(h, o, bk, I384, I3200, ["I384", "I-3200", "CE0"], [T.CE[:, part[h]]])
            ts(T.AD[:, part[h]], o, c_a2, float(E2), A.add, A.min, ["c_a2"], [bk, "AD%d" % h], HE)
        for h in hs:
            bk, o = "ps%d" % h, ps[h][:, 0:HE]
            gather(h, T.T3, "G2", T.T2[:, :], ["T2a", "T2b", "T2x", "T2e"], T.AD, 0, ["AD%d" % h])
            narrow(h, o, bk, T.ML, "M0", T.T3, "G2")
            cp(T.L2[:, part[h]], o, [], [bk, "L2%d" % h], HE)
            combine(h, ps[2][:, part[h]], "ps2", Im1, I9, ["I-1", "I9"], [])
        ts(T.cap[:], ps[2][:, 0:128], c_b2, 3.0, A.add, A.min, ["c_b2"], ["ps2"] + ["cap%d" % h for h in hs], 128)
        for h in hs:
            narrow(h, ps[2][:, 128 + HE * h:128 + HE * (h + 1)], "ps2", T.MP, "M4", T.T3, "G2")
        ts(T.Pn[:], ps[2][:, 128:256], 2048.0, None, A.add, None, [], ["ps2"] + ["Pn%d" % h for h in hs], 128)
        dma([(T.T3[r::8, BETA * j:BETA * j + 2048], T.T3[s::8, 0:2048]) for j, r, s in ((1, 0, 0), (1, 5, 1), (2, 0, 0), (2, 5, 6))],
            keys("G2"), ["T3b"], 1.0)
        if up:
            ts(T.sn2[:, a:b], T.L2[:], -2048.0, None, A.add, None, ["L2%d" % h for h in hs], ["sn2" + n], 64)
            send([(nxt, T.ln2[:, a:b])], T.sn2[:, a:b], ["sn2" + n], ["ln2" + n], 32e3)
            onehots(0, T.nm1[:, a:b], ["nm1"])
        for h in hs:
            gather(h, T.X1, "X1", T.F[:, :], ["F"], T.L1, a, ["L1"], T.Wg1, "Wg0")
        mm([(ps[3][:, 0:128], T.zero[:, 0:128], T.zero[:, 0:128], True, False)], ["zero"], ["ps3"], 128)
        for h in hs:
            reduce(h, T.X1, "X1", False)
        for h in hs:
            bk = "ps%d" % h
            strong(h, 1, T.Wg2, T.W2[:, :], ["W20", "W21"], T.L2, 0, ["L2%d" % h])
            tt(T.nn[:, part[h]], T.st[:, 128 + HE * h:128 + HE * (h + 1)], T.cap[:, part[h]], A.mult, ["st1%d" % h, "cap%d" % h], ["nn%d" % h], 2 * HE)
            lookup(h, T.OW, T.nn, ["OW", "nn%d" % h])
            o = ps[h][:, 320:320 + HE]
            mm([(o, T.Blk[:, 32:160], T.nn[:, part[h]], True, True)], ["Blk", "nn%d" % h], [bk], max(64, HE))
            ts(T.flag[:, part[h]], o, c_k, 8192.0, A.is_le, A.mult, ["c_k"], [bk, "flag%d" % h], HE)
            o = ps[h][:, 192:192 + HE]
            combine(h, o, bk, I1, I2304, ["I%d" % (-BETA - 8), "CE1", "flag%d" % h], [e16[h], T.flag[:, part[h]]])
            ts(T.AD[:, part[h]], o, c_a3, float(E3), A.add, A.min, ["c_a3"], [bk, "AD%d" % h], HE)
            combine(h, ps[2][:, 384 + HE * h:384 + HE * (h + 1)], "ps2", I1, Im8, ["I-8", "CE1"], [e16[h]])
        ts(T.pos[:], ps[2][:, 384:512], 4096.0, 2047.0, A.add, A.min, [], ["ps2"] + ["pos%d" % h for h in hs], 128)
        for h in hs:
            gather(h, T.V2, "V2", T.F[:, :], ["F"], T.Pn, 0, ["Pn%d" % h])
            gather(h, T.V2, "V2", T.F[:, :], ["F"], T.L2, 0, ["L2%d" % h], T.V2, "V2")
        if up:
            candidates(t + 1)
        for h in hs:
            bk, lk, lo = "ps%d" % h, "ps%d" % (6 + h), ps[6 + h][:, 448:448 + HE]
            gather(h, T.G3, "G3", T.T3[:, :], keys("G2") + ["T3b", "T3x", "T3e"], T.AD, 0, ["AD%d" % h])
            o = ps[h][:, 256:256 + HE]
            narrow(h, o, bk, T.ML, "M0", T.G3, "G3")
            lin(T.Lp[:, part[h]], o, 1.0, 1184.0, [], [bk, "Lp%d" % h], HE)
            lin(lo, T.Lp[:, part[h]], 2080.0, -2080.0 * 3232, ["Lp%d" % h], [lk, "PW%d" % h], HE)
            o = ps[h][:, 0:HE]
            narrow(h, o, bk, T.MB, "M5", T.G3, "G3")
            pa, pb = T.pa[:, part[h]], T.pb[:, part[h]]
            tt(pa, o, T.Lp[:, part[h]], A.mult, ["Lp%d" % h], [bk, "pa%d" % h], HE)
            tt(pa, lo, pa, A.add, ["PW%d" % h], [lk, "pa%d" % h], HE)
            ts(pb, pa, 5, 4095, A.arith_shift_right, A.bitwise_and, ["pa%d" % h], ["pb%d" % h], HE)
            cp(T.L3[:, part[h]], pb, ["pb%d" % h], ["L3%d" % h], HE)
        if up:
            ts(T.sn3[:, a:b], T.pb[:], -2048.0, None, A.add, None, ["pb%d" % h for h in hs], ["sn3" + n], 128)
            send([(nx2, T.ln3[:, a:b])], T.sn3[:, a:b], ["sn3" + n], ["ln3" + n], 32e3)
            halves(t)
        for h in hs:
            times(h, T.X2, "X2", T.V2, "V2", T.Wg2, "Wg1")
            reduce(h, T.X2, "X2", False)
        if up:
            onehots(1, T.ln2[:, a:b], ["ln2" + n])
            prime(6, 1)
        o = ps[2][:, 0:128]
        lst = [(o, T.M16[:, 32:160], T.st[:, 0:128], True, False), (o, T.M16[:, 32:160], T.st[:, 128:256], False, False)]
        if up:
            lst.append((o, I1, T.nask[:, a:b], False, False))
        mm(lst, ["M16", "Ib", "nask"] + ["st%d%d" % (d, h) for d in range(2) for h in hs], ["ps2"], 384)
        for h in hs:
            strong(h, 2, T.Wg3, T.W3[:, :], ["W30", "W31"], T.L3, 0, ["L3%d" % h])
            mm([(ps[2][:, part[h]], T.M16[:, 32:160], T.st[:, 256 + HE * h:256 + HE * (h + 1)], False, h == NH - 1)],
               ["M16", "st2%d" % h], ["ps2"], max(64, HE))
        if up:
            tt(T.sw[:, a:b], o, T.sig[:, a:b], A.mult, ["sig"], ["ps2", "sw" + n], 128)
            send([(nxt, T.lw2[:, a:b]), (nx2, T.lw3[:, a:b])], T.sw[:, a:b], ["sw" + n], ["lw" + n], 65e3)
            tt(T.cvs[:, a:b], o, T.nask[:, a:b], A.subtract, ["nask"], ["ps2", "cvs" + n], 128)
            onehots(2, T.ln3[:, a:b], ["ln3" + n])
            prime(7, 2)
            prime(1, 0)
            weigh(0, T.sw[:, a:b], "sw" + n, 1)
            weigh(1, T.lw2[:, a:b], "lw" + n, 6)
            weigh(2, T.lw3[:, a:b], "lw" + n, 7)
            for x in (0, 2):
                mm([(ps[x][:, 0:128], T.zero[:, 0:128], T.zero[:, 0:128], True, False)], ["zero"], ["ps%d" % x], 128)
            mm([(ps[1][:, 0:256], T.ones[:], T.Dg[:], True, False)], ["ones", "Dg0", "Dg1"], ["ps1"], 256)
            for d in range(3):
                for x in range(2):
                    cs = [c for c in range(16) if (c // 2 + d // 2) % 8 // 4 == x]
                    mm([(ps[2 * x][:, 32 * ((c // 2 + d // 2) % 4):32 * ((c // 2 + d // 2) % 4 + 1)], T.OH[:, 128 * (16 * d + c):128 * (16 * d + c + 1)],
                         T.Aw[:, 32 * (16 * d + c):32 * (16 * d + c + 1)], False, d == 2 and c == cs[-1]) for c in cs],
                       ["Aw%d" % d] + ["OH%d" % (4 * d + y) for y in range(4)], ["ps%d" % (2 * x)], 8 * 64)
            for s, k, x in ((T.s1, "s1", 0.5), (T.s2, "s2", 73300.5)):
                ts(s[:, 0:128], ps[0][:, 0:128], x, 2.0, A.is_gt, A.mult, [], ["ps0", k])
                act(s[:, 128:256], ps[2][:, 0:128], AF.Sign, -x, 1.0, [], ["ps2", k + "b"])
            for s, k, I in ((T.s1, "s1", Im4k if t else I2k), (T.s2, "s2", I2k)):
                mm([(ps[1][:, x:256:2], s[:, x::2], I, False, k == "s2" and x == 1) for x in range(2)], [k, k + "b", "I2048", "I-4096"], ["ps1"], 256)
            ts(T.UL[:], ps[1][:, 0:256], (c_ul, c_um)[t], None, A.add, None, ["c_ul", "c_um"], ["ps1", "UL"], 256)
            src = wk[t] + ["%s%d" % (x, j) for x in ("Hf", "Db") for j in range(4)] + ["Hz", "UL"]
            for j in range(8):
                pick(T.WA[:, W[t + 1] + 512 * j:W[t + 1] + 512 * (j + 1)], T.WA[:, NW * t:NW * (t + 3)].indirect(T.UL[:, 32 * j:32 * (j + 1)]),
                     src, [wk[t + 1][j]], 512, "vs")
            spread(t + 1, False)
            spread(t + 1, True)
        else:
            cp(T.cvs[:, a:b], o, [], ["ps2", "cvs" + n], 128, True)
        for h in hs:
            if t in EARLY:
                gather(h, T.X3, "X3", T.V2[:, :], keys("V2"), T.pos, 0, ["pos%d" % h])
                gather(h, T.X3, "X3", T.Fr[:, :], ["Fr"], T.L3, 0, ["L3%d" % h], T.X3, "X3")
                times(h, T.X3, "X3", T.X3, "X3", T.Wg3, "Wg2")
            else:
                gather(h, T.X3, "X3", T.V2[:, :], keys("V2"), T.pos, 0, ["pos%d" % h], T.Wg3, "Wg2")
                gather(h, T.X3, "X3", T.Fr[:, :], ["Fr"], T.L3, 0, ["L3%d" % h], T.X3, "X3")
            if up:
                reduce(h, T.X3, "X3", h == NH - 1)
                continue
            for j in chunks(h):
                sl = slice(CH * j, CH * (j + 1))
                add({"v": (vd(CH), lambda sl=sl: V.tensor_tensor_scan(T.X2[:, sl], T.keep[:], T.X3[:, sl], 0.0, A.mult, A.add))},
                    ["keep", "X3%d" % j], ["X2%d" % j])
                mm([(ps[3][:, 32 * j:32 * (j + 1)], T.IU[:], T.X2[:, CH * j + 15:CH * (j + 1):16], False, j == 3)], ["IU", "X2%d" % j], ["ps3"], 256)
        tt(T.ys[:, a:b], ps[3][:, 0:128], T.xvs[:, a:b], A.mult, ["xvs"], ["ps3", "ys" + n], 128)
        dma([(T.cv[:, a:b], T.cvs[0::16, a:b])], ["cvs" + n], ["cv" + n], 0.1)
        dma([(T.y[:, a:b], T.ys[:, a:b])], ["ys" + n], ["y" + n], 0.2)
    return ops


def depends(ops):
    lastw, readers, deps = {}, {}, []
    for i, o in enumerate(ops):
        d = set()
        for k in o["r"] + o["w"]:
            if k in lastw:
                d.add(lastw[k])
        for k in o["w"]:
            d.update(readers.get(k, []))
        d.discard(i)
        o["soft"] = {j for j in d if "p" not in o["alts"] and "p" not in ops[j]["alts"] and not any(k[:2] == "PW" for k in o["w"] + ops[j]["w"])
                     and all(k[:2] == "ps" for k in (set(o["r"]) | set(o["w"])) & set(ops[j]["w"]) | set(o["w"]) & set(ops[j]["r"]))}
        if "after" in o:
            d.add(o["after"])
            o["soft"].add(o["after"])
        deps.append(sorted(d))
        for k in o["r"]:
            readers.setdefault(k, []).append(i)
        for k in o["w"]:
            lastw[k] = i
            readers[k] = []
    return deps


def gap(busy, t, dur):
    lo, hi = 0, len(busy)
    while lo < hi:
        mid = (lo + hi) // 2
        if busy[mid][1] <= t:
            lo = mid + 1
        else:
            hi = mid
    while lo < len(busy) and busy[lo][0] < t + dur - 1e-9:
        t = max(t, busy[lo][1])
        lo += 1
    return t, lo


def place(ops, seq, before, can, back):
    n = len(ops)
    busy = {q: [] for q in "vspgyw"}
    where, start, fin = [None] * n, [0.0] * n, [0.0] * n
    for c in seq:
        o = ops[c]
        t0, pe = 0.0, can[c] == "p"
        for d in before[c]:
            t = fin[d] if pe and where[d] == "p" else fin[d] + WAKE
            if not back and d == o.get("after"):
                t = start[d] + 1e-3
            if t > t0:
                t0 = t
        if o["kind"] != "c":
            q = can[c]
            dur = o["alts"][q][0]
            if back:
                w, j = gap(busy["w"], t0 + 0.8, o["lat"])
                busy["w"].insert(j, (w, w + o["lat"]))
                t, j = gap(busy[q], w + o["lat"] + 1.0, dur)
                end = t + dur
            else:
                t, j = gap(busy[q], t0, dur)
                w, i = gap(busy["w"], t + dur + 1.0, o["lat"])
                busy["w"].insert(i, (w, w + o["lat"]))
                t, j = gap(busy[q], max(t, w - 1.0 - dur), dur)
                end = max(w + o["lat"], t + dur + 1.0) + 0.8
        else:
            end = 1e9
            for x in can[c]:
                u = o["alts"][x][0]
                s, i = gap(busy[x], t0, u)
                if s + u + (LEAN if x == "v" else 0.0) < end:
                    q, t, j, dur, end = x, s, i, u, s + u + (LEAN if x == "v" else 0.0)
            end = t + dur
        busy[q].insert(j, (t, t + dur))
        where[c], start[c], fin[c] = q, t, end
    return where, start, fin


def replay(cost, seq, where, old=None, first=0, again=3):
    n = len(seq)
    free, last = dict.fromkeys("vspgyw", 0.0), dict.fromkeys("vspgyw")
    issued, turned, lead = 0.0, False, cost[n]
    if old is None:
        end, off, by, held, first = [0.0] * n, [0.0] * n, [None] * n, [False] * n, 0
    else:
        end, off, by, held = [list(x) for x in old]
        for j in range(first - 1, -1, -1):
            c = seq[j]
            q = where[c]
            if last[q] is None:
                last[q], free[q] = c, off[c]
            if last["w"] is None and cost[c][q][1]:
                last["w"], free["w"], issued = c, end[c] - 0.7 * lead, off[c]
            if None not in last.values():
                break
    for j in range(first, n):
        c = seq[j]
        q = where[c]
        dur, wire, hard, soft = cost[c][q]
        t0, p = -1.0, None
        for d in hard:
            if end[d] > t0:
                t0, p = end[d], d
        t0 += WAKE
        for d in soft:
            if where[d] != q and end[d] + WAKE > t0:
                t0, p = end[d] + WAKE, d
        held[c] = free[q] > t0
        if held[c]:
            t0, p = free[q], last[q]
        e = off[c] = free[q] = t0 + dur
        last[q] = c
        if wire:
            turned, issued = turned or e < issued - 0.3, max(e, issued)
            if free["w"] > e + lead:
                p, held[c] = last["w"], True
                e = free["w"] - lead
            free["w"] = e + lead + wire
            last["w"] = c
            e += 1.7 * lead + wire
        end[c], by[c] = e, p
    if turned and again:
        seq.sort(key=lambda i: off[i] - 0.5 * cost[i][where[i]][0])
        return replay(cost, seq, where, None, 0, again - 1)
    total = max(end)
    tail, pairs = end.index(total), []
    while by[tail] is not None:
        if held[tail]:
            pairs.append((by[tail], tail))
        tail = by[tail]
    return total + MEAN * sum(end) / n, pairs, (end, off, by, held), again < 3


def schedule(ops, deps):
    n = len(ops)
    succ = [[] for _ in range(n)]
    for i in range(n):
        for d in deps[i]:
            succ[d].append(i)
    key = [0.0] * n
    for i in range(n - 1, -1, -1):
        o = ops[i]
        key[i] = (min(a[0] for a in o["alts"].values()) + o["lat"] + WAKE + (1.8 if o["kind"] != "c" else 0.0)
                  + max([key[s] for s in succ[i]] + [0.0]))
    can = [ops[i]["can"] or "".join(ops[i]["alts"]) for i in range(n)]
    soft = [[d for d in deps[i] if d in ops[i]["soft"] or ("p" in ops[i]["alts"] and "p" in ops[d]["alts"])] for i in range(n)]
    hard = [[d for d in deps[i] if d not in soft[i]] for i in range(n)]
    costs = [[{q: (o["alts"][q][0] * (1 + slow * (o["slow"] - 1) if o["kind"] == "c" else 1.0), o["lat"] * wire, hard[i], soft[i])
               for q in o["alts"]} for i, o in enumerate(ops)] + [lead] for slow, wire, lead, share in PACES]

    def judge(seq, where, old=None, first=0):
        m, pairs, keep = 0.0, [], []
        for x, pace in enumerate(PACES):
            y = replay(costs[x], seq, where, old and old[x], first, 0 if x else 3)
            if y[3] and x == 0:
                old = None
            m, pairs = m + pace[3] * y[0], pairs + y[1]
            keep.append(y[2])
        return m, seq, where, pairs, keep

    best = None
    for rnd in range(TURN):
        for i in range(n - 1, -1, -1):
            key[i] = max([key[i] + ops[i]["up"]] + [key[s] + 1e-6 for s in succ[i]])
        where, start, fin = place(ops, sorted(range(n), key=lambda i: (-key[i], i)), deps, can, False)
        now = judge(sorted(range(n), key=lambda i: (start[i], fin[i])), where)
        if best is None or now[0] < best[0]:
            best = now
        key = place(ops, sorted(range(n), key=lambda i: -fin[i]), succ, where, True)[2]
    dice = np.random.default_rng(SEED).random((ROUNDS, 4)).tolist()
    now = best
    for rnd in range(ROUNDS):
        level, seq, where, pairs, old = now
        u = dice[rnd]
        b, c = pairs[int(u[0] * len(pairs))]
        x = b if u[1] < 0.5 else c
        if len(ops[x]["alts"]) > 1 and u[2] < FLIP:
            where, seq = list(where), list(seq)
            where[x] = "s" if where[x] == "v" else "v"
            i = seq.index(x)
        else:
            i, j = seq.index(b), seq.index(c)
            if i > j:
                continue
            span = seq[i:j + 1] if x == b else seq[i:j + 1][::-1]
            moved = {x}
            for y in span[1:]:
                if any(z in moved for z in (deps if x == b else succ)[y]):
                    moved.add(y)
            if b in moved and c in moved:
                continue
            stay, go = [y for y in seq[i:j + 1] if y not in moved], [y for y in seq[i:j + 1] if y in moved]
            seq = seq[:i] + (stay + go if x == b else go + stay) + seq[j + 1:]
        new = judge(seq, where, old, i)
        if new[0] <= level - HEAT * (1.0 - rnd / ROUNDS) * math.log(u[3] + 1e-12):
            now = new
            if new[0] < best[0]:
                best = new
    seq, where = best[1:3]
    return {q: [i for i in seq if where[i] == q] for q in "vspgy"}, where, best[4][0][1], best[4][0][0]


PLAN = {}


def rank_program(g, core, T, topo):
    rank = T.rank_of(core)
    if rank is None:
        return
    N = len(T.cores)
    peer = [T.cores[(rank + j) % N] for j in (1, -1, -2, 2)]
    ops = build(g, T, peer[0], peer[1], peer[2], peer[3])
    if "p" not in PLAN:
        deps = depends(ops)
        PLAN["p"] = (deps, schedule(ops, deps))
        PLAN["soft"] = [o["soft"] for o in ops]
    deps, (order, where, start, fin) = PLAN["p"]
    soft = PLAN["soft"]
    queue = {"v": g.vector, "s": g.scalar, "p": g.tensor, "g": g, "y": g.sync}
    n = len(ops)
    pos = [0] * n
    for q in order:
        for j, i in enumerate(order[q]):
            pos[i] = j
    need, waits = [False] * n, [[] for _ in range(n)]
    for q in order:
        seen, got = {}, set()
        for i in order[q]:
            top = {}
            for d in deps[i]:
                if ops[d]["kind"] != "c":
                    if d not in got and d not in soft[i]:
                        got.add(d)
                        waits[i].append(d)
                elif not (q == where[d] and (q == "p" or d in soft[i])):
                    e = where[d]
                    if pos[d] > seen.get(e, -1) and (e not in top or pos[d] > pos[top[e]]):
                        top[e] = d
            for e in top:
                seen[e] = pos[top[e]]
                need[top[e]] = True
                waits[i].append(top[e])
    mark, nd, nm = [None] * n, 0, 0
    for q in order:
        c = 0
        for i in order[q]:
            if ops[i]["kind"] == "c" and need[i]:
                c += 1
                mark[i] = (T.sem["q" + q], c)
    for i in range(n):
        if ops[i]["kind"] == "dma":
            mark[i] = (T.sem["d%d" % nd], 16 * len(ops[i]["alts"][where[i]][1]))
            nd += 1
        elif ops[i]["kind"] == "msg":
            mark[i] = (T.sem["a%d" % nm], len(topo.engines(core, peer[0])))
            nm += 1
    waited = set()
    sent = 0
    for q in order:
        for i in order[q]:
            for d in waits[i]:
                queue[q].wait_ge(mark[d][0], mark[d][1])
                waited.add(d)
            o = ops[i]
            if o["kind"] == "msg":
                dsts, src = o["alts"][q][1]
                if len(dsts) == 1:
                    rid, pid, _ = topo.addr(dsts[0][0])
                    g.remote_dma(dsts[0][1], src, mark[i][0], T.sem.sent, pid, rid, topo.mask(core, dsts[0][0]))
                    sent += len(topo.engines(core, dsts[0][0]))
                else:
                    trs = []
                    for j, (dst, ap) in enumerate(dsts):
                        en = topo.engines(core, dst)
                        en = en[j * len(en) // 2:(j + 1) * len(en) // 2]
                        rid, pid, _ = topo.addr(dst)
                        trs.append(RemoteDMATransfer(dst_ids=[DstId(rid=rid, pnc=pid)], dma_engine_mask=sum(1 << x for x in en),
                                                     remote_sem=mark[i][0], src=src, dst=ap))
                        sent += len(en)
                    g.remote_dma_fused(trs, local_sem=T.sem.sent)
            elif o["kind"] == "dma":
                for f in o["alts"][q][1]:
                    f().then_inc(mark[i][0], 16)
            else:
                ins = o["alts"][q][1]()
                if need[i]:
                    ins.then_inc(mark[i][0], 1)
    for i in range(n):
        if ops[i]["kind"] != "c" and i not in waited:
            g.sync.wait_ge(mark[i][0], mark[i][1])
    g.wait_ge(T.sem.sent, sent)
